import numpy as np
import ml_dtypes


def mxq(x, axis, fmt="e4m3"):
    dtype, down = {"e4m3": (ml_dtypes.float8_e4m3fn, 7), "e5m2": (ml_dtypes.float8_e5m2, 14)}[fmt]
    v = np.moveaxis(np.asarray(x, np.float32).astype(ml_dtypes.bfloat16).astype(np.float64), axis, -1)
    blocks = v.reshape(v.shape[:-1] + (-1, 32))
    amax = np.abs(blocks).max(-1, keepdims=True)
    byte = np.maximum(np.where(amax > 0, np.frexp(amax)[1] - 1 + 127, 0) - down, 1)
    scale = np.exp2(byte - 127.0)
    codes = (blocks / scale).astype(np.float32).astype(dtype).astype(np.float64)
    return np.moveaxis((codes * scale).reshape(v.shape), -1, axis)


WIDE = False


def mx_kscale(k):
    if not WIDE:
        return np.ones(k)
    levels = np.array([10, -10, 5, -5, 0])
    if k % 512:
        return np.exp2(np.random.permutation(np.resize(levels, k // 32))).repeat(32)
    a = np.empty((k // 512, 16))
    for p in range(k // 512):
        a[p, :8] = np.random.permutation(np.resize(levels, 8))
        for g in range(8):
            far = levels[np.abs(levels - a[p, g]) >= 10]
            a[p, g + 8] = far[np.random.randint(len(far))]
    return np.exp2(a.ravel()).repeat(32)


def f64(x):
    return np.asarray(x).astype(np.float64)


def striped(idx):
    return np.tile(idx.reshape(-1, 16).T, (8, 1)).astype(np.uint16)


def unstriped(offs):
    return offs[:16].T.reshape(-1).astype(np.int64)


E2M1 = np.array([0.0, 0.5, 1.0, 1.5, 2.0, 3.0, 4.0, 6.0, -0.0, -0.5, -1.0, -1.5, -2.0, -3.0, -4.0, -6.0])


def pack_weight(w, fmt):
    k, n = w.shape
    w = f64(np.asarray(w, np.float32).astype(ml_dtypes.bfloat16)).reshape(k // 32, 32, n)
    amax = np.abs(w).max(1)
    if fmt == "e4m3":
        byte = np.frexp(amax)[1] - 1 + 127 - 7
    else:
        mant, ex = np.frexp(amax / 6.0)
        byte = np.where(mant > 0.5, ex, ex - 1) + 127
    byte = np.clip(np.where(amax > 0, byte, 1), 1, 254)
    scaled = (w * np.exp2(127.0 - byte)[:, None, :]).reshape(k, n).astype(np.float32)
    by_word = np.ascontiguousarray(scaled.reshape(k // 512, 128, 4, n).transpose(0, 1, 3, 2))
    if fmt == "e4m3":
        words = by_word.astype(ml_dtypes.float8_e4m3fn).view(np.uint8)
    else:
        c = by_word.astype(ml_dtypes.float4_e2m1fn).view(np.uint8) & 0xF
        words = (c[..., 0::2] | (c[..., 1::2] << 4)).reshape(k // 512, 128, 2 * n)
    return np.ascontiguousarray(words), np.ascontiguousarray(byte.astype(np.uint8).reshape(k // 512, 16, n))


def unpack_weight(words, scales, fmt):
    g, _, n = scales.shape
    words = np.ascontiguousarray(words).reshape(g, 128, n, -1)
    if fmt == "e4m3":
        vals = words.view(ml_dtypes.float8_e4m3fn).astype(np.float64)
    else:
        nib = np.empty((g, 128, n, 4), np.uint8)
        nib[..., 0::2] = words & 0xF
        nib[..., 1::2] = words >> 4
        vals = E2M1[nib]
    vals = vals * np.repeat(np.exp2(scales.astype(np.float64) - 127.0), 8, axis=1)[..., None]
    return vals.transpose(0, 1, 3, 2).reshape(g * 512, n)


def gelu(v):
    return 0.5 * v * (1.0 + np.tanh(np.sqrt(2.0 / np.pi) * (v + 0.044715 * v**3)))


K, H, N, T, S, P = 1024, 1024, 512, 2048, 1024, 512

def setup_inputs():
    n = np.random.standard_normal
    s = mx_kscale(K)[:, None]
    u = mx_kscale(H)[:, None]
    tab_words, tab_scales = pack_weight(n((K, T)) * s, "e4m3")
    w4_words, w4_scales = pack_weight(n((K, H)) / np.sqrt(K) / s, "e2m1")
    return {
        "tab_words": tab_words, "tab_scales": tab_scales,
        "offs": striped(np.random.permutation(T)[:S]),
        "pos1": striped(np.random.permutation(S)[:P]),
        "pos2": striped(np.random.permutation(S)[:P]),
        "pos3": striped(np.random.permutation(S)[:P]),
        "w4_words": w4_words, "w4_scales": w4_scales,
        "gain": (np.exp(0.3 * n(H)) * u[:, 0]).astype(np.float32),
        "w2": (n((H, N)) / np.sqrt(H) / u).astype(np.float32),
    }

def reference(tab_words, tab_scales, offs, pos1, pos2, pos3, w4_words, w4_scales, gain, w2):
    v = unpack_weight(tab_words, tab_scales, "e4m3")[:, unstriped(offs)]
    w4 = unpack_weight(w4_words, w4_scales, "e2m1")
    h = w4.T @ v
    sg = 1.0 / (1.0 + np.exp(-h))
    molar = sg[:, unstriped(pos1)]
    femur = sg[:, unstriped(pos2)]
    soil = h[:, unstriped(pos3)]
    z = (molar * femur / (molar + femur + 0.25) - soil) * f64(gain)[:, None]
    return mxq(f64(w2), 0, "e4m3").T @ mxq(z, 0, "e4m3")

@@ -1,0 +1,253 @@
+import math
+from contextlib import ExitStack
+
+import concourse.mybir as mybir
+
+K, H, N, T, S, M = 1024, 1024, 512, 2048, 1024, 512
+FLOPS = 2 * K * H * S + 2 * H * N * M
+
+F32 = mybir.dt.float32
+BF16 = mybir.dt.bfloat16
+I32 = mybir.dt.int32
+U32 = mybir.dt.uint32
+U16 = mybir.dt.uint16
+U8 = mybir.dt.uint8
+FP8X4 = mybir.dt.float8_e4m3fn_x4
+FP4X4 = mybir.dt.float4_e2m1fn_x4
+ACT = mybir.ActivationFunctionType
+ALU = mybir.AluOpType
+
+P = 128
+PACK = 4
+PASSES = 2
+TILES = H // P
+BANK = 512
+CHUNK = 256
+LN5 = math.log(5.0)
+FUSED = 6
+EARLY = 3
+
+
+def tile_list_burial_isotope_mobility_kernel(
+    tc, tab_words, tab_scales, offs, pos1, pos2, pos3, w4_words, w4_scales, gain, w2, out
+):
+    nc = tc.nc
+    with ExitStack() as ctx:
+        keep = ctx.enter_context(tc.tile_pool(name="keep", bufs=1))
+        psum = ctx.enter_context(tc.psum_pool(name="psum", bufs=4))
+
+        offs_sb = keep.tile([P, S // 16], U16, name="offs_sb")
+        pos_sb = [keep.tile([P, M // 16], U16, name="pos%d_sb" % j) for j in range(3)]
+        tab_scale_rows = keep.tile([P, T], U8, name="tab_scale_rows", align_bytes=64)
+        tab_sb = [
+            keep.tile([P, T], I32, name="tab_sb%d" % a, tag="table_w2_%d" % a, align_bytes=64) for a in range(PASSES)
+        ]
+        w4_raw = keep.tile([P, PASSES, H // 2], I32, name="w4_raw", align_bytes=64)
+        w4_scale_rows = keep.tile([32, H], U8, name="w4_scale_rows", align_bytes=64)
+        w4_sb = keep.tile([P, PASSES, 2 * H], U8, name="w4_sb", align_bytes=64)
+        staged = keep.tile([32, S + H], U8, name="staged", tag="staged_gain", align_bytes=64)
+        planes = [keep.tile([P, S + H], U8, name="planes%d" % a, align_bytes=64) for a in range(PASSES)]
+
+        nc.sync.dma_start(offs_sb[:], offs)
+        nc.sync.dma_start(
+            tab_scale_rows[0:32, :].bitcast(I32), tab_scales.rearrange("a q t -> (a q) t").bitcast(I32)
+        )
+        nc.sync.dma_start(w4_scale_rows[:].bitcast(I32), w4_scales.rearrange("a q c -> (a q) c").bitcast(I32))
+        nc.sync.dma_start(tab_sb[0][:], tab_words[0].rearrange("p t i -> p (t i)").bitcast(I32))
+        nc.sync.dma_start(w4_raw[:], w4_words.rearrange("a p c -> p a c").bitcast(I32))
+        nc.sync.dma_start(tab_sb[1][:], tab_words[1].rearrange("p t i -> p (t i)").bitcast(I32))
+        for j, pos in enumerate((pos1, pos2, pos3)):
+            nc.sync.dma_start(pos_sb[j][:], pos)
+
+        nc.vector.memset(tab_scale_rows[32:64, :].bitcast(I32), 0)
+        nc.gpsimd.memset(tab_scale_rows[64:128, :].bitcast(I32), 0)
+        for a in range(PASSES):
+            nc.vector.memset(planes[a][:].bitcast(I32), 0)
+
+        picked_scale_rows = keep.tile([P, S], U8, name="picked_scale_rows", align_bytes=64)
+        nc.vector.tensor_copy(picked_scale_rows[:], tab_scale_rows[:].indirect(offs_sb[:]))
+        nc.gpsimd.tensor_copy(
+            staged[:, S:].bitcast(I32).rearrange("p (b t u) -> p b t u", t=4, u=32),
+            w4_scale_rows[:].bitcast(I32).rearrange("p (b u t) -> p b t u", t=4, u=32),
+        )
+        nc.vector.tensor_copy(staged[:, :S].bitcast(I32), picked_scale_rows[0:32, :].bitcast(I32))
+        for a in range(PASSES):
+            for q in range(4):
+                nc.scalar.dma_start(
+                    planes[a][32 * q : 32 * q + 4, :].bitcast(I32),
+                    staged[16 * a + 4 * q : 16 * a + 4 * q + 4, :].bitcast(I32),
+                )
+
+        for a in range(PASSES):
+            nc.gpsimd.tensor_copy(
+                w4_sb[:, a, :].bitcast(I32).rearrange("p (b t u e) -> p b t u e", t=4, u=32, e=2),
+                w4_raw[:, a, :].rearrange("p (b u t e) -> p b t u e", t=4, u=32, e=2),
+            )
+
+        v_words = {}
+        for a in range(PASSES):
+            for half in range(2):
+                v_words[a, half] = keep.tile(
+                    [P, BANK], U32, name="v_words%d_%d" % (a, half), tag="words_soil%d" % (2 * a + half), align_bytes=64
+                )
+                nc.vector.tensor_copy(
+                    v_words[a, half][:],
+                    tab_sb[a][:].bitcast(U32).indirect(offs_sb[:, 32 * half : 32 * half + 32]),
+                )
+
+        w2_raw = []
+        for b in range(PASSES):
+            w2_raw.append(keep.tile([P, PACK, N], F32, name="w2_raw%d" % b, tag="table_w2_%d" % b, align_bytes=64))
+            for e in range(4):
+                nc.sync.dma_start(
+                    w2_raw[b][e:P:4, :, :],
+                    w2[512 * b : 512 * (b + 1), :].rearrange("(u t e) n -> e u t n", t=4, e=4)[e],
+                )
+        gain_sb = keep.tile([P, PASSES, 8], F32, name="gain_sb", tag="staged_gain", align_bytes=64)
+        with nc.allow_non_contiguous_dma(reason="gain: one value for each partition and row tile"):
+            for b in range(PASSES):
+                for e in range(4):
+                    nc.sync.dma_start(
+                        gain_sb[e:P:4, b, 0:PACK], gain.rearrange("(b u t e) -> b e u t", u=32, t=4, e=4)[b, e]
+                    )
+
+        def gain_of(i):
+            return gain_sb[:, i // PACK, i % PACK : i % PACK + 1]
+
+        h = [keep.tile([P, S], F32, name="h%d" % i, tag="h_z%d" % i) for i in range(TILES)]
+        tissue = [
+            keep.tile([P, 2, M], F32, name="tissue%d" % i, tag="tissue_later%d" % i, align_bytes=64)
+            for i in range(TILES)
+        ]
+        for i in range(TILES):
+            banks = []
+            for half in range(2):
+                banks.append(psum.tile([P, BANK], F32, name="bank", tag="bank"))
+                for a in range(PASSES):
+                    nc.tensor.matmul_mx(
+                        out=banks[half][:],
+                        lhsT=w4_sb[:, a, 2 * P * i : 2 * P * (i + 1)].bitcast(FP4X4),
+                        lhsT_scale=planes[a][:, S + P * i : S + P * (i + 1)],
+                        rhs=v_words[a, half][:].bitcast(FP8X4),
+                        rhs_scale=planes[a][:, BANK * half : BANK * (half + 1)],
+                        start=(a == 0),
+                        stop=(a == PASSES - 1),
+                    )
+            for half in range(2):
+                copy = nc.scalar.copy if (i, half) == (0, 0) else nc.vector.tensor_copy
+                copy(h[i][:, BANK * half : BANK * (half + 1)], banks[half][:])
+            if i < FUSED:
+                for j in range(2):
+                    nc.scalar.activation(tissue[i][:, j, :], h[i][:].indirect(pos_sb[j][:]), ACT.Sigmoid, bias=LN5)
+        for i in range(FUSED, TILES):
+            logits = keep.tile([P, 2, M], F32, name="logits%d" % i)
+            for j in range(2):
+                nc.vector.tensor_copy(logits[:, j, :], h[i][:].indirect(pos_sb[j][:]))
+            nc.scalar.activation(tissue[i][:], logits[:], ACT.Sigmoid, bias=LN5)
+
+        w2_bf = []
+        for b in range(PASSES):
+            w2_bf.append(keep.tile([P, N, PACK], BF16, name="w2_bf%d" % b, align_bytes=64))
+            nc.gpsimd.tensor_scalar(
+                w2_bf[b][:], w2_raw[b][:].rearrange("p t n -> p n t"), 1.0, 0.0, ALU.mult, ALU.add
+            )
+        both = keep.tile([P, TILES, M], F32, name="both", tag="table_w2_1", align_bytes=64)
+        for i in range(FUSED):
+            nc.gpsimd.tensor_tensor(both[:, i, :], tissue[i][:, 0, :], tissue[i][:, 1, :], ALU.mult)
+
+        soil = keep.tile([P, TILES, M], F32, name="soil")
+
+        def pick_soil(i, picked):
+            nc.vector.tensor_copy(picked, h[i][:].indirect(pos_sb[2][:]))
+            nc.gpsimd.tensor_scalar(soil[:, i, :], picked, 0.25, gain_of(i), ALU.add, ALU.mult)
+
+        for i in range(EARLY):
+            picked_early = keep.tile([P, M], F32, name="picked%d" % i, tag="words_soil%d" % i, align_bytes=64)
+            pick_soil(i, picked_early[:])
+        for i in range(FUSED, TILES):
+            nc.vector.tensor_tensor(both[:, i, :], tissue[i][:, 0, :], tissue[i][:, 1, :], ALU.mult)
+        picked_late = keep.tile(
+            [P, TILES - EARLY, M], F32, name="picked_late", tag="tissue_later%d" % (TILES - 1), align_bytes=64
+        )
+        for i in range(EARLY, TILES):
+            pick_soil(i, picked_late[:, i - EARLY, :])
+
+        w2_codes = keep.tile(
+            [P, PASSES, N], U32, name="w2_codes", tag="tissue_later%d" % (TILES - 2), align_bytes=64
+        )
+        w2_scale = keep.tile([P, PASSES, N], U8, name="w2_scale", align_bytes=64)
+        for b in range(PASSES):
+            nc.vector.quantize_mx(
+                out=w2_codes[:, b, :].bitcast(FP8X4),
+                scales=w2_scale[:, b, :],
+                in_=w2_bf[b][:].rearrange("p n t -> p (n t)"),
+            )
+
+        nc.scalar.activation(both[:], both[:], ACT.Ln, bias=3.0, scale=-2.56)
+
+        recip = keep.tile([P, TILES, M], F32, name="recip")
+        z = keep.tile([P, TILES, M], F32, name="z", tag="h_z%d" % (TILES - 1))
+        chunk = [slice(CHUNK * c, CHUNK * (c + 1)) for c in range(M // CHUNK)]
+        z_bf, z_codes, z_scale = {}, {}, {}
+
+        def combine(i, cols):
+            nc.vector.scalar_tensor_tensor(
+                z[:, i, cols], recip[:, i, cols], gain_of(i), soil[:, i, cols], ALU.mult, ALU.subtract
+            )
+
+        def interleave(c, b, copy):
+            z_bf[c, b] = keep.tile([P, CHUNK * PACK], BF16, name="z_bf%d_%d" % (c, b), align_bytes=64)
+            copy(
+                z_bf[c, b][:].rearrange("p (g i t) -> p g t i", i=4, t=PACK),
+                z[:, PACK * b : PACK * (b + 1), chunk[c]].rearrange("p t (g i) -> p g t i", i=4),
+            )
+
+        def quantize(c, b):
+            z_codes[c, b] = keep.tile([P, CHUNK], U32, name="z_codes%d_%d" % (c, b), align_bytes=64)
+            z_scale[c, b] = keep.tile([P, CHUNK], U8, name="z_scale%d_%d" % (c, b), align_bytes=64)
+            nc.vector.quantize_mx(out=z_codes[c, b][:].bitcast(FP8X4), scales=z_scale[c, b][:], in_=z_bf[c, b][:])
+
+        for i in range(PACK):
+            nc.scalar.activation(recip[:, i, :], both[:, i, :], ACT.Sigmoid, scale=-1.0)
+        for cols in chunk:
+            nc.scalar.activation(recip[:, PACK:, cols], both[:, PACK:, cols], ACT.Sigmoid, scale=-1.0)
+        for i in range(PACK):
+            combine(i, slice(0, M))
+        interleave(0, 0, nc.vector.tensor_copy)
+        interleave(1, 0, nc.scalar.copy)
+        for i in range(PACK, TILES):
+            combine(i, chunk[0])
+        quantize(0, 0)
+        interleave(0, 1, nc.vector.tensor_copy)
+        combine(PACK, chunk[1])
+        quantize(0, 1)
+        for i in range(PACK + 1, TILES):
+            combine(i, chunk[1])
+        interleave(1, 1, nc.vector.tensor_copy)
+        quantize(1, 0)
+        quantize(1, 1)
+
+        for c in range(M // CHUNK):
+            result = keep.tile([P, N // P, CHUNK], F32, name="result%d" % c)
+            acc = [psum.tile([P, CHUNK], F32, name="acc", tag=("bank", "acc")[c]) for j in range(N // P)]
+            for b in range(PASSES):
+                for j in range(N // P):
+                    nc.tensor.matmul_mx(
+                        out=acc[j][:],
+                        lhsT=w2_codes[:, b, P * j : P * (j + 1)].bitcast(FP8X4),
+                        lhsT_scale=w2_scale[:, b, P * j : P * (j + 1)],
+                        rhs=z_codes[c, b][:].bitcast(FP8X4),
+                        rhs_scale=z_scale[c, b][:],
+                        start=(b == 0),
+                        stop=(b == PASSES - 1),
+                    )
+            for j in range(N // P):
+                if c == M // CHUNK - 1 and j % 2 == 1:
+                    nc.vector.tensor_copy(result[:, j, :], acc[j][:])
+                else:
+                    nc.scalar.copy(result[:, j, :], acc[j][:])
+                if j % 2 == 1:
+                    nc.sync.dma_start(
+                        out[P * (j - 1) : P * (j + 1), chunk[c]].rearrange("(j p) m -> p j m", p=P),
+                        result[:, j - 1 : j + 1, :],
+                    )

@@ -22,7 +22,8 @@ PACK = 4
 PASSES = 2
 TILES = H // P
 BANK = 512
-CHUNK = 256
+PIECES = (slice(0, 256), slice(256, 384), slice(384, 512))
+HALVES = (slice(0, 256), slice(256, 512))
 LN5 = math.log(5.0)
 FUSED = 6
 EARLY = 3
@@ -187,67 +188,76 @@ def tile_list_burial_isotope_mobility_kernel(
 
         recip = keep.tile([P, TILES, M], F32, name="recip")
         z = keep.tile([P, TILES, M], F32, name="z", tag="h_z%d" % (TILES - 1))
-        chunk = [slice(CHUNK * c, CHUNK * (c + 1)) for c in range(M // CHUNK)]
-        z_bf, z_codes, z_scale = {}, {}, {}
+        z_bf = keep.tile([P, PASSES, M * PACK], BF16, name="z_bf", align_bytes=64)
+        z_codes = keep.tile([P, PASSES, M], U32, name="z_codes", align_bytes=64)
+        z_scale = keep.tile([P, PASSES, M], U8, name="z_scale", align_bytes=64)
 
         def combine(i, cols):
             nc.vector.scalar_tensor_tensor(
                 z[:, i, cols], recip[:, i, cols], gain_of(i), soil[:, i, cols], ALU.mult, ALU.subtract
             )
 
-        def interleave(c, b, copy):
-            z_bf[c, b] = keep.tile([P, CHUNK * PACK], BF16, name="z_bf%d_%d" % (c, b), align_bytes=64)
+        def interleave(b, cols, copy):
             copy(
-                z_bf[c, b][:].rearrange("p (g i t) -> p g t i", i=4, t=PACK),
-                z[:, PACK * b : PACK * (b + 1), chunk[c]].rearrange("p t (g i) -> p g t i", i=4),
+                z_bf[:, b, PACK * cols.start : PACK * cols.stop].rearrange("p (g i t) -> p g t i", i=4, t=PACK),
+                z[:, PACK * b : PACK * (b + 1), cols].rearrange("p t (g i) -> p g t i", i=4),
             )
 
-        def quantize(c, b):
-            z_codes[c, b] = keep.tile([P, CHUNK], U32, name="z_codes%d_%d" % (c, b), align_bytes=64)
-            z_scale[c, b] = keep.tile([P, CHUNK], U8, name="z_scale%d_%d" % (c, b), align_bytes=64)
-            nc.vector.quantize_mx(out=z_codes[c, b][:].bitcast(FP8X4), scales=z_scale[c, b][:], in_=z_bf[c, b][:])
+        def quantize(b, cols):
+            nc.vector.quantize_mx(
+                out=z_codes[:, b, cols].bitcast(FP8X4),
+                scales=z_scale[:, b, cols],
+                in_=z_bf[:, b, PACK * cols.start : PACK * cols.stop],
+            )
 
         for i in range(PACK):
             nc.scalar.activation(recip[:, i, :], both[:, i, :], ACT.Sigmoid, scale=-1.0)
-        for cols in chunk:
+        for cols in HALVES:
             nc.scalar.activation(recip[:, PACK:, cols], both[:, PACK:, cols], ACT.Sigmoid, scale=-1.0)
         for i in range(PACK):
             combine(i, slice(0, M))
-        interleave(0, 0, nc.vector.tensor_copy)
-        interleave(1, 0, nc.scalar.copy)
-        for i in range(PACK, TILES):
-            combine(i, chunk[0])
-        quantize(0, 0)
-        interleave(0, 1, nc.vector.tensor_copy)
-        combine(PACK, chunk[1])
-        quantize(0, 1)
+        interleave(0, HALVES[0], nc.vector.tensor_copy)
+        interleave(0, HALVES[1], nc.scalar.copy)
+        combine(PACK, PIECES[0])
+        quantize(0, HALVES[0])
         for i in range(PACK + 1, TILES):
-            combine(i, chunk[1])
-        interleave(1, 1, nc.vector.tensor_copy)
-        quantize(1, 0)
-        quantize(1, 1)
+            combine(i, PIECES[0])
+        interleave(1, PIECES[0], nc.vector.tensor_copy)
+        combine(PACK, PIECES[1])
+        quantize(1, PIECES[0])
+        for i in range(PACK + 1, TILES):
+            combine(i, PIECES[1])
+        quantize(0, HALVES[1])
+        interleave(1, PIECES[1], nc.vector.tensor_copy)
+        combine(PACK, PIECES[2])
+        quantize(1, PIECES[1])
+        for i in range(PACK + 1, TILES):
+            combine(i, PIECES[2])
+        interleave(1, PIECES[2], nc.vector.tensor_copy)
+        quantize(1, PIECES[2])
 
-        for c in range(M // CHUNK):
-            result = keep.tile([P, N // P, CHUNK], F32, name="result%d" % c)
-            acc = [psum.tile([P, CHUNK], F32, name="acc", tag=("bank", "acc")[c]) for j in range(N // P)]
+        for c, cols in enumerate(PIECES):
+            width = cols.stop - cols.start
+            result = keep.tile([P, N // P, width], F32, name="result%d" % c)
+            acc = [psum.tile([P, width], F32, name="acc", tag=("bank", "acc")[c % 2]) for j in range(N // P)]
             for b in range(PASSES):
                 for j in range(N // P):
                     nc.tensor.matmul_mx(
                         out=acc[j][:],
                         lhsT=w2_codes[:, b, P * j : P * (j + 1)].bitcast(FP8X4),
                         lhsT_scale=w2_scale[:, b, P * j : P * (j + 1)],
-                        rhs=z_codes[c, b][:].bitcast(FP8X4),
-                        rhs_scale=z_scale[c, b][:],
+                        rhs=z_codes[:, b, cols].bitcast(FP8X4),
+                        rhs_scale=z_scale[:, b, cols],
                         start=(b == 0),
                         stop=(b == PASSES - 1),
                     )
             for j in range(N // P):
-                if c == M // CHUNK - 1 and j % 2 == 1:
+                if c == len(PIECES) - 1 and j % 2 == 1:
                     nc.vector.tensor_copy(result[:, j, :], acc[j][:])
                 else:
                     nc.scalar.copy(result[:, j, :], acc[j][:])
                 if j % 2 == 1:
                     nc.sync.dma_start(
-                        out[P * (j - 1) : P * (j + 1), chunk[c]].rearrange("(j p) m -> p j m", p=P),
+                        out[P * (j - 1) : P * (j + 1), cols].rearrange("(j p) m -> p j m", p=P),
                         result[:, j - 1 : j + 1, :],
                     )

@@ -60,6 +60,10 @@ def tile_list_burial_isotope_mobility_kernel(
         for j, pos in enumerate((pos1, pos2, pos3)):
             nc.sync.dma_start(pos_sb[j][:], pos)
 
+        warm = keep.tile([P, 2, 8], F32, name="warm")
+        nc.gpsimd.memset(warm[:, 0, :], 0.0)
+        nc.scalar.activation(warm[:, 1, :], warm[:, 0, :], ACT.Sigmoid)
+
         nc.vector.memset(tab_scale_rows[32:64, :].bitcast(I32), 0)
         nc.gpsimd.memset(tab_scale_rows[64:128, :].bitcast(I32), 0)
         for a in range(PASSES):
@@ -184,7 +188,7 @@ def tile_list_burial_isotope_mobility_kernel(
                 in_=w2_bf[b][:].rearrange("p n t -> p (n t)"),
             )
 
-        nc.scalar.activation(both[:], both[:], ACT.Ln, bias=3.0, scale=-2.56)
+        nc.scalar.activation(both[:], both[:], ACT.Abs_reciprocal_sqrt, bias=4.0, scale=-2.56)
 
         recip = keep.tile([P, TILES, M], F32, name="recip")
         z = keep.tile([P, TILES, M], F32, name="z", tag="h_z%d" % (TILES - 1))
@@ -211,9 +215,9 @@ def tile_list_burial_isotope_mobility_kernel(
             )
 
         for i in range(PACK):
-            nc.scalar.activation(recip[:, i, :], both[:, i, :], ACT.Sigmoid, scale=-1.0)
+            nc.scalar.activation(recip[:, i, :], both[:, i, :], ACT.Square)
         for cols in HALVES:
-            nc.scalar.activation(recip[:, PACK:, cols], both[:, PACK:, cols], ACT.Sigmoid, scale=-1.0)
+            nc.scalar.activation(recip[:, PACK:, cols], both[:, PACK:, cols], ACT.Square)
         for i in range(PACK):
             combine(i, slice(0, M))
         interleave(0, HALVES[0], nc.vector.tensor_copy)

@@ -25,8 +25,9 @@ BANK = 512
 PIECES = (slice(0, 256), slice(256, 384), slice(384, 512))
 HALVES = (slice(0, 256), slice(256, 512))
 LN5 = math.log(5.0)
-FUSED = 6
-EARLY = 3
+WORDS_AT = 20480
+TISSUE_AT = 28672
+TABLE0_AT = 43008
 
 
 def tile_list_burial_isotope_mobility_kernel(
@@ -35,18 +36,22 @@ def tile_list_burial_isotope_mobility_kernel(
     nc = tc.nc
     with ExitStack() as ctx:
         keep = ctx.enter_context(tc.tile_pool(name="keep", bufs=1))
-        psum = ctx.enter_context(tc.psum_pool(name="psum", bufs=4))
+        shared = ctx.enter_context(tc.tile_pool(name="shared", bufs=1))
+        psum = ctx.enter_context(tc.psum_pool(name="psum", bufs=8))
 
         offs_sb = keep.tile([P, S // 16], U16, name="offs_sb")
         pos_sb = [keep.tile([P, M // 16], U16, name="pos%d_sb" % j) for j in range(3)]
         tab_scale_rows = keep.tile([P, T], U8, name="tab_scale_rows", align_bytes=64)
         tab_sb = [
-            keep.tile([P, T], I32, name="tab_sb%d" % a, tag="table_w2_%d" % a, align_bytes=64) for a in range(PASSES)
+            shared.tile([P, T], I32, name="tab_sb0", align_bytes=64, offset=TABLE0_AT),
+            shared.tile([P, T], I32, name="tab_sb1", align_bytes=64, offset=0),
         ]
-        w4_raw = keep.tile([P, PASSES, H // 2], I32, name="w4_raw", align_bytes=64)
+        w4_raw = [
+            keep.tile([P, PASSES, H // 4], I32, name="w4_raw0", tag="w4_gain", align_bytes=64),
+            shared.tile([P, PASSES, H // 4], I32, name="w4_raw1", align_bytes=64, offset=TABLE0_AT),
+        ]
+        w4_halves = w4_words.rearrange("a p (b c) -> b p a c", b=2)
         w4_scale_rows = keep.tile([32, H], U8, name="w4_scale_rows", align_bytes=64)
-        w4_sb = keep.tile([P, PASSES, 2 * H], U8, name="w4_sb", align_bytes=64)
-        staged = keep.tile([32, S + H], U8, name="staged", tag="staged_gain", align_bytes=64)
         planes = [keep.tile([P, S + H], U8, name="planes%d" % a, align_bytes=64) for a in range(PASSES)]
 
         nc.sync.dma_start(offs_sb[:], offs)
@@ -54,76 +59,98 @@ def tile_list_burial_isotope_mobility_kernel(
             tab_scale_rows[0:32, :].bitcast(I32), tab_scales.rearrange("a q t -> (a q) t").bitcast(I32)
         )
         nc.sync.dma_start(w4_scale_rows[:].bitcast(I32), w4_scales.rearrange("a q c -> (a q) c").bitcast(I32))
+        nc.sync.dma_start(pos_sb[0][:], pos1)
+        nc.sync.dma_start(pos_sb[1][:], pos2)
         nc.sync.dma_start(tab_sb[0][:], tab_words[0].rearrange("p t i -> p (t i)").bitcast(I32))
-        nc.sync.dma_start(w4_raw[:], w4_words.rearrange("a p c -> p a c").bitcast(I32))
+        nc.sync.dma_start(w4_raw[0][:], w4_halves[0].bitcast(I32))
         nc.sync.dma_start(tab_sb[1][:], tab_words[1].rearrange("p t i -> p (t i)").bitcast(I32))
-        for j, pos in enumerate((pos1, pos2, pos3)):
-            nc.sync.dma_start(pos_sb[j][:], pos)
+        nc.sync.dma_start(pos_sb[2][:], pos3)
 
         warm = keep.tile([P, 2, 8], F32, name="warm")
         nc.gpsimd.memset(warm[:, 0, :], 0.0)
         nc.scalar.activation(warm[:, 1, :], warm[:, 0, :], ACT.Sigmoid)
 
         nc.vector.memset(tab_scale_rows[32:64, :].bitcast(I32), 0)
-        nc.gpsimd.memset(tab_scale_rows[64:128, :].bitcast(I32), 0)
+        nc.vector.memset(tab_scale_rows[64:128, :].bitcast(I32), 0)
         for a in range(PASSES):
-            nc.vector.memset(planes[a][:].bitcast(I32), 0)
+            nc.gpsimd.memset(planes[a][:].bitcast(I32), 0)
 
-        picked_scale_rows = keep.tile([P, S], U8, name="picked_scale_rows", align_bytes=64)
-        nc.vector.tensor_copy(picked_scale_rows[:], tab_scale_rows[:].indirect(offs_sb[:]))
-        nc.gpsimd.tensor_copy(
-            staged[:, S:].bitcast(I32).rearrange("p (b t u) -> p b t u", t=4, u=32),
+        nc.vector.tensor_copy(
+            planes[0][0:32, S:].bitcast(I32).rearrange("p (b t u) -> p b t u", t=4, u=32),
             w4_scale_rows[:].bitcast(I32).rearrange("p (b u t) -> p b t u", t=4, u=32),
         )
-        nc.vector.tensor_copy(staged[:, :S].bitcast(I32), picked_scale_rows[0:32, :].bitcast(I32))
+        picked_scale_rows = keep.tile([P, S], U8, name="picked_scale_rows", align_bytes=64)
+        nc.vector.tensor_copy(picked_scale_rows[:], tab_scale_rows[:].indirect(offs_sb[:]))
+        nc.vector.tensor_copy(planes[0][0:32, :S].bitcast(I32), picked_scale_rows[0:32, :].bitcast(I32))
         for a in range(PASSES):
             for q in range(4):
-                nc.scalar.dma_start(
-                    planes[a][32 * q : 32 * q + 4, :].bitcast(I32),
-                    staged[16 * a + 4 * q : 16 * a + 4 * q + 4, :].bitcast(I32),
-                )
-
-        for a in range(PASSES):
-            nc.gpsimd.tensor_copy(
-                w4_sb[:, a, :].bitcast(I32).rearrange("p (b t u e) -> p b t u e", t=4, u=32, e=2),
-                w4_raw[:, a, :].rearrange("p (b u t e) -> p b t u e", t=4, u=32, e=2),
-            )
+                if (a, q) != (0, 0):
+                    nc.scalar.dma_start(
+                        planes[a][32 * q : 32 * q + 4, :].bitcast(I32),
+                        planes[0][16 * a + 4 * q : 16 * a + 4 * q + 4, :].bitcast(I32),
+                    )
 
         v_words = {}
-        for a in range(PASSES):
+
+        def pick_words(a):
             for half in range(2):
-                v_words[a, half] = keep.tile(
-                    [P, BANK], U32, name="v_words%d_%d" % (a, half), tag="words_soil%d" % (2 * a + half), align_bytes=64
+                v_words[a, half] = shared.tile(
+                    [P, BANK], U32, name="v_words%d_%d" % (a, half), align_bytes=64, offset=WORDS_AT + 2048 * (2 * a + half)
                 )
                 nc.vector.tensor_copy(
                     v_words[a, half][:],
                     tab_sb[a][:].bitcast(U32).indirect(offs_sb[:, 32 * half : 32 * half + 32]),
                 )
 
-        w2_raw = []
+        w4_of = {}
+
+        def order_w4(run, first):
+            count = run.shape[1]
+            b, t = divmod(first, PACK)
+            nc.vector.tensor_copy(
+                run[:].bitcast(I32).rearrange("p t a (u e) -> p t a u e", e=2), w4_raw[b][:].rearrange("p a (u t e) -> p t a u e", t=4, e=2)[:, t : t + count]
+            )
+            for k in range(count):
+                w4_of[first + k] = (run, k)
+
+        pick_words(0)
+        nc.sync.dma_start(w4_raw[1][:], w4_halves[1].bitcast(I32))
+        order_w4(keep.tile([P, 1, PASSES, 2 * P], U8, name="w4_first", align_bytes=64), 0)
+        pick_words(1)
+        order_w4(shared.tile([P, 3, PASSES, 2 * P], U8, name="w4_next", align_bytes=64, offset=0), 1)
+        order_w4(shared.tile([P, 4, PASSES, 2 * P], U8, name="w4_last", align_bytes=64, offset=2048), 4)
+
+        w2_raw = [
+            shared.tile([P, PACK, N], F32, name="w2_raw0", align_bytes=64, offset=TABLE0_AT + 2048),
+            shared.tile([P, PACK, N], F32, name="w2_raw1", align_bytes=64, offset=4096),
+        ]
         for b in range(PASSES):
-            w2_raw.append(keep.tile([P, PACK, N], F32, name="w2_raw%d" % b, tag="table_w2_%d" % b, align_bytes=64))
             for e in range(4):
                 nc.sync.dma_start(
                     w2_raw[b][e:P:4, :, :],
                     w2[512 * b : 512 * (b + 1), :].rearrange("(u t e) n -> e u t n", t=4, e=4)[e],
                 )
-        gain_sb = keep.tile([P, PASSES, 8], F32, name="gain_sb", tag="staged_gain", align_bytes=64)
-        with nc.allow_non_contiguous_dma(reason="gain: one value for each partition and row tile"):
-            for b in range(PASSES):
-                for e in range(4):
-                    nc.sync.dma_start(
-                        gain_sb[e:P:4, b, 0:PACK], gain.rearrange("(b u t e) -> b e u t", u=32, t=4, e=4)[b, e]
-                    )
-
         def gain_of(i):
             return gain_sb[:, i // PACK, i % PACK : i % PACK + 1]
 
-        h = [keep.tile([P, S], F32, name="h%d" % i, tag="h_z%d" % i) for i in range(TILES)]
-        tissue = [
-            keep.tile([P, 2, M], F32, name="tissue%d" % i, tag="tissue_later%d" % i, align_bytes=64)
-            for i in range(TILES)
+        h = [keep.tile([P, S], F32, name="h%d" % i, tag="h_later%d" % i, align_bytes=64) for i in range(TILES)]
+        tissue = [shared.tile([P, 2, 2, M], F32, name="tissue0", align_bytes=64, offset=TISSUE_AT)] + [
+            keep.tile([P, 2, 2, M], F32, name="tissue%d" % k) for k in range(1, TILES // 2)
         ]
+        w2_bf = []
+
+        def pick_soil(i):
+            nc.vector.tensor_copy(soil[:, i, :], h[i][:].indirect(pos_sb[2][:]))
+
+        def scale_soil(i):
+            nc.vector.tensor_scalar(soil[:, i, :], soil[:, i, :], 0.25, gain_of(i), ALU.add, ALU.mult)
+
+        def cast_w2(b):
+            w2_bf.append(keep.tile([P, N, PACK], BF16, name="w2_bf%d" % b, align_bytes=64))
+            nc.gpsimd.tensor_scalar(
+                w2_bf[b][:], w2_raw[b][:].rearrange("p t n -> p n t"), 1.0, 0.0, ALU.mult, ALU.add
+            )
+
         for i in range(TILES):
             banks = []
             for half in range(2):
@@ -131,7 +158,7 @@ def tile_list_burial_isotope_mobility_kernel(
                 for a in range(PASSES):
                     nc.tensor.matmul_mx(
                         out=banks[half][:],
-                        lhsT=w4_sb[:, a, 2 * P * i : 2 * P * (i + 1)].bitcast(FP4X4),
+                        lhsT=w4_of[i][0][:, w4_of[i][1], a, :].bitcast(FP4X4),
                         lhsT_scale=planes[a][:, S + P * i : S + P * (i + 1)],
                         rhs=v_words[a, half][:].bitcast(FP8X4),
                         rhs_scale=planes[a][:, BANK * half : BANK * (half + 1)],
@@ -139,47 +166,48 @@ def tile_list_burial_isotope_mobility_kernel(
                         stop=(a == PASSES - 1),
                     )
             for half in range(2):
-                copy = nc.scalar.copy if (i, half) == (0, 0) else nc.vector.tensor_copy
+                copy = nc.scalar.copy if i == 0 else nc.vector.tensor_copy
                 copy(h[i][:, BANK * half : BANK * (half + 1)], banks[half][:])
-            if i < FUSED:
-                for j in range(2):
-                    nc.scalar.activation(tissue[i][:, j, :], h[i][:].indirect(pos_sb[j][:]), ACT.Sigmoid, bias=LN5)
-        for i in range(FUSED, TILES):
-            logits = keep.tile([P, 2, M], F32, name="logits%d" % i)
             for j in range(2):
-                nc.vector.tensor_copy(logits[:, j, :], h[i][:].indirect(pos_sb[j][:]))
-            nc.scalar.activation(tissue[i][:], logits[:], ACT.Sigmoid, bias=LN5)
+                nc.scalar.activation(
+                    tissue[i // 2][:, j, i % 2, :], h[i][:].indirect(pos_sb[j][:]), ACT.Sigmoid, bias=LN5
+                )
 
-        w2_bf = []
+        def product(pair, engine):
+            engine.tensor_tensor(both[pair][:], tissue[pair][:, 0], tissue[pair][:, 1], ALU.mult)
+
         for b in range(PASSES):
-            w2_bf.append(keep.tile([P, N, PACK], BF16, name="w2_bf%d" % b, align_bytes=64))
-            nc.gpsimd.tensor_scalar(
-                w2_bf[b][:], w2_raw[b][:].rearrange("p t n -> p n t"), 1.0, 0.0, ALU.mult, ALU.add
-            )
-        both = keep.tile([P, TILES, M], F32, name="both", tag="table_w2_1", align_bytes=64)
-        for i in range(FUSED):
-            nc.gpsimd.tensor_tensor(both[:, i, :], tissue[i][:, 0, :], tissue[i][:, 1, :], ALU.mult)
+            cast_w2(b)
+        both = [shared.tile([P, 2, M], F32, name="both0", align_bytes=64, offset=4096)] + [
+            keep.tile([P, 2, M], F32, name="both%d" % (k + 1), tag="h_later%d" % after, align_bytes=64)
+            for k, after in enumerate((0, 2, 5))
+        ]
+        product(0, nc.gpsimd)
+        gain_sb = keep.tile([P, PASSES, 8], F32, name="gain_sb", tag="w4_gain", align_bytes=64)
+        with nc.allow_non_contiguous_dma(reason="gain: one value for each partition and row tile"):
+            for b in range(PASSES):
+                for e in range(4):
+                    nc.sync.dma_start(
+                        gain_sb[e:P:4, b, 0:PACK], gain.rearrange("(b u t e) -> b e u t", u=32, t=4, e=4)[b, e]
+                    )
 
-        soil = keep.tile([P, TILES, M], F32, name="soil")
+        soil = shared.tile([P, TILES, M], F32, name="soil", align_bytes=64, offset=TISSUE_AT - 2048)
+        pick_soil(7)
+        pick_soil(0)
+        product(1, nc.vector)
+        pick_soil(1)
+        pick_soil(2)
+        for i in (7, 0, 1):
+            scale_soil(i)
+        product(2, nc.vector)
+        for i in range(3, 6):
+            pick_soil(i)
+        product(3, nc.vector)
+        pick_soil(6)
+        for i in range(2, 7):
+            scale_soil(i)
 
-        def pick_soil(i, picked):
-            nc.vector.tensor_copy(picked, h[i][:].indirect(pos_sb[2][:]))
-            nc.gpsimd.tensor_scalar(soil[:, i, :], picked, 0.25, gain_of(i), ALU.add, ALU.mult)
-
-        for i in range(EARLY):
-            picked_early = keep.tile([P, M], F32, name="picked%d" % i, tag="words_soil%d" % i, align_bytes=64)
-            pick_soil(i, picked_early[:])
-        for i in range(FUSED, TILES):
-            nc.vector.tensor_tensor(both[:, i, :], tissue[i][:, 0, :], tissue[i][:, 1, :], ALU.mult)
-        picked_late = keep.tile(
-            [P, TILES - EARLY, M], F32, name="picked_late", tag="tissue_later%d" % (TILES - 1), align_bytes=64
-        )
-        for i in range(EARLY, TILES):
-            pick_soil(i, picked_late[:, i - EARLY, :])
-
-        w2_codes = keep.tile(
-            [P, PASSES, N], U32, name="w2_codes", tag="tissue_later%d" % (TILES - 2), align_bytes=64
-        )
+        w2_codes = keep.tile([P, PASSES, N], U32, name="w2_codes", tag="h_later%d" % (TILES - 2), align_bytes=64)
         w2_scale = keep.tile([P, PASSES, N], U8, name="w2_scale", align_bytes=64)
         for b in range(PASSES):
             nc.vector.quantize_mx(
@@ -188,24 +216,31 @@ def tile_list_burial_isotope_mobility_kernel(
                 in_=w2_bf[b][:].rearrange("p n t -> p (n t)"),
             )
 
-        nc.scalar.activation(both[:], both[:], ACT.Abs_reciprocal_sqrt, bias=4.0, scale=-2.56)
+        root = keep.tile([P, TILES, M], F32, name="root", tag="h_later%d" % (TILES - 1), align_bytes=64)
 
-        recip = keep.tile([P, TILES, M], F32, name="recip")
-        z = keep.tile([P, TILES, M], F32, name="z", tag="h_z%d" % (TILES - 1))
+        def inverse_root(rows):
+            nc.scalar.activation(root[:, rows, :], both[rows.start // 2][:], ACT.Abs_reciprocal_sqrt, bias=4.0, scale=-2.56)
+
+        def square(rows):
+            nc.scalar.activation(root[:, rows, :], root[:, rows, :], ACT.Square)
+
+        pairs = [slice(i, i + 2) for i in range(0, TILES, 2)]
+        inverse_root(pairs[0])
+        for rows, following in zip(pairs, pairs[1:]):
+            inverse_root(following)
+            square(rows)
+        square(pairs[-1])
+
+        term = keep.tile([P, TILES, M], F32, name="term")
         z_bf = keep.tile([P, PASSES, M * PACK], BF16, name="z_bf", align_bytes=64)
         z_codes = keep.tile([P, PASSES, M], U32, name="z_codes", align_bytes=64)
         z_scale = keep.tile([P, PASSES, M], U8, name="z_scale", align_bytes=64)
 
-        def combine(i, cols):
-            nc.vector.scalar_tensor_tensor(
-                z[:, i, cols], recip[:, i, cols], gain_of(i), soil[:, i, cols], ALU.mult, ALU.subtract
-            )
+        def woven(b, cols):
+            return z_bf[:, b, PACK * cols.start : PACK * cols.stop].rearrange("p (g i t) -> p g t i", i=4, t=PACK)
 
-        def interleave(b, cols, copy):
-            copy(
-                z_bf[:, b, PACK * cols.start : PACK * cols.stop].rearrange("p (g i t) -> p g t i", i=4, t=PACK),
-                z[:, PACK * b : PACK * (b + 1), cols].rearrange("p t (g i) -> p g t i", i=4),
-            )
+        def rows_of(tile, b, cols):
+            return tile[:, PACK * b : PACK * (b + 1), cols].rearrange("p t (g i) -> p g t i", i=4)
 
         def quantize(b, cols):
             nc.vector.quantize_mx(
@@ -214,36 +249,31 @@ def tile_list_burial_isotope_mobility_kernel(
                 in_=z_bf[:, b, PACK * cols.start : PACK * cols.stop],
             )
 
+        def combine(i):
+            nc.vector.scalar_tensor_tensor(
+                term[:, i, :], root[:, i, :], gain_of(i), soil[:, i, :], ALU.mult, ALU.subtract
+            )
+
         for i in range(PACK):
-            nc.scalar.activation(recip[:, i, :], both[:, i, :], ACT.Square)
-        for cols in HALVES:
-            nc.scalar.activation(recip[:, PACK:, cols], both[:, PACK:, cols], ACT.Square)
-        for i in range(PACK):
-            combine(i, slice(0, M))
-        interleave(0, HALVES[0], nc.vector.tensor_copy)
-        interleave(0, HALVES[1], nc.scalar.copy)
-        combine(PACK, PIECES[0])
-        quantize(0, HALVES[0])
-        for i in range(PACK + 1, TILES):
-            combine(i, PIECES[0])
-        interleave(1, PIECES[0], nc.vector.tensor_copy)
-        combine(PACK, PIECES[1])
-        quantize(1, PIECES[0])
-        for i in range(PACK + 1, TILES):
-            combine(i, PIECES[1])
-        quantize(0, HALVES[1])
-        interleave(1, PIECES[1], nc.vector.tensor_copy)
-        combine(PACK, PIECES[2])
-        quantize(1, PIECES[1])
-        for i in range(PACK + 1, TILES):
-            combine(i, PIECES[2])
-        interleave(1, PIECES[2], nc.vector.tensor_copy)
-        quantize(1, PIECES[2])
+            combine(i)
+        for cols, copy in zip(HALVES, (nc.vector.tensor_copy, nc.scalar.copy)):
+            copy(woven(0, cols), rows_of(term, 0, cols))
+        for i in range(PACK, TILES):
+            combine(i)
+            if i == PACK:
+                quantize(0, HALVES[0])
+        for c, cols in enumerate(PIECES):
+            nc.vector.tensor_copy(woven(1, cols), rows_of(term, 1, cols))
+            if c == 0:
+                quantize(0, HALVES[1])
+            else:
+                quantize(1, PIECES[c - 1])
+        quantize(1, PIECES[-1])
 
         for c, cols in enumerate(PIECES):
             width = cols.stop - cols.start
             result = keep.tile([P, N // P, width], F32, name="result%d" % c)
-            acc = [psum.tile([P, width], F32, name="acc", tag=("bank", "acc")[c % 2]) for j in range(N // P)]
+            acc = [psum.tile([P, width], F32, name="acc", tag="bank") for j in range(N // P)]
             for b in range(PASSES):
                 for j in range(N // P):
                     nc.tensor.matmul_mx(

@@ -26,7 +26,7 @@ PIECES = (slice(0, 256), slice(256, 384), slice(384, 512))
 HALVES = (slice(0, 256), slice(256, 512))
 LN5 = math.log(5.0)
 WORDS_AT = 20480
-TISSUE_AT = 28672
+EARLY = 2
 TABLE0_AT = 43008
 
 
@@ -115,14 +115,14 @@ def tile_list_burial_isotope_mobility_kernel(
 
         pick_words(0)
         nc.sync.dma_start(w4_raw[1][:], w4_halves[1].bitcast(I32))
-        order_w4(keep.tile([P, 1, PASSES, 2 * P], U8, name="w4_first", align_bytes=64), 0)
+        order_w4(keep.tile([P, 2, PASSES, 2 * P], U8, name="w4_first", align_bytes=64), 0)
         pick_words(1)
-        order_w4(shared.tile([P, 3, PASSES, 2 * P], U8, name="w4_next", align_bytes=64, offset=0), 1)
+        order_w4(shared.tile([P, 2, PASSES, 2 * P], U8, name="w4_next", align_bytes=64, offset=0), 2)
         order_w4(shared.tile([P, 4, PASSES, 2 * P], U8, name="w4_last", align_bytes=64, offset=2048), 4)
 
         w2_raw = [
             shared.tile([P, PACK, N], F32, name="w2_raw0", align_bytes=64, offset=TABLE0_AT + 2048),
-            shared.tile([P, PACK, N], F32, name="w2_raw1", align_bytes=64, offset=4096),
+            shared.tile([P, PACK, N], F32, name="w2_raw1", align_bytes=64, offset=6144),
         ]
         for b in range(PASSES):
             for e in range(4):
@@ -134,19 +134,20 @@ def tile_list_burial_isotope_mobility_kernel(
             return gain_sb[:, i // PACK, i % PACK : i % PACK + 1]
 
         h = [keep.tile([P, S], F32, name="h%d" % i, tag="h_later%d" % i, align_bytes=64) for i in range(TILES)]
-        tissue = [shared.tile([P, 2, 2, M], F32, name="tissue0", align_bytes=64, offset=TISSUE_AT)] + [
-            keep.tile([P, 2, 2, M], F32, name="tissue%d" % k) for k in range(1, TILES // 2)
-        ]
+        tissue = [keep.tile([P, 2, 2, M], F32, name="tissue%d" % k, tag="tissue_term%d" % k) for k in range(TILES // 2)]
         w2_bf = []
 
         def pick_soil(i):
             nc.vector.tensor_copy(soil[:, i, :], h[i][:].indirect(pos_sb[2][:]))
 
-        def scale_soil(i):
-            nc.vector.tensor_scalar(soil[:, i, :], soil[:, i, :], 0.25, gain_of(i), ALU.add, ALU.mult)
+        def scale_soil(i, engine, scaled_rows):
+            engine.tensor_scalar(scaled_rows, soil[:, i, :], 0.25, gain_of(i), ALU.add, ALU.mult)
+            offset_of[i] = scaled_rows
+
+        offset_of = {}
 
         def cast_w2(b):
-            w2_bf.append(keep.tile([P, N, PACK], BF16, name="w2_bf%d" % b, align_bytes=64))
+            w2_bf.append(keep.tile([P, N, PACK], BF16, name="w2_bf%d" % b, tag="w2_both%d" % b, align_bytes=64))
             nc.gpsimd.tensor_scalar(
                 w2_bf[b][:], w2_raw[b][:].rearrange("p t n -> p n t"), 1.0, 0.0, ALU.mult, ALU.add
             )
@@ -168,20 +169,23 @@ def tile_list_burial_isotope_mobility_kernel(
             for half in range(2):
                 copy = nc.scalar.copy if i == 0 else nc.vector.tensor_copy
                 copy(h[i][:, BANK * half : BANK * (half + 1)], banks[half][:])
-            for j in range(2):
-                nc.scalar.activation(
-                    tissue[i // 2][:, j, i % 2, :], h[i][:].indirect(pos_sb[j][:]), ACT.Sigmoid, bias=LN5
-                )
+            if i < TILES - 1:
+                for j in range(2):
+                    nc.scalar.activation(
+                        tissue[i // 2][:, j, i % 2, :], h[i][:].indirect(pos_sb[j][:]), ACT.Sigmoid, bias=LN5
+                    )
+            else:
+                logits = keep.tile([P, 2, M], F32, name="logits")
+                for j in range(2):
+                    nc.vector.tensor_copy(logits[:, j, :], h[i][:].indirect(pos_sb[j][:]))
+                nc.scalar.activation(tissue[i // 2][:, :, i % 2, :], logits[:], ACT.Sigmoid, bias=LN5)
 
         def product(pair, engine):
             engine.tensor_tensor(both[pair][:], tissue[pair][:, 0], tissue[pair][:, 1], ALU.mult)
 
         for b in range(PASSES):
             cast_w2(b)
-        both = [shared.tile([P, 2, M], F32, name="both0", align_bytes=64, offset=4096)] + [
-            keep.tile([P, 2, M], F32, name="both%d" % (k + 1), tag="h_later%d" % after, align_bytes=64)
-            for k, after in enumerate((0, 2, 5))
-        ]
+        both = [shared.tile([P, 2, M], F32, name="both%d" % k, align_bytes=64, offset=4096 * (k + 1)) for k in range(2)]
         product(0, nc.gpsimd)
         gain_sb = keep.tile([P, PASSES, 8], F32, name="gain_sb", tag="w4_gain", align_bytes=64)
         with nc.allow_non_contiguous_dma(reason="gain: one value for each partition and row tile"):
@@ -191,23 +195,21 @@ def tile_list_burial_isotope_mobility_kernel(
                         gain_sb[e:P:4, b, 0:PACK], gain.rearrange("(b u t e) -> b e u t", u=32, t=4, e=4)[b, e]
                     )
 
-        soil = shared.tile([P, TILES, M], F32, name="soil", align_bytes=64, offset=TISSUE_AT - 2048)
-        pick_soil(7)
-        pick_soil(0)
-        product(1, nc.vector)
-        pick_soil(1)
-        pick_soil(2)
-        for i in (7, 0, 1):
-            scale_soil(i)
-        product(2, nc.vector)
-        for i in range(3, 6):
+        soil = shared.tile([P, TILES, M], F32, name="soil", align_bytes=64, offset=WORDS_AT + 3 * 2048)
+        order = [TILES - 1] + list(range(TILES - 1))
+        for i in order:
             pick_soil(i)
-        product(3, nc.vector)
-        pick_soil(6)
-        for i in range(2, 7):
-            scale_soil(i)
+        product(1, nc.gpsimd)
+        soil_early = shared.tile([P, 4, M], F32, name="soil_early", align_bytes=64, offset=12288)
+        for k, i in enumerate((0, 1, 2, TILES - 1)):
+            scale_soil(i, nc.gpsimd, soil_early[:, k, :])
+        both.append(keep.tile([P, 2, M], F32, name="both2", tag="tissue_term1"))
+        product(2, nc.gpsimd)
+        soil_late = keep.tile([P, 4, M], F32, name="soil_late", tag="tissue_term2")
+        for k, i in enumerate(order[4:]):
+            scale_soil(i, nc.vector, soil_late[:, k, :])
 
-        w2_codes = keep.tile([P, PASSES, N], U32, name="w2_codes", tag="h_later%d" % (TILES - 2), align_bytes=64)
+        w2_codes = shared.tile([P, PASSES, N], U32, name="w2_codes", align_bytes=64, offset=WORDS_AT + 3 * 2048)
         w2_scale = keep.tile([P, PASSES, N], U8, name="w2_scale", align_bytes=64)
         for b in range(PASSES):
             nc.vector.quantize_mx(
@@ -216,22 +218,29 @@ def tile_list_burial_isotope_mobility_kernel(
                 in_=w2_bf[b][:].rearrange("p n t -> p (n t)"),
             )
 
+        both.append(keep.tile([P, 2, M], F32, name="both3", tag="w2_both1", align_bytes=64))
+        product(3, nc.vector)
         root = keep.tile([P, TILES, M], F32, name="root", tag="h_later%d" % (TILES - 1), align_bytes=64)
 
-        def inverse_root(rows):
-            nc.scalar.activation(root[:, rows, :], both[rows.start // 2][:], ACT.Abs_reciprocal_sqrt, bias=4.0, scale=-2.56)
+        def inverse_root(pair):
+            rows = slice(2 * pair, 2 * pair + 2)
+            nc.scalar.activation(root[:, rows, :], both[pair][:], ACT.Abs_reciprocal_sqrt, bias=4.0, scale=-2.56)
 
-        def square(rows):
-            nc.scalar.activation(root[:, rows, :], root[:, rows, :], ACT.Square)
+        def square(pair, cols):
+            rows = slice(2 * pair, 2 * pair + 2)
+            nc.scalar.activation(root[:, rows, cols], root[:, rows, cols], ACT.Square)
 
-        pairs = [slice(i, i + 2) for i in range(0, TILES, 2)]
-        inverse_root(pairs[0])
-        for rows, following in zip(pairs, pairs[1:]):
-            inverse_root(following)
-            square(rows)
-        square(pairs[-1])
+        whole = slice(0, M)
+        inverse_root(0)
+        inverse_root(1)
+        square(1, whole)
+        inverse_root(2)
+        square(2, whole)
+        inverse_root(3)
+        for cols in HALVES:
+            square(3, cols)
 
-        term = keep.tile([P, TILES, M], F32, name="term")
+        term = keep.tile([P, TILES, M], F32, name="term", tag="tissue_term3")
         z_bf = keep.tile([P, PASSES, M * PACK], BF16, name="z_bf", align_bytes=64)
         z_codes = keep.tile([P, PASSES, M], U32, name="z_codes", align_bytes=64)
         z_scale = keep.tile([P, PASSES, M], U8, name="z_scale", align_bytes=64)
@@ -249,26 +258,35 @@ def tile_list_burial_isotope_mobility_kernel(
                 in_=z_bf[:, b, PACK * cols.start : PACK * cols.stop],
             )
 
-        def combine(i):
+        def combine(i, cols):
             nc.vector.scalar_tensor_tensor(
-                term[:, i, :], root[:, i, :], gain_of(i), soil[:, i, :], ALU.mult, ALU.subtract
+                term[:, i, cols], root[:, i, cols], gain_of(i), offset_of[i][:, cols], ALU.mult, ALU.subtract
             )
 
-        for i in range(PACK):
-            combine(i)
-        for cols, copy in zip(HALVES, (nc.vector.tensor_copy, nc.scalar.copy)):
-            copy(woven(0, cols), rows_of(term, 0, cols))
-        for i in range(PACK, TILES):
-            combine(i)
-            if i == PACK:
-                quantize(0, HALVES[0])
-        for c, cols in enumerate(PIECES):
-            nc.vector.tensor_copy(woven(1, cols), rows_of(term, 1, cols))
-            if c == 0:
-                quantize(0, HALVES[1])
-            else:
-                quantize(1, PIECES[c - 1])
-        quantize(1, PIECES[-1])
+        def interleave(b, cols, copy):
+            copy(woven(b, cols), rows_of(term, b, cols))
+
+        for i in range(EARLY):
+            nc.vector.scalar_tensor_tensor(term[:, i, :], root[:, i, :], gain_of(i), root[:, i, :], ALU.mult, ALU.mult)
+        nc.vector.tensor_tensor(term[:, :EARLY, :], term[:, :EARLY, :], soil_early[:, :EARLY, :], ALU.subtract)
+        for i in range(EARLY, PACK):
+            combine(i, whole)
+        interleave(0, HALVES[0], nc.vector.tensor_copy)
+        interleave(0, HALVES[1], nc.scalar.copy)
+        combine(4, whole)
+        quantize(0, HALVES[0])
+        combine(5, whole)
+        combine(6, HALVES[0])
+        combine(7, HALVES[0])
+        combine(6, HALVES[1])
+        interleave(1, PIECES[0], nc.vector.tensor_copy)
+        combine(7, HALVES[1])
+        quantize(1, PIECES[0])
+        interleave(1, PIECES[1], nc.vector.tensor_copy)
+        quantize(0, HALVES[1])
+        interleave(1, PIECES[2], nc.vector.tensor_copy)
+        quantize(1, PIECES[1])
+        quantize(1, PIECES[2])
 
         for c, cols in enumerate(PIECES):
             width = cols.stop - cols.start

@@ -2,6 +2,7 @@ import math
 from contextlib import ExitStack
 
 import concourse.mybir as mybir
+from concourse.masks import make_identity
 
 K, H, N, T, S, M = 1024, 1024, 512, 2048, 1024, 512
 FLOPS = 2 * K * H * S + 2 * H * N * M
@@ -21,13 +22,15 @@ P = 128
 PACK = 4
 PASSES = 2
 TILES = H // P
+PAIRS = TILES // 2
 BANK = 512
-PIECES = (slice(0, 256), slice(256, 384), slice(384, 512))
-HALVES = (slice(0, 256), slice(256, 512))
+CHUNKS = M // P
+FIRST = 2
 LN5 = math.log(5.0)
-WORDS_AT = 20480
-EARLY = 2
-TABLE0_AT = 43008
+
+TABLE1_AT = 4096
+TABLE0_AT = 16384
+WORDS_AT = 27648
 
 
 def tile_list_burial_isotope_mobility_kernel(
@@ -37,32 +40,31 @@ def tile_list_burial_isotope_mobility_kernel(
     with ExitStack() as ctx:
         keep = ctx.enter_context(tc.tile_pool(name="keep", bufs=1))
         shared = ctx.enter_context(tc.tile_pool(name="shared", bufs=1))
-        psum = ctx.enter_context(tc.psum_pool(name="psum", bufs=8))
+        psum = ctx.enter_context(tc.psum_pool(name="psum", bufs=1))
+
+        def bank(number, shape, name):
+            return psum.tile(shape, F32, name=name, tag="bank%d" % number)
 
         offs_sb = keep.tile([P, S // 16], U16, name="offs_sb")
         pos_sb = [keep.tile([P, M // 16], U16, name="pos%d_sb" % j) for j in range(3)]
         tab_scale_rows = keep.tile([P, T], U8, name="tab_scale_rows", align_bytes=64)
         tab_sb = [
             shared.tile([P, T], I32, name="tab_sb0", align_bytes=64, offset=TABLE0_AT),
-            shared.tile([P, T], I32, name="tab_sb1", align_bytes=64, offset=0),
+            shared.tile([P, T], I32, name="tab_sb1", align_bytes=64, offset=TABLE1_AT),
         ]
-        w4_raw = [
-            keep.tile([P, PASSES, H // 4], I32, name="w4_raw0", tag="w4_gain", align_bytes=64),
-            shared.tile([P, PASSES, H // 4], I32, name="w4_raw1", align_bytes=64, offset=TABLE0_AT),
-        ]
-        w4_halves = w4_words.rearrange("a p (b c) -> b p a c", b=2)
-        w4_scale_rows = keep.tile([32, H], U8, name="w4_scale_rows", align_bytes=64)
+        w4_rows = w4_words.rearrange("a p c -> p a c")
+        w4_first = keep.tile([P, PASSES, 2 * P * FIRST], U8, name="w4_first", align_bytes=64)
         planes = [keep.tile([P, S + H], U8, name="planes%d" % a, align_bytes=64) for a in range(PASSES)]
 
         nc.sync.dma_start(offs_sb[:], offs)
         nc.sync.dma_start(
             tab_scale_rows[0:32, :].bitcast(I32), tab_scales.rearrange("a q t -> (a q) t").bitcast(I32)
         )
-        nc.sync.dma_start(w4_scale_rows[:].bitcast(I32), w4_scales.rearrange("a q c -> (a q) c").bitcast(I32))
+        nc.sync.dma_start(planes[0][0:32, S:].bitcast(I32), w4_scales.rearrange("a q c -> (a q) c").bitcast(I32))
         nc.sync.dma_start(pos_sb[0][:], pos1)
         nc.sync.dma_start(pos_sb[1][:], pos2)
         nc.sync.dma_start(tab_sb[0][:], tab_words[0].rearrange("p t i -> p (t i)").bitcast(I32))
-        nc.sync.dma_start(w4_raw[0][:], w4_halves[0].bitcast(I32))
+        nc.sync.dma_start(w4_first[:].bitcast(I32), w4_rows[:, :, : 2 * P * FIRST].bitcast(I32))
         nc.sync.dma_start(tab_sb[1][:], tab_words[1].rearrange("p t i -> p (t i)").bitcast(I32))
         nc.sync.dma_start(pos_sb[2][:], pos3)
 
@@ -70,15 +72,13 @@ def tile_list_burial_isotope_mobility_kernel(
         nc.gpsimd.memset(warm[:, 0, :], 0.0)
         nc.scalar.activation(warm[:, 1, :], warm[:, 0, :], ACT.Sigmoid)
 
-        nc.vector.memset(tab_scale_rows[32:64, :].bitcast(I32), 0)
-        nc.vector.memset(tab_scale_rows[64:128, :].bitcast(I32), 0)
-        for a in range(PASSES):
-            nc.gpsimd.memset(planes[a][:].bitcast(I32), 0)
+        for rows in (slice(32, 64), slice(64, 128)):
+            nc.vector.memset(tab_scale_rows[rows, :].bitcast(I32), 0)
+            nc.gpsimd.memset(planes[0][rows, :].bitcast(I32), 0)
+        nc.gpsimd.memset(planes[1][:].bitcast(I32), 0)
+        ident = keep.tile([P, P], F32, name="ident", align_bytes=64)
+        make_identity(nc, ident[:])
 
-        nc.vector.tensor_copy(
-            planes[0][0:32, S:].bitcast(I32).rearrange("p (b t u) -> p b t u", t=4, u=32),
-            w4_scale_rows[:].bitcast(I32).rearrange("p (b u t) -> p b t u", t=4, u=32),
-        )
         picked_scale_rows = keep.tile([P, S], U8, name="picked_scale_rows", align_bytes=64)
         nc.vector.tensor_copy(picked_scale_rows[:], tab_scale_rows[:].indirect(offs_sb[:]))
         nc.vector.tensor_copy(planes[0][0:32, :S].bitcast(I32), picked_scale_rows[0:32, :].bitcast(I32))
@@ -102,64 +102,36 @@ def tile_list_burial_isotope_mobility_kernel(
                     tab_sb[a][:].bitcast(U32).indirect(offs_sb[:, 32 * half : 32 * half + 32]),
                 )
 
-        w4_of = {}
-
-        def order_w4(run, first):
-            count = run.shape[1]
-            b, t = divmod(first, PACK)
-            nc.vector.tensor_copy(
-                run[:].bitcast(I32).rearrange("p t a (u e) -> p t a u e", e=2), w4_raw[b][:].rearrange("p a (u t e) -> p t a u e", t=4, e=2)[:, t : t + count]
-            )
-            for k in range(count):
-                w4_of[first + k] = (run, k)
-
         pick_words(0)
-        nc.sync.dma_start(w4_raw[1][:], w4_halves[1].bitcast(I32))
-        order_w4(keep.tile([P, 2, PASSES, 2 * P], U8, name="w4_first", align_bytes=64), 0)
+        w4_rest = shared.tile([P, PASSES, 2 * P * (TILES - FIRST)], U8, name="w4_rest", align_bytes=64, offset=TABLE0_AT)
+        nc.sync.dma_start(w4_rest[:].bitcast(I32), w4_rows[:, :, 2 * P * FIRST :].bitcast(I32))
         pick_words(1)
-        order_w4(shared.tile([P, 2, PASSES, 2 * P], U8, name="w4_next", align_bytes=64, offset=0), 2)
-        order_w4(shared.tile([P, 4, PASSES, 2 * P], U8, name="w4_last", align_bytes=64, offset=2048), 4)
+
+        def w4_of(i, a):
+            if i < FIRST:
+                return w4_first[:, a, 2 * P * i : 2 * P * (i + 1)]
+            return w4_rest[:, a, 2 * P * (i - FIRST) : 2 * P * (i - FIRST + 1)]
 
         w2_raw = [
-            shared.tile([P, PACK, N], F32, name="w2_raw0", align_bytes=64, offset=TABLE0_AT + 2048),
-            shared.tile([P, PACK, N], F32, name="w2_raw1", align_bytes=64, offset=6144),
+            shared.tile([P, PACK, N], F32, name="w2_raw0", align_bytes=64, offset=TABLE0_AT + 3072),
+            shared.tile([P, PACK, N], F32, name="w2_raw1", align_bytes=64, offset=TABLE1_AT + 4096),
         ]
         for b in range(PASSES):
-            for e in range(4):
-                nc.sync.dma_start(
-                    w2_raw[b][e:P:4, :, :],
-                    w2[512 * b : 512 * (b + 1), :].rearrange("(u t e) n -> e u t n", t=4, e=4)[e],
-                )
-        def gain_of(i):
-            return gain_sb[:, i // PACK, i % PACK : i % PACK + 1]
+            nc.sync.dma_start(w2_raw[b][:], w2[512 * b : 512 * (b + 1), :].rearrange("(p t) n -> p t n", t=PACK))
+        gain_rows = shared.tile([P, H], F32, name="gain_rows", align_bytes=64, offset=TABLE1_AT - 2048)
+        nc.sync.dma_start(gain_rows[:], gain.partition_broadcast(P))
 
-        h = [keep.tile([P, S], F32, name="h%d" % i, tag="h_later%d" % i, align_bytes=64) for i in range(TILES)]
-        tissue = [keep.tile([P, 2, 2, M], F32, name="tissue%d" % k, tag="tissue_term%d" % k) for k in range(TILES // 2)]
-        w2_bf = []
-
-        def pick_soil(i):
-            nc.vector.tensor_copy(soil[:, i, :], h[i][:].indirect(pos_sb[2][:]))
-
-        def scale_soil(i, engine, scaled_rows):
-            engine.tensor_scalar(scaled_rows, soil[:, i, :], 0.25, gain_of(i), ALU.add, ALU.mult)
-            offset_of[i] = scaled_rows
-
-        offset_of = {}
-
-        def cast_w2(b):
-            w2_bf.append(keep.tile([P, N, PACK], BF16, name="w2_bf%d" % b, tag="w2_both%d" % b, align_bytes=64))
-            nc.gpsimd.tensor_scalar(
-                w2_bf[b][:], w2_raw[b][:].rearrange("p t n -> p n t"), 1.0, 0.0, ALU.mult, ALU.add
-            )
+        neg_h = [keep.tile([P, S], F32, name="neg_h%d" % i, tag="h_later%d" % i, align_bytes=64) for i in range(TILES)]
+        tissue = [keep.tile([P, 2, 2, M], F32, name="tissue%d" % k, tag="tissue%d" % k, align_bytes=64) for k in range(PAIRS)]
 
         for i in range(TILES):
             banks = []
             for half in range(2):
-                banks.append(psum.tile([P, BANK], F32, name="bank", tag="bank"))
+                banks.append(bank((2 * i + half) % 8, [P, BANK], "h_bank"))
                 for a in range(PASSES):
                     nc.tensor.matmul_mx(
                         out=banks[half][:],
-                        lhsT=w4_of[i][0][:, w4_of[i][1], a, :].bitcast(FP4X4),
+                        lhsT=w4_of(i, a).bitcast(FP4X4),
                         lhsT_scale=planes[a][:, S + P * i : S + P * (i + 1)],
                         rhs=v_words[a, half][:].bitcast(FP8X4),
                         rhs_scale=planes[a][:, BANK * half : BANK * (half + 1)],
@@ -167,49 +139,54 @@ def tile_list_burial_isotope_mobility_kernel(
                         stop=(a == PASSES - 1),
                     )
             for half in range(2):
-                copy = nc.scalar.copy if i == 0 else nc.vector.tensor_copy
-                copy(h[i][:, BANK * half : BANK * (half + 1)], banks[half][:])
-            if i < TILES - 1:
-                for j in range(2):
-                    nc.scalar.activation(
-                        tissue[i // 2][:, j, i % 2, :], h[i][:].indirect(pos_sb[j][:]), ACT.Sigmoid, bias=LN5
-                    )
-            else:
-                logits = keep.tile([P, 2, M], F32, name="logits")
-                for j in range(2):
-                    nc.vector.tensor_copy(logits[:, j, :], h[i][:].indirect(pos_sb[j][:]))
-                nc.scalar.activation(tissue[i // 2][:, :, i % 2, :], logits[:], ACT.Sigmoid, bias=LN5)
+                cols = slice(BANK * half, BANK * (half + 1))
+                if (i, half) == (0, 1):
+                    nc.scalar.activation(neg_h[i][:, cols], banks[half][:], ACT.Copy, scale=-1.0)
+                else:
+                    nc.vector.tensor_scalar(neg_h[i][:, cols], banks[half][:], -1.0, None, ALU.mult)
+            for j in range(2):
+                nc.scalar.activation(
+                    tissue[i // 2][:, j, i % 2, :], neg_h[i][:].indirect(pos_sb[j][:]), ACT.Sigmoid, bias=LN5, scale=-1.0
+                )
 
-        def product(pair, engine):
-            engine.tensor_tensor(both[pair][:], tissue[pair][:, 0], tissue[pair][:, 1], ALU.mult)
-
+        w2_bf = []
         for b in range(PASSES):
-            cast_w2(b)
-        both = [shared.tile([P, 2, M], F32, name="both%d" % k, align_bytes=64, offset=4096 * (k + 1)) for k in range(2)]
-        product(0, nc.gpsimd)
-        gain_sb = keep.tile([P, PASSES, 8], F32, name="gain_sb", tag="w4_gain", align_bytes=64)
-        with nc.allow_non_contiguous_dma(reason="gain: one value for each partition and row tile"):
-            for b in range(PASSES):
-                for e in range(4):
-                    nc.sync.dma_start(
-                        gain_sb[e:P:4, b, 0:PACK], gain.rearrange("(b u t e) -> b e u t", u=32, t=4, e=4)[b, e]
-                    )
+            w2_bf.append(keep.tile([P, N, PACK], BF16, name="w2_bf%d" % b, tag="w2_bf%d" % b, align_bytes=64))
+            nc.gpsimd.tensor_scalar(w2_bf[b][:], w2_raw[b][:].rearrange("p t n -> p n t"), 1.0, 0.0, ALU.mult, ALU.add)
 
-        soil = shared.tile([P, TILES, M], F32, name="soil", align_bytes=64, offset=WORDS_AT + 3 * 2048)
-        order = [TILES - 1] + list(range(TILES - 1))
-        for i in order:
-            pick_soil(i)
-        product(1, nc.gpsimd)
-        soil_early = shared.tile([P, 4, M], F32, name="soil_early", align_bytes=64, offset=12288)
-        for k, i in enumerate((0, 1, 2, TILES - 1)):
-            scale_soil(i, nc.gpsimd, soil_early[:, k, :])
-        both.append(keep.tile([P, 2, M], F32, name="both2", tag="tissue_term1"))
-        product(2, nc.gpsimd)
-        soil_late = keep.tile([P, 4, M], F32, name="soil_late", tag="tissue_term2")
-        for k, i in enumerate(order[4:]):
-            scale_soil(i, nc.vector, soil_late[:, k, :])
+        neg_soil = shared.tile([P, TILES, M], F32, name="neg_soil", align_bytes=64, offset=WORDS_AT + 3 * 2048)
+        sums = {}
+        for i in range(TILES):
+            nc.vector.tensor_copy(neg_soil[:, i, :], neg_h[i][:].indirect(pos_sb[2][:]))
+            b, t = divmod(i, PACK)
+            for c in range(CHUNKS):
+                if t == 0:
+                    sums[c, b] = bank(2 * c + b, [P, BANK], "sums")
+                nc.tensor.matmul(
+                    sums[c, b][:, P * t : P * (t + 1)],
+                    neg_soil[:, i, P * c : P * (c + 1)],
+                    ident[:],
+                    start=(t == 0),
+                    stop=False,
+                    is_transpose=True,
+                )
 
-        w2_codes = shared.tile([P, PASSES, N], U32, name="w2_codes", align_bytes=64, offset=WORDS_AT + 3 * 2048)
+        both = {}
+        squared = {}
+
+        def product(pair, engine, tile):
+            both[pair] = tile
+            engine.tensor_tensor(tile[:], tissue[pair][:, 0], tissue[pair][:, 1], ALU.mult)
+
+        product(0, nc.gpsimd, shared.tile([P, 2, M], F32, name="both0", align_bytes=64, offset=TABLE1_AT + 4096))
+        shifted = keep.tile([P, 2, M], F32, name="shifted", tag="shifted_both1")
+        nc.gpsimd.tensor_scalar(shifted[:], both[0][:], 1.0, -3.125, ALU.mult, ALU.add)
+        squared[0] = keep.tile([P, 2, M], F32, name="squared0", tag="tissue0", align_bytes=64)
+        nc.gpsimd.tensor_tensor(squared[0][:], shifted[:], both[0][:], ALU.mult)
+        product(1, nc.gpsimd, keep.tile([P, 2, M], F32, name="both1", tag="shifted_both1"))
+        product(2, nc.gpsimd, keep.tile([P, 2, M], F32, name="both2", tag="tissue1", align_bytes=64))
+
+        w2_codes = keep.tile([P, PASSES, N], U32, name="w2_codes", tag="tissue2", align_bytes=64)
         w2_scale = keep.tile([P, PASSES, N], U8, name="w2_scale", align_bytes=64)
         for b in range(PASSES):
             nc.vector.quantize_mx(
@@ -218,98 +195,94 @@ def tile_list_burial_isotope_mobility_kernel(
                 in_=w2_bf[b][:].rearrange("p n t -> p (n t)"),
             )
 
-        both.append(keep.tile([P, 2, M], F32, name="both3", tag="w2_both1", align_bytes=64))
-        product(3, nc.vector)
-        root = keep.tile([P, TILES, M], F32, name="root", tag="h_later%d" % (TILES - 1), align_bytes=64)
+        def square_on_vector(pair, tile):
+            squared[pair] = tile
+            nc.vector.scalar_tensor_tensor(tile[:], both[pair][:], -3.125, both[pair][:], ALU.add, ALU.mult)
 
-        def inverse_root(pair):
-            rows = slice(2 * pair, 2 * pair + 2)
-            nc.scalar.activation(root[:, rows, :], both[pair][:], ACT.Abs_reciprocal_sqrt, bias=4.0, scale=-2.56)
+        square_on_vector(1, keep.tile([P, 2, M], F32, name="squared1", tag="w2_bf0", align_bytes=64))
+        square_on_vector(2, keep.tile([P, 2, M], F32, name="squared2", tag="w2_bf1", align_bytes=64))
+        product(3, nc.vector, keep.tile([P, 2, M], F32, name="both3", tag="shifted_both1"))
+        square_on_vector(3, keep.tile([P, 2, M], F32, name="squared3", tag="tissue3", align_bytes=64))
 
-        def square(pair, cols):
-            rows = slice(2 * pair, 2 * pair + 2)
-            nc.scalar.activation(root[:, rows, cols], root[:, rows, cols], ACT.Square)
+        inverse = keep.tile([P, TILES, M], F32, name="inverse", tag="h_later7", align_bytes=64)
 
-        whole = slice(0, M)
-        inverse_root(0)
-        inverse_root(1)
-        square(1, whole)
-        inverse_root(2)
-        square(2, whole)
-        inverse_root(3)
-        for cols in HALVES:
-            square(3, cols)
-
-        term = keep.tile([P, TILES, M], F32, name="term", tag="tissue_term3")
-        z_bf = keep.tile([P, PASSES, M * PACK], BF16, name="z_bf", align_bytes=64)
-        z_codes = keep.tile([P, PASSES, M], U32, name="z_codes", align_bytes=64)
-        z_scale = keep.tile([P, PASSES, M], U8, name="z_scale", align_bytes=64)
-
-        def woven(b, cols):
-            return z_bf[:, b, PACK * cols.start : PACK * cols.stop].rearrange("p (g i t) -> p g t i", i=4, t=PACK)
-
-        def rows_of(tile, b, cols):
-            return tile[:, PACK * b : PACK * (b + 1), cols].rearrange("p t (g i) -> p g t i", i=4)
-
-        def quantize(b, cols):
-            nc.vector.quantize_mx(
-                out=z_codes[:, b, cols].bitcast(FP8X4),
-                scales=z_scale[:, b, cols],
-                in_=z_bf[:, b, PACK * cols.start : PACK * cols.stop],
+        def invert(half, pair):
+            cols = slice(2 * P * half, 2 * P * (half + 1))
+            nc.scalar.activation(
+                inverse[:, 2 * pair : 2 * pair + 2, cols], squared[pair][:, :, cols], ACT.Abs_reciprocal_sqrt, bias=16.0, scale=6.5536
             )
+            for c in (2 * half, 2 * half + 1):
+                for i in (2 * pair, 2 * pair + 1):
+                    b, t = divmod(i, PACK)
+                    nc.tensor.matmul(
+                        sums[c, b][:, P * t : P * (t + 1)],
+                        inverse[:, i, P * c : P * (c + 1)],
+                        ident[:],
+                        start=False,
+                        stop=(t == PACK - 1),
+                        is_transpose=True,
+                    )
 
-        def combine(i, cols):
+        z_rows = {}
+        acc = {}
+
+        def scale_by_gain(c, b):
+            z_rows[c, b] = keep.tile([P, BANK], BF16, name="z_rows%d_%d" % (c, b), align_bytes=64)
             nc.vector.scalar_tensor_tensor(
-                term[:, i, cols], root[:, i, cols], gain_of(i), offset_of[i][:, cols], ALU.mult, ALU.subtract
+                z_rows[c, b][:], sums[c, b][:], -0.25, gain_rows[:, BANK * b : BANK * (b + 1)], ALU.add, ALU.mult
             )
 
-        def interleave(b, cols, copy):
-            copy(woven(b, cols), rows_of(term, b, cols))
+        z_words = {}
 
-        for i in range(EARLY):
-            nc.vector.scalar_tensor_tensor(term[:, i, :], root[:, i, :], gain_of(i), root[:, i, :], ALU.mult, ALU.mult)
-        nc.vector.tensor_tensor(term[:, :EARLY, :], term[:, :EARLY, :], soil_early[:, :EARLY, :], ALU.subtract)
-        for i in range(EARLY, PACK):
-            combine(i, whole)
-        interleave(0, HALVES[0], nc.vector.tensor_copy)
-        interleave(0, HALVES[1], nc.scalar.copy)
-        combine(4, whole)
-        quantize(0, HALVES[0])
-        combine(5, whole)
-        combine(6, HALVES[0])
-        combine(7, HALVES[0])
-        combine(6, HALVES[1])
-        interleave(1, PIECES[0], nc.vector.tensor_copy)
-        combine(7, HALVES[1])
-        quantize(1, PIECES[0])
-        interleave(1, PIECES[1], nc.vector.tensor_copy)
-        quantize(0, HALVES[1])
-        interleave(1, PIECES[2], nc.vector.tensor_copy)
-        quantize(1, PIECES[1])
-        quantize(1, PIECES[2])
+        def turn_back(c, b, copy_words):
+            turned = bank(2 * c + b, [P, 2, P], "turned")
+            words = z_rows[c, b][:].bitcast(F32)
+            for u in range(2):
+                nc.tensor.transpose(turned[:, u, :], words[:, u : 2 * P : 2], ident[:])
+            z_words[c, b] = keep.tile([P, P, 2], F32, name="z_words%d_%d" % (c, b), align_bytes=64)
+            copy_words(z_words[c, b][:], turned[:].rearrange("p u m -> p m u"))
 
-        for c, cols in enumerate(PIECES):
-            width = cols.stop - cols.start
-            result = keep.tile([P, N // P, width], F32, name="result%d" % c)
-            acc = [psum.tile([P, width], F32, name="acc", tag="bank") for j in range(N // P)]
-            for b in range(PASSES):
-                for j in range(N // P):
-                    nc.tensor.matmul_mx(
-                        out=acc[j][:],
-                        lhsT=w2_codes[:, b, P * j : P * (j + 1)].bitcast(FP8X4),
-                        lhsT_scale=w2_scale[:, b, P * j : P * (j + 1)],
-                        rhs=z_codes[:, b, cols].bitcast(FP8X4),
-                        rhs_scale=z_scale[:, b, cols],
-                        start=(b == 0),
-                        stop=(b == PASSES - 1),
-                    )
+        def multiply(c, b):
+            z_codes = keep.tile([P, P], U32, name="z_codes%d_%d" % (c, b), align_bytes=64)
+            z_scale = keep.tile([P, P], U8, name="z_scale%d_%d" % (c, b), align_bytes=64)
+            nc.vector.quantize_mx(
+                out=z_codes[:].bitcast(FP8X4),
+                scales=z_scale[:],
+                in_=z_words[c, b][:].rearrange("p m u -> p (m u)").bitcast(BF16),
+            )
+            if b == 0:
+                acc[c] = bank(2 * c, [P, N // P, P], "acc")
             for j in range(N // P):
-                if c == len(PIECES) - 1 and j % 2 == 1:
-                    nc.vector.tensor_copy(result[:, j, :], acc[j][:])
-                else:
-                    nc.scalar.copy(result[:, j, :], acc[j][:])
-                if j % 2 == 1:
-                    nc.sync.dma_start(
-                        out[P * (j - 1) : P * (j + 1), cols].rearrange("(j p) m -> p j m", p=P),
-                        result[:, j - 1 : j + 1, :],
-                    )
+                nc.tensor.matmul_mx(
+                    out=acc[c][:, j, :],
+                    lhsT=w2_codes[:, b, P * j : P * (j + 1)].bitcast(FP8X4),
+                    lhsT_scale=w2_scale[:, b, P * j : P * (j + 1)],
+                    rhs=z_codes[:].bitcast(FP8X4),
+                    rhs_scale=z_scale[:],
+                    start=(b == 0 and j == 0),
+                    stop=(b == PASSES - 1 and j == N // P - 1),
+                )
+
+        def store(c, copy_out):
+            result = keep.tile([P, N // P, P], F32, name="result%d" % c)
+            copy_out(result[:], acc[c][:])
+            nc.sync.dma_start(out[:, P * c : P * (c + 1)].rearrange("(j p) m -> p j m", p=P), result[:])
+
+        for b in range(PASSES):
+            for half in range(2):
+                for pair in (2 * b, 2 * b + 1):
+                    invert(half, pair)
+        for c in range(CHUNKS):
+            scale_by_gain(c, 0)
+        for c in range(CHUNKS):
+            turn_back(c, 0, nc.vector.tensor_copy if c < 2 else nc.scalar.copy)
+        for half in range(2):
+            for c in (2 * half, 2 * half + 1):
+                multiply(c, 0)
+            for c in (2 * half, 2 * half + 1):
+                scale_by_gain(c, 1)
+                turn_back(c, 1, nc.scalar.copy)
+        for c in range(CHUNKS):
+            multiply(c, 1)
+        for c in range(CHUNKS):
+            store(c, nc.vector.tensor_copy if c == 2 else nc.scalar.copy)

@@ -27,10 +27,13 @@ BANK = 512
 CHUNKS = M // P
 FIRST = 2
 LN5 = math.log(5.0)
+HALVES = (slice(0, 256), slice(256, 512))
+PIECES = (slice(0, 256), slice(256, 384), slice(384, 512))
 
 TABLE1_AT = 4096
 TABLE0_AT = 16384
 WORDS_AT = 27648
+LATE_AT = 51200
 
 
 def tile_list_burial_isotope_mobility_kernel(
@@ -60,7 +63,8 @@ def tile_list_burial_isotope_mobility_kernel(
         nc.sync.dma_start(
             tab_scale_rows[0:32, :].bitcast(I32), tab_scales.rearrange("a q t -> (a q) t").bitcast(I32)
         )
-        nc.sync.dma_start(planes[0][0:32, S:].bitcast(I32), w4_scales.rearrange("a q c -> (a q) c").bitcast(I32))
+        w4_scale_rows = keep.tile([32, H], U8, name="w4_scale_rows", align_bytes=64)
+        nc.sync.dma_start(w4_scale_rows[:].bitcast(I32), w4_scales.rearrange("a q c -> (a q) c").bitcast(I32))
         nc.sync.dma_start(pos_sb[0][:], pos1)
         nc.sync.dma_start(pos_sb[1][:], pos2)
         nc.sync.dma_start(tab_sb[0][:], tab_words[0].rearrange("p t i -> p (t i)").bitcast(I32))
@@ -79,6 +83,11 @@ def tile_list_burial_isotope_mobility_kernel(
         ident = keep.tile([P, P], F32, name="ident", align_bytes=64)
         make_identity(nc, ident[:])
 
+        nc.vector.tensor_copy(planes[0][0:32, S : S + BANK].bitcast(I32), w4_scale_rows[:, :BANK].bitcast(I32))
+        nc.vector.tensor_copy(
+            planes[0][0:32, S + BANK :].bitcast(I32).rearrange("p (t u) -> p t u", t=PACK),
+            w4_scale_rows[:, BANK:].bitcast(I32).rearrange("p (u t) -> p t u", t=PACK),
+        )
         picked_scale_rows = keep.tile([P, S], U8, name="picked_scale_rows", align_bytes=64)
         nc.vector.tensor_copy(picked_scale_rows[:], tab_scale_rows[:].indirect(offs_sb[:]))
         nc.vector.tensor_copy(planes[0][0:32, :S].bitcast(I32), picked_scale_rows[0:32, :].bitcast(I32))
@@ -95,7 +104,7 @@ def tile_list_burial_isotope_mobility_kernel(
         def pick_words(a):
             for half in range(2):
                 v_words[a, half] = shared.tile(
-                    [P, BANK], U32, name="v_words%d_%d" % (a, half), align_bytes=64, offset=WORDS_AT + 2048 * (2 * a + half)
+                    [P, BANK], U32, name="v_words%d_%d" % (a, half), align_bytes=64, offset=WORDS_AT + 4096 * (2 * a + half)
                 )
                 nc.vector.tensor_copy(
                     v_words[a, half][:],
@@ -103,23 +112,37 @@ def tile_list_burial_isotope_mobility_kernel(
                 )
 
         pick_words(0)
-        w4_rest = shared.tile([P, PASSES, 2 * P * (TILES - FIRST)], U8, name="w4_rest", align_bytes=64, offset=TABLE0_AT)
-        nc.sync.dma_start(w4_rest[:].bitcast(I32), w4_rows[:, :, 2 * P * FIRST :].bitcast(I32))
-        pick_words(1)
-
-        def w4_of(i, a):
-            if i < FIRST:
-                return w4_first[:, a, 2 * P * i : 2 * P * (i + 1)]
-            return w4_rest[:, a, 2 * P * (i - FIRST) : 2 * P * (i - FIRST + 1)]
-
+        w4_next = shared.tile([P, PASSES, 2 * P * (PACK - FIRST)], U8, name="w4_next", align_bytes=64, offset=TABLE0_AT)
+        nc.sync.dma_start(w4_next[:].bitcast(I32), w4_rows[:, :, 2 * P * FIRST : 2 * P * PACK].bitcast(I32))
         w2_raw = [
             shared.tile([P, PACK, N], F32, name="w2_raw0", align_bytes=64, offset=TABLE0_AT + 3072),
             shared.tile([P, PACK, N], F32, name="w2_raw1", align_bytes=64, offset=TABLE1_AT + 4096),
         ]
-        for b in range(PASSES):
-            nc.sync.dma_start(w2_raw[b][:], w2[512 * b : 512 * (b + 1), :].rearrange("(p t) n -> p t n", t=PACK))
-        gain_rows = shared.tile([P, H], F32, name="gain_rows", align_bytes=64, offset=TABLE1_AT - 2048)
-        nc.sync.dma_start(gain_rows[:], gain.partition_broadcast(P))
+        nc.sync.dma_start(w2_raw[0][:], w2[:BANK, :].rearrange("(p t) n -> p t n", t=PACK))
+        w4_raw = shared.tile([P, PASSES, H // 4], I32, name="w4_raw", align_bytes=64, offset=TABLE0_AT + 1024)
+        nc.sync.dma_start(w4_raw[:], w4_rows[:, :, 2 * P * PACK :].bitcast(I32))
+        pick_words(1)
+        w4_last = keep.tile([P, PACK, PASSES, 2 * P], U8, name="w4_last", align_bytes=64)
+        nc.vector.tensor_copy(
+            w4_last[:].bitcast(I32).rearrange("p t a (u e) -> p t a u e", e=2),
+            w4_raw[:].rearrange("p a (u t e) -> p t a u e", t=PACK, e=2),
+        )
+
+        def w4_of(i, a):
+            if i < FIRST:
+                return w4_first[:, a, 2 * P * i : 2 * P * (i + 1)]
+            if i < PACK:
+                return w4_next[:, a, 2 * P * (i - FIRST) : 2 * P * (i - FIRST + 1)]
+            return w4_last[:, i - PACK, a, :]
+
+        for e in range(4):
+            nc.sync.dma_start(w2_raw[1][e:P:4, :, :], w2[BANK:, :].rearrange("(u t e) n -> e u t n", t=PACK, e=4)[e])
+        gain_rows = shared.tile([P, BANK], F32, name="gain_rows", align_bytes=64, offset=TABLE1_AT)
+        nc.sync.dma_start(gain_rows[:], gain[:BANK].partition_broadcast(P))
+        gain_cols = shared.tile([P, 8], F32, name="gain_cols", align_bytes=64, offset=TABLE1_AT + 2048)
+        with nc.allow_non_contiguous_dma(reason="gain: one value for each partition and row tile"):
+            for e in range(4):
+                nc.sync.dma_start(gain_cols[e:P:4, 0:PACK], gain[BANK:].rearrange("(u t e) -> e u t", t=PACK, e=4)[e])
 
         neg_h = [keep.tile([P, S], F32, name="neg_h%d" % i, tag="h_later%d" % i, align_bytes=64) for i in range(TILES)]
         tissue = [keep.tile([P, 2, 2, M], F32, name="tissue%d" % k, tag="tissue%d" % k, align_bytes=64) for k in range(PAIRS)]
@@ -154,36 +177,44 @@ def tile_list_burial_isotope_mobility_kernel(
             w2_bf.append(keep.tile([P, N, PACK], BF16, name="w2_bf%d" % b, tag="w2_bf%d" % b, align_bytes=64))
             nc.gpsimd.tensor_scalar(w2_bf[b][:], w2_raw[b][:].rearrange("p t n -> p n t"), 1.0, 0.0, ALU.mult, ALU.add)
 
-        neg_soil = shared.tile([P, TILES, M], F32, name="neg_soil", align_bytes=64, offset=WORDS_AT + 3 * 2048)
+        soil_pairs = [
+            shared.tile([P, 2, M], F32, name="neg_soil%d" % k, align_bytes=64, offset=WORDS_AT + 4096 * k) for k in range(PAIRS)
+        ]
+        neg_soil = [soil_pairs[i // 2][:, i % 2, :] for i in range(TILES)]
         sums = {}
-        for i in range(TILES):
-            nc.vector.tensor_copy(neg_soil[:, i, :], neg_h[i][:].indirect(pos_sb[2][:]))
-            b, t = divmod(i, PACK)
-            for c in range(CHUNKS):
-                if t == 0:
-                    sums[c, b] = bank(2 * c + b, [P, BANK], "sums")
-                nc.tensor.matmul(
-                    sums[c, b][:, P * t : P * (t + 1)],
-                    neg_soil[:, i, P * c : P * (c + 1)],
-                    ident[:],
-                    start=(t == 0),
-                    stop=False,
-                    is_transpose=True,
-                )
+        for i in list(range(PACK, TILES)) + list(range(PACK)):
+            nc.vector.tensor_copy(neg_soil[i], neg_h[i][:].indirect(pos_sb[2][:]))
+            if i < PACK:
+                for c in range(CHUNKS):
+                    if i == 0:
+                        sums[c] = bank(c, [P, BANK], "sums")
+                    nc.tensor.matmul(
+                        sums[c][:, P * i : P * (i + 1)],
+                        neg_soil[i][:, P * c : P * (c + 1)],
+                        ident[:],
+                        start=(i == 0),
+                        stop=False,
+                        is_transpose=True,
+                    )
 
         both = {}
         squared = {}
+        offset_of = {}
 
         def product(pair, engine, tile):
             both[pair] = tile
             engine.tensor_tensor(tile[:], tissue[pair][:, 0], tissue[pair][:, 1], ALU.mult)
 
+        def scale_soil(t, engine, rows):
+            offset_of[t] = rows
+            engine.tensor_scalar(rows, neg_soil[PACK + t], -0.25, gain_cols[:, t : t + 1], ALU.add, ALU.mult)
+
         product(0, nc.gpsimd, shared.tile([P, 2, M], F32, name="both0", align_bytes=64, offset=TABLE1_AT + 4096))
-        shifted = keep.tile([P, 2, M], F32, name="shifted", tag="shifted_both1")
+        shifted = shared.tile([P, 2, M], F32, name="shifted", align_bytes=64, offset=LATE_AT)
         nc.gpsimd.tensor_scalar(shifted[:], both[0][:], 1.0, -3.125, ALU.mult, ALU.add)
         squared[0] = keep.tile([P, 2, M], F32, name="squared0", tag="tissue0", align_bytes=64)
         nc.gpsimd.tensor_tensor(squared[0][:], shifted[:], both[0][:], ALU.mult)
-        product(1, nc.gpsimd, keep.tile([P, 2, M], F32, name="both1", tag="shifted_both1"))
+        product(1, nc.gpsimd, shared.tile([P, 2, M], F32, name="both1", align_bytes=64, offset=LATE_AT))
         product(2, nc.gpsimd, keep.tile([P, 2, M], F32, name="both2", tag="tissue1", align_bytes=64))
 
         w2_codes = keep.tile([P, PASSES, N], U32, name="w2_codes", tag="tissue2", align_bytes=64)
@@ -199,90 +230,130 @@ def tile_list_burial_isotope_mobility_kernel(
             squared[pair] = tile
             nc.vector.scalar_tensor_tensor(tile[:], both[pair][:], -3.125, both[pair][:], ALU.add, ALU.mult)
 
-        square_on_vector(1, keep.tile([P, 2, M], F32, name="squared1", tag="w2_bf0", align_bytes=64))
-        square_on_vector(2, keep.tile([P, 2, M], F32, name="squared2", tag="w2_bf1", align_bytes=64))
-        product(3, nc.vector, keep.tile([P, 2, M], F32, name="both3", tag="shifted_both1"))
+        square_on_vector(1, keep.tile([P, 2, M], F32, name="squared1", tag="w2_bf1", align_bytes=64))
+        product(3, nc.vector, shared.tile([P, 2, M], F32, name="both3", align_bytes=64, offset=LATE_AT))
         square_on_vector(3, keep.tile([P, 2, M], F32, name="squared3", tag="tissue3", align_bytes=64))
+        scaled_soil = shared.tile([P, PACK, M], F32, name="scaled_soil", align_bytes=64, offset=LATE_AT - 6144)
+        for t in (2, 3, 0, 1):
+            scale_soil(t, nc.gpsimd, scaled_soil[:, t, :])
 
         inverse = keep.tile([P, TILES, M], F32, name="inverse", tag="h_later7", align_bytes=64)
 
         def invert(half, pair):
-            cols = slice(2 * P * half, 2 * P * (half + 1))
+            cols = HALVES[half]
+            scale, bias = (1.0, 0.0) if pair == 2 else (6.5536, 16.0)
             nc.scalar.activation(
-                inverse[:, 2 * pair : 2 * pair + 2, cols], squared[pair][:, :, cols], ACT.Abs_reciprocal_sqrt, bias=16.0, scale=6.5536
+                inverse[:, 2 * pair : 2 * pair + 2, cols], squared[pair][:, :, cols], ACT.Abs_reciprocal_sqrt, bias=bias, scale=scale
             )
-            for c in (2 * half, 2 * half + 1):
-                for i in (2 * pair, 2 * pair + 1):
-                    b, t = divmod(i, PACK)
-                    nc.tensor.matmul(
-                        sums[c, b][:, P * t : P * (t + 1)],
-                        inverse[:, i, P * c : P * (c + 1)],
-                        ident[:],
-                        start=False,
-                        stop=(t == PACK - 1),
-                        is_transpose=True,
-                    )
+            if pair < 2:
+                for c in (2 * half, 2 * half + 1):
+                    for i in (2 * pair, 2 * pair + 1):
+                        nc.tensor.matmul(
+                            sums[c][:, P * i : P * (i + 1)],
+                            inverse[:, i, P * c : P * (c + 1)],
+                            ident[:],
+                            start=False,
+                            stop=(i == PACK - 1),
+                            is_transpose=True,
+                        )
 
         z_rows = {}
-        acc = {}
+        z_bf = keep.tile([P, M * PACK], BF16, name="z_bf", align_bytes=64)
+        z_codes = keep.tile([P, PASSES, M], U32, name="z_codes", align_bytes=64)
+        z_scale = keep.tile([P, PASSES, M], U8, name="z_scale", align_bytes=64)
+        term = keep.tile([P, PACK, M], F32, name="term")
 
-        def scale_by_gain(c, b):
-            z_rows[c, b] = keep.tile([P, BANK], BF16, name="z_rows%d_%d" % (c, b), align_bytes=64)
-            nc.vector.scalar_tensor_tensor(
-                z_rows[c, b][:], sums[c, b][:], -0.25, gain_rows[:, BANK * b : BANK * (b + 1)], ALU.add, ALU.mult
-            )
+        def scale_by_gain(c):
+            z_rows[c] = shared.tile([P, BANK], BF16, name="z_rows%d" % c, align_bytes=64, offset=LATE_AT + 2048 + 1024 * c)
+            nc.vector.scalar_tensor_tensor(z_rows[c][:], sums[c][:], -0.25, gain_rows[:], ALU.add, ALU.mult)
 
         z_words = {}
 
-        def turn_back(c, b, copy_words):
-            turned = bank(2 * c + b, [P, 2, P], "turned")
-            words = z_rows[c, b][:].bitcast(F32)
+        def turn_back(c, copy):
+            turned = bank(c, [P, 2, P], "turned")
+            words = z_rows[c][:].bitcast(F32)
             for u in range(2):
                 nc.tensor.transpose(turned[:, u, :], words[:, u : 2 * P : 2], ident[:])
-            z_words[c, b] = keep.tile([P, P, 2], F32, name="z_words%d_%d" % (c, b), align_bytes=64)
-            copy_words(z_words[c, b][:], turned[:].rearrange("p u m -> p m u"))
+            if c % 2 == 0:
+                z_words[c // 2] = keep.tile([P, 2, P, 2], F32, name="z_words%d" % (c // 2), align_bytes=64)
+            copy(z_words[c // 2][:, c % 2], turned[:].rearrange("p u m -> p m u"))
 
-        def multiply(c, b):
-            z_codes = keep.tile([P, P], U32, name="z_codes%d_%d" % (c, b), align_bytes=64)
-            z_scale = keep.tile([P, P], U8, name="z_scale%d_%d" % (c, b), align_bytes=64)
+        def quantize_first(half):
             nc.vector.quantize_mx(
-                out=z_codes[:].bitcast(FP8X4),
-                scales=z_scale[:],
-                in_=z_words[c, b][:].rearrange("p m u -> p (m u)").bitcast(BF16),
+                out=z_codes[:, 0, HALVES[half]].bitcast(FP8X4),
+                scales=z_scale[:, 0, HALVES[half]],
+                in_=z_words[half][:].rearrange("p c m u -> p (c m u)").bitcast(BF16),
             )
+
+        def combine(t, cols):
+            nc.vector.scalar_tensor_tensor(
+                term[:, t, cols], inverse[:, PACK + t, cols], gain_cols[:, t : t + 1], offset_of[t][:, cols], ALU.mult, ALU.add
+            )
+
+        def interleave(cols, copy):
+            copy(
+                z_bf[:, PACK * cols.start : PACK * cols.stop].rearrange("p (g i t) -> p g t i", i=4, t=PACK),
+                term[:, :, cols].rearrange("p t (g i) -> p g t i", i=4),
+            )
+
+        def quantize_second(cols):
+            nc.vector.quantize_mx(
+                out=z_codes[:, 1, cols].bitcast(FP8X4),
+                scales=z_scale[:, 1, cols],
+                in_=z_bf[:, PACK * cols.start : PACK * cols.stop],
+            )
+
+        results = [(4, PIECES[0], (0, 1)), (5, PIECES[0], (2, 3)), (6, PIECES[1], (0, 1, 2, 3)), (7, PIECES[2], (0, 1)), (0, PIECES[2], (2, 3))]
+        acc = {}
+
+        def multiply(k, b):
+            number, cols, rows = results[k]
             if b == 0:
-                acc[c] = bank(2 * c, [P, N // P, P], "acc")
-            for j in range(N // P):
+                acc[k] = bank(number, [P, len(rows), cols.stop - cols.start], "acc")
+            for place, j in enumerate(rows):
                 nc.tensor.matmul_mx(
-                    out=acc[c][:, j, :],
+                    out=acc[k][:, place, :],
                     lhsT=w2_codes[:, b, P * j : P * (j + 1)].bitcast(FP8X4),
                     lhsT_scale=w2_scale[:, b, P * j : P * (j + 1)],
-                    rhs=z_codes[:].bitcast(FP8X4),
-                    rhs_scale=z_scale[:],
-                    start=(b == 0 and j == 0),
-                    stop=(b == PASSES - 1 and j == N // P - 1),
+                    rhs=z_codes[:, b, cols].bitcast(FP8X4),
+                    rhs_scale=z_scale[:, b, cols],
+                    start=(b == 0 and place == 0),
+                    stop=(b == PASSES - 1 and place == len(rows) - 1),
                 )
 
-        def store(c, copy_out):
-            result = keep.tile([P, N // P, P], F32, name="result%d" % c)
-            copy_out(result[:], acc[c][:])
-            nc.sync.dma_start(out[:, P * c : P * (c + 1)].rearrange("(j p) m -> p j m", p=P), result[:])
+        def store(k, copy_out):
+            number, cols, rows = results[k]
+            result = keep.tile([P, len(rows), cols.stop - cols.start], F32, name="result%d" % k)
+            copy_out(result[:], acc[k][:])
+            nc.sync.dma_start(
+                out[P * rows[0] : P * (rows[-1] + 1), cols].rearrange("(j p) m -> p j m", p=P), result[:]
+            )
 
-        for b in range(PASSES):
-            for half in range(2):
-                for pair in (2 * b, 2 * b + 1):
-                    invert(half, pair)
-        for c in range(CHUNKS):
-            scale_by_gain(c, 0)
-        for c in range(CHUNKS):
-            turn_back(c, 0, nc.vector.tensor_copy if c < 2 else nc.scalar.copy)
         for half in range(2):
-            for c in (2 * half, 2 * half + 1):
-                multiply(c, 0)
-            for c in (2 * half, 2 * half + 1):
-                scale_by_gain(c, 1)
-                turn_back(c, 1, nc.scalar.copy)
+            for pair in (0, 1):
+                invert(half, pair)
+        squared[2] = keep.tile([P, 2, M], F32, name="squared2", tag="w2_bf1", align_bytes=64)
+        nc.scalar.activation(squared[2][:], both[2][:], ACT.Square, bias=4.0, scale=-2.56)
+        for half in range(2):
+            for pair in (3, 2):
+                invert(half, pair)
         for c in range(CHUNKS):
-            multiply(c, 1)
+            scale_by_gain(c)
         for c in range(CHUNKS):
-            store(c, nc.vector.tensor_copy if c == 2 else nc.scalar.copy)
+            turn_back(c, nc.scalar.copy)
+        for t in (2, 3, 0, 1):
+            combine(t, HALVES[0])
+        interleave(PIECES[0], nc.scalar.copy)
+        quantize_first(0)
+        for t in (2, 3, 0, 1):
+            combine(t, HALVES[1])
+        quantize_first(1)
+        for k in range(5):
+            multiply(k, 0)
+        interleave(PIECES[1], nc.vector.tensor_copy)
+        interleave(PIECES[2], nc.vector.tensor_copy)
+        for cols in PIECES:
+            quantize_second(cols)
+        for k in range(5):
+            multiply(k, 1)
+            store(k, nc.vector.tensor_copy if k == 3 else nc.scalar.copy)

@@ -33,7 +33,8 @@ PIECES = (slice(0, 256), slice(256, 384), slice(384, 512))
 TABLE1_AT = 4096
 TABLE0_AT = 16384
 WORDS_AT = 27648
-LATE_AT = 51200
+LAST_AT = 45056
+H7_AT = 65536
 
 
 def tile_list_burial_isotope_mobility_kernel(
@@ -144,8 +145,10 @@ def tile_list_burial_isotope_mobility_kernel(
             for e in range(4):
                 nc.sync.dma_start(gain_cols[e:P:4, 0:PACK], gain[BANK:].rearrange("(u t e) -> e u t", t=PACK, e=4)[e])
 
-        neg_h = [keep.tile([P, S], F32, name="neg_h%d" % i, tag="h_later%d" % i, align_bytes=64) for i in range(TILES)]
-        tissue = [keep.tile([P, 2, 2, M], F32, name="tissue%d" % k, tag="tissue%d" % k, align_bytes=64) for k in range(PAIRS)]
+        neg_h = [keep.tile([P, S], F32, name="neg_h%d" % i, align_bytes=64) for i in range(TILES - 1)]
+        neg_h.append(shared.tile([P, S], F32, name="neg_h7", align_bytes=64, offset=H7_AT))
+        tissue = [keep.tile([P, 2, 2, M], F32, name="tissue%d" % k, tag="tissue%d" % k, align_bytes=64) for k in range(PAIRS - 1)]
+        tissue.append(shared.tile([P, 2, 2, M], F32, name="tissue3", align_bytes=64, offset=LAST_AT))
 
         for i in range(TILES):
             banks = []
@@ -198,24 +201,30 @@ def tile_list_burial_isotope_mobility_kernel(
                     )
 
         both = {}
-        squared = {}
         offset_of = {}
 
         def product(pair, engine, tile):
             both[pair] = tile
-            engine.tensor_tensor(tile[:], tissue[pair][:, 0], tissue[pair][:, 1], ALU.mult)
+            engine.tensor_tensor(tile, tissue[pair][:, 0], tissue[pair][:, 1], ALU.mult)
 
         def scale_soil(t, engine, rows):
             offset_of[t] = rows
             engine.tensor_scalar(rows, neg_soil[PACK + t], -0.25, gain_cols[:, t : t + 1], ALU.add, ALU.mult)
 
-        product(0, nc.gpsimd, shared.tile([P, 2, M], F32, name="both0", align_bytes=64, offset=TABLE1_AT + 4096))
-        shifted = shared.tile([P, 2, M], F32, name="shifted", align_bytes=64, offset=LATE_AT)
-        nc.gpsimd.tensor_scalar(shifted[:], both[0][:], 1.0, -3.125, ALU.mult, ALU.add)
-        squared[0] = keep.tile([P, 2, M], F32, name="squared0", tag="tissue0", align_bytes=64)
-        nc.gpsimd.tensor_tensor(squared[0][:], shifted[:], both[0][:], ALU.mult)
-        product(1, nc.gpsimd, shared.tile([P, 2, M], F32, name="both1", align_bytes=64, offset=LATE_AT))
-        product(2, nc.gpsimd, keep.tile([P, 2, M], F32, name="both2", tag="tissue1", align_bytes=64))
+        both0 = shared.tile([P, 2, M], F32, name="both0", align_bytes=64, offset=TABLE1_AT + 4096)
+        product(0, nc.gpsimd, both0[:])
+        shifted = keep.tile([P, 2, M], F32, name="shifted", tag="shifted_both1")
+        nc.gpsimd.tensor_scalar(shifted[:], both0[:], 1.0, -3.125, ALU.mult, ALU.add)
+        squared = keep.tile([P, PACK, M], F32, name="squared", tag="tissue0", align_bytes=64)
+        nc.gpsimd.tensor_tensor(squared[:, 0:2, :], shifted[:], both0[:], ALU.mult)
+        both1 = keep.tile([P, 2, M], F32, name="both1", tag="shifted_both1")
+        product(1, nc.gpsimd, both1[:])
+        scaled_soil = keep.tile([P, PACK, M], F32, name="scaled_soil", tag="tissue1", align_bytes=64)
+        for t in range(2):
+            scale_soil(t, nc.gpsimd, scaled_soil[:, t, :])
+        both2 = shared.tile([P, 2, M], F32, name="both2", align_bytes=64, offset=WORDS_AT + 2 * 4096)
+        product(2, nc.gpsimd, both2[:])
+        nc.vector.scalar_tensor_tensor(squared[:, 2:4, :], both1[:], -3.125, both1[:], ALU.add, ALU.mult)
 
         w2_codes = keep.tile([P, PASSES, N], U32, name="w2_codes", tag="tissue2", align_bytes=64)
         w2_scale = keep.tile([P, PASSES, N], U8, name="w2_scale", align_bytes=64)
@@ -226,45 +235,40 @@ def tile_list_burial_isotope_mobility_kernel(
                 in_=w2_bf[b][:].rearrange("p n t -> p (n t)"),
             )
 
-        def square_on_vector(pair, tile):
-            squared[pair] = tile
-            nc.vector.scalar_tensor_tensor(tile[:], both[pair][:], -3.125, both[pair][:], ALU.add, ALU.mult)
+        both3 = keep.tile([P, 2, M], F32, name="both3", tag="w2_bf1", align_bytes=64)
+        product(3, nc.vector, both3[:])
 
-        square_on_vector(1, keep.tile([P, 2, M], F32, name="squared1", tag="w2_bf1", align_bytes=64))
-        product(3, nc.vector, shared.tile([P, 2, M], F32, name="both3", align_bytes=64, offset=LATE_AT))
-        square_on_vector(3, keep.tile([P, 2, M], F32, name="squared3", tag="tissue3", align_bytes=64))
-        scaled_soil = shared.tile([P, PACK, M], F32, name="scaled_soil", align_bytes=64, offset=LATE_AT - 6144)
-        for t in (2, 3, 0, 1):
-            scale_soil(t, nc.gpsimd, scaled_soil[:, t, :])
+        inverse = shared.tile([P, PACK, M], F32, name="inverse", align_bytes=64, offset=H7_AT - 6144)
+        root_first = shared.tile([P, 2, 2 * P], F32, name="root_first", align_bytes=64, offset=H7_AT + 2048)
+        root_last = keep.tile([P, PACK, 2 * P], F32, name="root_last", tag="tissue0", align_bytes=64)
+        root = {
+            (0, 2): root_first[:],
+            (0, 3): scaled_soil[:, 2:4, : 2 * P],
+            (1, 2): root_last[:, 0:2, :],
+            (1, 3): root_last[:, 2:4, :],
+        }
 
-        inverse = keep.tile([P, TILES, M], F32, name="inverse", tag="h_later7", align_bytes=64)
-
-        def invert(half, pair):
-            cols = HALVES[half]
-            scale, bias = (1.0, 0.0) if pair == 2 else (6.5536, 16.0)
-            nc.scalar.activation(
-                inverse[:, 2 * pair : 2 * pair + 2, cols], squared[pair][:, :, cols], ACT.Abs_reciprocal_sqrt, bias=bias, scale=scale
-            )
-            if pair < 2:
-                for c in (2 * half, 2 * half + 1):
-                    for i in (2 * pair, 2 * pair + 1):
-                        nc.tensor.matmul(
-                            sums[c][:, P * i : P * (i + 1)],
-                            inverse[:, i, P * c : P * (c + 1)],
-                            ident[:],
-                            start=False,
-                            stop=(i == PACK - 1),
-                            is_transpose=True,
-                        )
+        def invert(c):
+            cols = slice(P * c, P * (c + 1))
+            nc.scalar.activation(inverse[:, :, cols], squared[:, :, cols], ACT.Abs_reciprocal_sqrt, bias=16.0, scale=6.5536)
+            for i in range(PACK):
+                nc.tensor.matmul(
+                    sums[c][:, P * i : P * (i + 1)],
+                    inverse[:, i, cols],
+                    ident[:],
+                    start=False,
+                    stop=(i == PACK - 1),
+                    is_transpose=True,
+                )
 
         z_rows = {}
         z_bf = keep.tile([P, M * PACK], BF16, name="z_bf", align_bytes=64)
         z_codes = keep.tile([P, PASSES, M], U32, name="z_codes", align_bytes=64)
         z_scale = keep.tile([P, PASSES, M], U8, name="z_scale", align_bytes=64)
-        term = keep.tile([P, PACK, M], F32, name="term")
+        term = shared.tile([P, PACK, M], F32, name="term", align_bytes=64, offset=LAST_AT + 64 + 4096)
 
         def scale_by_gain(c):
-            z_rows[c] = shared.tile([P, BANK], BF16, name="z_rows%d" % c, align_bytes=64, offset=LATE_AT + 2048 + 1024 * c)
+            z_rows[c] = shared.tile([P, BANK], BF16, name="z_rows%d" % c, align_bytes=64, offset=LAST_AT + 64 + 1024 * c)
             nc.vector.scalar_tensor_tensor(z_rows[c][:], sums[c][:], -0.25, gain_rows[:], ALU.add, ALU.mult)
 
         z_words = {}
@@ -275,7 +279,9 @@ def tile_list_burial_isotope_mobility_kernel(
             for u in range(2):
                 nc.tensor.transpose(turned[:, u, :], words[:, u : 2 * P : 2], ident[:])
             if c % 2 == 0:
-                z_words[c // 2] = keep.tile([P, 2, P, 2], F32, name="z_words%d" % (c // 2), align_bytes=64)
+                z_words[c // 2] = shared.tile(
+                    [P, 2, P, 2], F32, name="z_words%d" % (c // 2), align_bytes=64, offset=WORDS_AT + 2 * 4096 + 2048 * (c // 2)
+                )
             copy(z_words[c // 2][:, c % 2], turned[:].rearrange("p u m -> p m u"))
 
         def quantize_first(half):
@@ -285,15 +291,16 @@ def tile_list_burial_isotope_mobility_kernel(
                 in_=z_words[half][:].rearrange("p c m u -> p (c m u)").bitcast(BF16),
             )
 
-        def combine(t, cols):
-            nc.vector.scalar_tensor_tensor(
-                term[:, t, cols], inverse[:, PACK + t, cols], gain_cols[:, t : t + 1], offset_of[t][:, cols], ALU.mult, ALU.add
-            )
+        def square_root(t, half):
+            rows = root[half, 2 + t // 2][:, t % 2, :]
+            nc.vector.scalar_tensor_tensor(term[:, t, HALVES[half]], rows, gain_cols[:, t : t + 1], rows, ALU.mult, ALU.mult)
 
-        def interleave(cols, copy):
-            copy(
+        def add_and_weave(cols):
+            nc.vector.tensor_tensor(
                 z_bf[:, PACK * cols.start : PACK * cols.stop].rearrange("p (g i t) -> p g t i", i=4, t=PACK),
                 term[:, :, cols].rearrange("p t (g i) -> p g t i", i=4),
+                scaled_soil[:, :, cols].rearrange("p t (g i) -> p g t i", i=4),
+                ALU.add,
             )
 
         def quantize_second(cols):
@@ -303,7 +310,7 @@ def tile_list_burial_isotope_mobility_kernel(
                 in_=z_bf[:, PACK * cols.start : PACK * cols.stop],
             )
 
-        results = [(4, PIECES[0], (0, 1)), (5, PIECES[0], (2, 3)), (6, PIECES[1], (0, 1, 2, 3)), (7, PIECES[2], (0, 1)), (0, PIECES[2], (2, 3))]
+        results = [(4, PIECES[0], (0, 1)), (5, PIECES[0], (2, 3)), (6, PIECES[1], (0, 1)), (1, PIECES[1], (2, 3)), (7, PIECES[2], (0, 1)), (0, PIECES[2], (2, 3))]
         acc = {}
 
         def multiply(k, b):
@@ -329,31 +336,41 @@ def tile_list_burial_isotope_mobility_kernel(
                 out[P * rows[0] : P * (rows[-1] + 1), cols].rearrange("(j p) m -> p j m", p=P), result[:]
             )
 
-        for half in range(2):
-            for pair in (0, 1):
-                invert(half, pair)
-        squared[2] = keep.tile([P, 2, M], F32, name="squared2", tag="w2_bf1", align_bytes=64)
-        nc.scalar.activation(squared[2][:], both[2][:], ACT.Square, bias=4.0, scale=-2.56)
-        for half in range(2):
-            for pair in (3, 2):
-                invert(half, pair)
+        def roots(half):
+            for pair in (2, 3):
+                nc.scalar.activation(
+                    root[half, pair],
+                    both[pair][:, :, HALVES[half]],
+                    ACT.Abs_reciprocal_sqrt,
+                    bias=4.0,
+                    scale=-2.56,
+                )
+
+        invert(0)
+        roots(0)
+        for c in range(1, CHUNKS):
+            invert(c)
+        roots(1)
+        for t in range(PACK):
+            square_root(t, 0)
+        for t in range(2, PACK):
+            scale_soil(t, nc.gpsimd, scaled_soil[:, t, :])
         for c in range(CHUNKS):
             scale_by_gain(c)
         for c in range(CHUNKS):
             turn_back(c, nc.scalar.copy)
-        for t in (2, 3, 0, 1):
-            combine(t, HALVES[0])
-        interleave(PIECES[0], nc.scalar.copy)
+        add_and_weave(PIECES[0])
         quantize_first(0)
-        for t in (2, 3, 0, 1):
-            combine(t, HALVES[1])
+        square_root(0, 1)
+        quantize_second(PIECES[0])
+        for t in range(1, PACK):
+            square_root(t, 1)
         quantize_first(1)
-        for k in range(5):
+        add_and_weave(PIECES[1])
+        add_and_weave(PIECES[2])
+        quantize_second(PIECES[1])
+        quantize_second(PIECES[2])
+        for k in range(6):
             multiply(k, 0)
-        interleave(PIECES[1], nc.vector.tensor_copy)
-        interleave(PIECES[2], nc.vector.tensor_copy)
-        for cols in PIECES:
-            quantize_second(cols)
-        for k in range(5):
             multiply(k, 1)
-            store(k, nc.vector.tensor_copy if k == 3 else nc.scalar.copy)
+            store(k, nc.vector.tensor_copy if k in (3, 5) else nc.scalar.copy)

@@ -33,8 +33,8 @@ PIECES = (slice(0, 256), slice(256, 384), slice(384, 512))
 TABLE1_AT = 4096
 TABLE0_AT = 16384
 WORDS_AT = 27648
-LAST_AT = 45056
-H7_AT = 65536
+LAST_AT = 49152
+H7_AT = 69632
 
 
 def tile_list_burial_isotope_mobility_kernel(
@@ -219,12 +219,15 @@ def tile_list_burial_isotope_mobility_kernel(
         nc.gpsimd.tensor_tensor(squared[:, 0:2, :], shifted[:], both0[:], ALU.mult)
         both1 = keep.tile([P, 2, M], F32, name="both1", tag="shifted_both1")
         product(1, nc.gpsimd, both1[:])
-        scaled_soil = keep.tile([P, PACK, M], F32, name="scaled_soil", tag="tissue1", align_bytes=64)
+        scaled_soil = keep.tile([P, 2, M], F32, name="scaled_soil", tag="tissue1", align_bytes=64)
         for t in range(2):
             scale_soil(t, nc.gpsimd, scaled_soil[:, t, :])
         both2 = shared.tile([P, 2, M], F32, name="both2", align_bytes=64, offset=WORDS_AT + 2 * 4096)
         product(2, nc.gpsimd, both2[:])
         nc.vector.scalar_tensor_tensor(squared[:, 2:4, :], both1[:], -3.125, both1[:], ALU.add, ALU.mult)
+
+        squared2 = keep.tile([P, 2, M], F32, name="squared2", tag="shifted_both1")
+        nc.vector.scalar_tensor_tensor(squared2[:], both2[:], -3.125, both2[:], ALU.add, ALU.mult)
 
         w2_codes = keep.tile([P, PASSES, N], U32, name="w2_codes", tag="tissue2", align_bytes=64)
         w2_scale = keep.tile([P, PASSES, N], U8, name="w2_scale", align_bytes=64)
@@ -239,14 +242,7 @@ def tile_list_burial_isotope_mobility_kernel(
         product(3, nc.vector, both3[:])
 
         inverse = shared.tile([P, PACK, M], F32, name="inverse", align_bytes=64, offset=H7_AT - 6144)
-        root_first = shared.tile([P, 2, 2 * P], F32, name="root_first", align_bytes=64, offset=H7_AT + 2048)
-        root_last = keep.tile([P, PACK, 2 * P], F32, name="root_last", tag="tissue0", align_bytes=64)
-        root = {
-            (0, 2): root_first[:],
-            (0, 3): scaled_soil[:, 2:4, : 2 * P],
-            (1, 2): root_last[:, 0:2, :],
-            (1, 3): root_last[:, 2:4, :],
-        }
+        second = keep.tile([P, PACK, M], F32, name="second", tag="tissue0", align_bytes=64)
 
         def invert(c):
             cols = slice(P * c, P * (c + 1))
@@ -279,9 +275,7 @@ def tile_list_burial_isotope_mobility_kernel(
             for u in range(2):
                 nc.tensor.transpose(turned[:, u, :], words[:, u : 2 * P : 2], ident[:])
             if c % 2 == 0:
-                z_words[c // 2] = shared.tile(
-                    [P, 2, P, 2], F32, name="z_words%d" % (c // 2), align_bytes=64, offset=WORDS_AT + 2 * 4096 + 2048 * (c // 2)
-                )
+                z_words[c // 2] = keep.tile([P, 2, P, 2], F32, name="z_words%d" % (c // 2), align_bytes=64)
             copy(z_words[c // 2][:, c % 2], turned[:].rearrange("p u m -> p m u"))
 
         def quantize_first(half):
@@ -291,16 +285,15 @@ def tile_list_burial_isotope_mobility_kernel(
                 in_=z_words[half][:].rearrange("p c m u -> p (c m u)").bitcast(BF16),
             )
 
-        def square_root(t, half):
-            rows = root[half, 2 + t // 2][:, t % 2, :]
-            nc.vector.scalar_tensor_tensor(term[:, t, HALVES[half]], rows, gain_cols[:, t : t + 1], rows, ALU.mult, ALU.mult)
+        def combine(t, cols):
+            nc.vector.scalar_tensor_tensor(
+                term[:, t, cols], second[:, t, cols], gain_cols[:, t : t + 1], offset_of[t][:, cols], ALU.mult, ALU.add
+            )
 
-        def add_and_weave(cols):
-            nc.vector.tensor_tensor(
+        def weave(cols, copy):
+            copy(
                 z_bf[:, PACK * cols.start : PACK * cols.stop].rearrange("p (g i t) -> p g t i", i=4, t=PACK),
                 term[:, :, cols].rearrange("p t (g i) -> p g t i", i=4),
-                scaled_soil[:, :, cols].rearrange("p t (g i) -> p g t i", i=4),
-                ALU.add,
             )
 
         def quantize_second(cols):
@@ -336,38 +329,35 @@ def tile_list_burial_isotope_mobility_kernel(
                 out[P * rows[0] : P * (rows[-1] + 1), cols].rearrange("(j p) m -> p j m", p=P), result[:]
             )
 
-        def roots(half):
-            for pair in (2, 3):
-                nc.scalar.activation(
-                    root[half, pair],
-                    both[pair][:, :, HALVES[half]],
-                    ACT.Abs_reciprocal_sqrt,
-                    bias=4.0,
-                    scale=-2.56,
-                )
+        def invert_second(cols):
+            nc.scalar.activation(second[:, 2:4, cols], both[3][:, :, cols], ACT.Abs_reciprocal_sqrt, bias=4.0, scale=-2.56)
+            nc.scalar.activation(second[:, 0:2, cols], squared2[:, :, cols], ACT.Abs_reciprocal_sqrt, bias=16.0, scale=6.5536)
+            nc.scalar.activation(second[:, 2:4, cols], second[:, 2:4, cols], ACT.Square)
 
-        invert(0)
-        roots(0)
-        for c in range(1, CHUNKS):
+        for c in range(CHUNKS):
             invert(c)
-        roots(1)
-        for t in range(PACK):
-            square_root(t, 0)
+        invert_second(HALVES[0])
+        soil_late = shared.tile([P, 2, M], F32, name="soil_late", align_bytes=64, offset=LAST_AT + 64 - 4096)
         for t in range(2, PACK):
-            scale_soil(t, nc.gpsimd, scaled_soil[:, t, :])
+            scale_soil(t, nc.gpsimd, soil_late[:, t - 2, :])
         for c in range(CHUNKS):
             scale_by_gain(c)
-        for c in range(CHUNKS):
+        for c in range(2):
             turn_back(c, nc.scalar.copy)
-        add_and_weave(PIECES[0])
+        invert_second(HALVES[1])
+        for c in range(2, CHUNKS):
+            turn_back(c, nc.scalar.copy)
+        for t in range(PACK):
+            combine(t, HALVES[0])
         quantize_first(0)
-        square_root(0, 1)
+        weave(PIECES[0], nc.vector.tensor_copy)
+        combine(0, HALVES[1])
         quantize_second(PIECES[0])
         for t in range(1, PACK):
-            square_root(t, 1)
+            combine(t, HALVES[1])
         quantize_first(1)
-        add_and_weave(PIECES[1])
-        add_and_weave(PIECES[2])
+        weave(PIECES[1], nc.vector.tensor_copy)
+        weave(PIECES[2], nc.vector.tensor_copy)
         quantize_second(PIECES[1])
         quantize_second(PIECES[2])
         for k in range(6):

@@ -211,22 +211,17 @@ def tile_list_burial_isotope_mobility_kernel(
             offset_of[t] = rows
             engine.tensor_scalar(rows, neg_soil[PACK + t], -0.25, gain_cols[:, t : t + 1], ALU.add, ALU.mult)
 
-        both0 = shared.tile([P, 2, M], F32, name="both0", align_bytes=64, offset=TABLE1_AT + 4096)
-        product(0, nc.gpsimd, both0[:])
-        shifted = keep.tile([P, 2, M], F32, name="shifted", tag="shifted_both1")
-        nc.gpsimd.tensor_scalar(shifted[:], both0[:], 1.0, -3.125, ALU.mult, ALU.add)
+        both_first = shared.tile([P, PACK, M], F32, name="both_first", align_bytes=64, offset=TABLE1_AT + 4096)
+        product(0, nc.gpsimd, both_first[:, 0:2, :])
+        shifted = keep.tile([P, M], F32, name="shifted")
+        nc.gpsimd.tensor_scalar(shifted[:], both_first[:, 0, :], 1.0, -3.125, ALU.mult, ALU.add)
         squared = keep.tile([P, PACK, M], F32, name="squared", tag="tissue0", align_bytes=64)
-        nc.gpsimd.tensor_tensor(squared[:, 0:2, :], shifted[:], both0[:], ALU.mult)
-        both1 = keep.tile([P, 2, M], F32, name="both1", tag="shifted_both1")
-        product(1, nc.gpsimd, both1[:])
-        scaled_soil = keep.tile([P, 2, M], F32, name="scaled_soil", tag="tissue1", align_bytes=64)
-        for t in range(2):
-            scale_soil(t, nc.gpsimd, scaled_soil[:, t, :])
-        both2 = shared.tile([P, 2, M], F32, name="both2", align_bytes=64, offset=WORDS_AT + 2 * 4096)
+        nc.gpsimd.tensor_tensor(squared[:, 0, :], shifted[:], both_first[:, 0, :], ALU.mult)
+        product(1, nc.gpsimd, both_first[:, 2:4, :])
+        both2 = keep.tile([P, 2, M], F32, name="both2", tag="tissue1", align_bytes=64)
         product(2, nc.gpsimd, both2[:])
-        nc.vector.scalar_tensor_tensor(squared[:, 2:4, :], both1[:], -3.125, both1[:], ALU.add, ALU.mult)
-
-        squared2 = keep.tile([P, 2, M], F32, name="squared2", tag="shifted_both1")
+        nc.vector.scalar_tensor_tensor(squared[:, 1:, :], both_first[:, 1:, :], -3.125, both_first[:, 1:, :], ALU.add, ALU.mult)
+        squared2 = shared.tile([P, 2, M], F32, name="squared2", align_bytes=64, offset=TABLE1_AT + 4096)
         nc.vector.scalar_tensor_tensor(squared2[:], both2[:], -3.125, both2[:], ALU.add, ALU.mult)
 
         w2_codes = keep.tile([P, PASSES, N], U32, name="w2_codes", tag="tissue2", align_bytes=64)
@@ -238,6 +233,9 @@ def tile_list_burial_isotope_mobility_kernel(
                 in_=w2_bf[b][:].rearrange("p n t -> p (n t)"),
             )
 
+        soil_early = keep.tile([P, 2, M], F32, name="soil_early", tag="w2_bf0", align_bytes=64)
+        for t in range(2):
+            scale_soil(t, nc.vector, soil_early[:, t, :])
         both3 = keep.tile([P, 2, M], F32, name="both3", tag="w2_bf1", align_bytes=64)
         product(3, nc.vector, both3[:])
 

@@ -212,17 +212,15 @@ def tile_list_burial_isotope_mobility_kernel(
             engine.tensor_scalar(rows, neg_soil[PACK + t], -0.25, gain_cols[:, t : t + 1], ALU.add, ALU.mult)
 
         both_first = shared.tile([P, PACK, M], F32, name="both_first", align_bytes=64, offset=TABLE1_AT + 4096)
-        product(0, nc.gpsimd, both_first[:, 0:2, :])
-        shifted = keep.tile([P, M], F32, name="shifted")
-        nc.gpsimd.tensor_scalar(shifted[:], both_first[:, 0, :], 1.0, -3.125, ALU.mult, ALU.add)
-        squared = keep.tile([P, PACK, M], F32, name="squared", tag="tissue0", align_bytes=64)
-        nc.gpsimd.tensor_tensor(squared[:, 0, :], shifted[:], both_first[:, 0, :], ALU.mult)
-        product(1, nc.gpsimd, both_first[:, 2:4, :])
+        shifted = keep.tile([P, PACK, M], F32, name="shifted")
+        for pair in range(2):
+            rows = slice(2 * pair, 2 * pair + 2)
+            product(pair, nc.gpsimd, both_first[:, rows, :])
+            nc.gpsimd.tensor_scalar(shifted[:, rows, :], both_first[:, rows, :], 1.0, -3.125, ALU.mult, ALU.add)
         both2 = keep.tile([P, 2, M], F32, name="both2", tag="tissue1", align_bytes=64)
         product(2, nc.gpsimd, both2[:])
-        nc.vector.scalar_tensor_tensor(squared[:, 1:, :], both_first[:, 1:, :], -3.125, both_first[:, 1:, :], ALU.add, ALU.mult)
-        squared2 = shared.tile([P, 2, M], F32, name="squared2", align_bytes=64, offset=TABLE1_AT + 4096)
-        nc.vector.scalar_tensor_tensor(squared2[:], both2[:], -3.125, both2[:], ALU.add, ALU.mult)
+        squared = keep.tile([P, PACK, M], F32, name="squared", tag="tissue0", align_bytes=64)
+        nc.vector.tensor_tensor(squared[:], shifted[:], both_first[:], ALU.mult)
 
         w2_codes = keep.tile([P, PASSES, N], U32, name="w2_codes", tag="tissue2", align_bytes=64)
         w2_scale = keep.tile([P, PASSES, N], U8, name="w2_scale", align_bytes=64)
@@ -328,9 +326,10 @@ def tile_list_burial_isotope_mobility_kernel(
             )
 
         def invert_second(cols):
-            nc.scalar.activation(second[:, 2:4, cols], both[3][:, :, cols], ACT.Abs_reciprocal_sqrt, bias=4.0, scale=-2.56)
-            nc.scalar.activation(second[:, 0:2, cols], squared2[:, :, cols], ACT.Abs_reciprocal_sqrt, bias=16.0, scale=6.5536)
-            nc.scalar.activation(second[:, 2:4, cols], second[:, 2:4, cols], ACT.Square)
+            for pair in (2, 3):
+                rows = second[:, 2 * pair - 4 : 2 * pair - 2, cols]
+                nc.scalar.activation(rows, both[pair][:, :, cols], ACT.Abs_reciprocal_sqrt, bias=4.0, scale=-2.56)
+                nc.scalar.activation(rows, rows, ACT.Square)
 
         for c in range(CHUNKS):
             invert(c)
@@ -353,8 +352,8 @@ def tile_list_burial_isotope_mobility_kernel(
         quantize_second(PIECES[0])
         for t in range(1, PACK):
             combine(t, HALVES[1])
-        quantize_first(1)
         weave(PIECES[1], nc.vector.tensor_copy)
+        quantize_first(1)
         weave(PIECES[2], nc.vector.tensor_copy)
         quantize_second(PIECES[1])
         quantize_second(PIECES[2])

@@ -33,8 +33,8 @@ PIECES = (slice(0, 256), slice(256, 384), slice(384, 512))
 TABLE1_AT = 4096
 TABLE0_AT = 16384
 WORDS_AT = 27648
-LAST_AT = 49152
-H7_AT = 69632
+LAST_AT = 53248
+H7_AT = 73728
 
 
 def tile_list_burial_isotope_mobility_kernel(
@@ -84,13 +84,13 @@ def tile_list_burial_isotope_mobility_kernel(
         ident = keep.tile([P, P], F32, name="ident", align_bytes=64)
         make_identity(nc, ident[:])
 
+        picked_scale_rows = keep.tile([P, S], U8, name="picked_scale_rows", align_bytes=64)
+        nc.vector.tensor_copy(picked_scale_rows[:], tab_scale_rows[:].indirect(offs_sb[:]))
         nc.vector.tensor_copy(planes[0][0:32, S : S + BANK].bitcast(I32), w4_scale_rows[:, :BANK].bitcast(I32))
         nc.vector.tensor_copy(
             planes[0][0:32, S + BANK :].bitcast(I32).rearrange("p (t u) -> p t u", t=PACK),
             w4_scale_rows[:, BANK:].bitcast(I32).rearrange("p (u t) -> p t u", t=PACK),
         )
-        picked_scale_rows = keep.tile([P, S], U8, name="picked_scale_rows", align_bytes=64)
-        nc.vector.tensor_copy(picked_scale_rows[:], tab_scale_rows[:].indirect(offs_sb[:]))
         nc.vector.tensor_copy(planes[0][0:32, :S].bitcast(I32), picked_scale_rows[0:32, :].bitcast(I32))
         for a in range(PASSES):
             for q in range(4):
@@ -213,14 +213,16 @@ def tile_list_burial_isotope_mobility_kernel(
 
         both_first = shared.tile([P, PACK, M], F32, name="both_first", align_bytes=64, offset=TABLE1_AT + 4096)
         shifted = keep.tile([P, PACK, M], F32, name="shifted")
+        squared = keep.tile([P, PACK, M], F32, name="squared", tag="tissue0", align_bytes=64)
         for pair in range(2):
             rows = slice(2 * pair, 2 * pair + 2)
             product(pair, nc.gpsimd, both_first[:, rows, :])
             nc.gpsimd.tensor_scalar(shifted[:, rows, :], both_first[:, rows, :], 1.0, -3.125, ALU.mult, ALU.add)
+            if pair == 0:
+                nc.gpsimd.tensor_tensor(squared[:, 0, :], shifted[:, 0, :], both_first[:, 0, :], ALU.mult)
         both2 = keep.tile([P, 2, M], F32, name="both2", tag="tissue1", align_bytes=64)
         product(2, nc.gpsimd, both2[:])
-        squared = keep.tile([P, PACK, M], F32, name="squared", tag="tissue0", align_bytes=64)
-        nc.vector.tensor_tensor(squared[:], shifted[:], both_first[:], ALU.mult)
+        nc.vector.tensor_tensor(squared[:, 1:, :], shifted[:, 1:, :], both_first[:, 1:, :], ALU.mult)
 
         w2_codes = keep.tile([P, PASSES, N], U32, name="w2_codes", tag="tissue2", align_bytes=64)
         w2_scale = keep.tile([P, PASSES, N], U8, name="w2_scale", align_bytes=64)
@@ -231,12 +233,13 @@ def tile_list_burial_isotope_mobility_kernel(
                 in_=w2_bf[b][:].rearrange("p n t -> p (n t)"),
             )
 
-        soil_early = keep.tile([P, 2, M], F32, name="soil_early", tag="w2_bf0", align_bytes=64)
-        for t in range(2):
-            scale_soil(t, nc.vector, soil_early[:, t, :])
+        shifted2 = keep.tile([P, 2, M], F32, name="shifted2", tag="w2_bf0", align_bytes=64)
+        nc.vector.tensor_scalar(shifted2[:], both2[:], -3.125, None, ALU.add)
         both3 = keep.tile([P, 2, M], F32, name="both3", tag="w2_bf1", align_bytes=64)
         product(3, nc.vector, both3[:])
 
+        squared2 = keep.tile([P, 2, M], F32, name="squared2")
+        nc.vector.tensor_tensor(squared2[:], shifted2[:], both2[:], ALU.mult)
         inverse = shared.tile([P, PACK, M], F32, name="inverse", align_bytes=64, offset=H7_AT - 6144)
         second = keep.tile([P, PACK, M], F32, name="second", tag="tissue0", align_bytes=64)
 
@@ -328,15 +331,18 @@ def tile_list_burial_isotope_mobility_kernel(
         def invert_second(cols):
             for pair in (2, 3):
                 rows = second[:, 2 * pair - 4 : 2 * pair - 2, cols]
+                if pair == 2:
+                    nc.scalar.activation(rows, squared2[:, :, cols], ACT.Abs_reciprocal_sqrt, bias=16.0, scale=6.5536)
+                    continue
                 nc.scalar.activation(rows, both[pair][:, :, cols], ACT.Abs_reciprocal_sqrt, bias=4.0, scale=-2.56)
                 nc.scalar.activation(rows, rows, ACT.Square)
 
         for c in range(CHUNKS):
             invert(c)
         invert_second(HALVES[0])
-        soil_late = shared.tile([P, 2, M], F32, name="soil_late", align_bytes=64, offset=LAST_AT + 64 - 4096)
-        for t in range(2, PACK):
-            scale_soil(t, nc.gpsimd, soil_late[:, t - 2, :])
+        soil_late = shared.tile([P, PACK, M], F32, name="soil_late", align_bytes=64, offset=LAST_AT + 64 - 8192)
+        for t in range(PACK):
+            scale_soil(t, nc.gpsimd, soil_late[:, t, :])
         for c in range(CHUNKS):
             scale_by_gain(c)
         for c in range(2):

@@ -212,12 +212,13 @@ def tile_list_burial_isotope_mobility_kernel(
             engine.tensor_scalar(rows, neg_soil[PACK + t], -0.25, gain_cols[:, t : t + 1], ALU.add, ALU.mult)
 
         both_first = shared.tile([P, PACK, M], F32, name="both_first", align_bytes=64, offset=TABLE1_AT + 4096)
-        shifted = keep.tile([P, PACK, M], F32, name="shifted")
+        shifted = keep.tile([P, PACK, M], F32, name="shifted", tag="shifted", align_bytes=64)
         squared = keep.tile([P, PACK, M], F32, name="squared", tag="tissue0", align_bytes=64)
         for pair in range(2):
-            rows = slice(2 * pair, 2 * pair + 2)
-            product(pair, nc.gpsimd, both_first[:, rows, :])
-            nc.gpsimd.tensor_scalar(shifted[:, rows, :], both_first[:, rows, :], 1.0, -3.125, ALU.mult, ALU.add)
+            for i in (2 * pair, 2 * pair + 1):
+                nc.gpsimd.tensor_tensor(both_first[:, i, :], tissue[pair][:, 0, i % 2], tissue[pair][:, 1, i % 2], ALU.mult)
+            for i in (2 * pair, 2 * pair + 1):
+                nc.gpsimd.tensor_scalar(shifted[:, i, :], both_first[:, i, :], 1.0, -3.125, ALU.mult, ALU.add)
             if pair == 0:
                 nc.gpsimd.tensor_tensor(squared[:, 0, :], shifted[:, 0, :], both_first[:, 0, :], ALU.mult)
         both2 = keep.tile([P, 2, M], F32, name="both2", tag="tissue1", align_bytes=64)
@@ -233,13 +234,16 @@ def tile_list_burial_isotope_mobility_kernel(
                 in_=w2_bf[b][:].rearrange("p n t -> p (n t)"),
             )
 
-        shifted2 = keep.tile([P, 2, M], F32, name="shifted2", tag="w2_bf0", align_bytes=64)
-        nc.vector.tensor_scalar(shifted2[:], both2[:], -3.125, None, ALU.add)
+        shifted2 = keep.tile([P, 2, 2 * P], F32, name="shifted2", tag="w2_bf0", align_bytes=64)
+        nc.vector.tensor_scalar(shifted2[:], both2[:, :, HALVES[0]], -3.125, None, ALU.add)
+        scaled_soil = keep.tile([P, PACK, M], F32, name="scaled_soil", tag="shifted", align_bytes=64)
+        for t in range(PACK):
+            scale_soil(t, nc.vector, scaled_soil[:, t, :])
         both3 = keep.tile([P, 2, M], F32, name="both3", tag="w2_bf1", align_bytes=64)
         product(3, nc.vector, both3[:])
 
-        squared2 = keep.tile([P, 2, M], F32, name="squared2")
-        nc.vector.tensor_tensor(squared2[:], shifted2[:], both2[:], ALU.mult)
+        squared2 = keep.tile([P, 2, 2 * P], F32, name="squared2")
+        nc.vector.tensor_tensor(squared2[:], shifted2[:], both2[:, :, HALVES[0]], ALU.mult)
         inverse = shared.tile([P, PACK, M], F32, name="inverse", align_bytes=64, offset=H7_AT - 6144)
         second = keep.tile([P, PACK, M], F32, name="second", tag="tissue0", align_bytes=64)
 
@@ -331,8 +335,8 @@ def tile_list_burial_isotope_mobility_kernel(
         def invert_second(cols):
             for pair in (2, 3):
                 rows = second[:, 2 * pair - 4 : 2 * pair - 2, cols]
-                if pair == 2:
-                    nc.scalar.activation(rows, squared2[:, :, cols], ACT.Abs_reciprocal_sqrt, bias=16.0, scale=6.5536)
+                if pair == 2 and cols == HALVES[0]:
+                    nc.scalar.activation(rows, squared2[:], ACT.Abs_reciprocal_sqrt, bias=16.0, scale=6.5536)
                     continue
                 nc.scalar.activation(rows, both[pair][:, :, cols], ACT.Abs_reciprocal_sqrt, bias=4.0, scale=-2.56)
                 nc.scalar.activation(rows, rows, ACT.Square)
@@ -340,9 +344,6 @@ def tile_list_burial_isotope_mobility_kernel(
         for c in range(CHUNKS):
             invert(c)
         invert_second(HALVES[0])
-        soil_late = shared.tile([P, PACK, M], F32, name="soil_late", align_bytes=64, offset=LAST_AT + 64 - 8192)
-        for t in range(PACK):
-            scale_soil(t, nc.gpsimd, soil_late[:, t, :])
         for c in range(CHUNKS):
             scale_by_gain(c)
         for c in range(2):

@@ -212,18 +212,16 @@ def tile_list_burial_isotope_mobility_kernel(
             engine.tensor_scalar(rows, neg_soil[PACK + t], -0.25, gain_cols[:, t : t + 1], ALU.add, ALU.mult)
 
         both_first = shared.tile([P, PACK, M], F32, name="both_first", align_bytes=64, offset=TABLE1_AT + 4096)
-        shifted = keep.tile([P, PACK, M], F32, name="shifted", tag="shifted", align_bytes=64)
+        shifted = keep.tile([P, M], F32, name="shifted")
         squared = keep.tile([P, PACK, M], F32, name="squared", tag="tissue0", align_bytes=64)
-        for pair in range(2):
-            for i in (2 * pair, 2 * pair + 1):
-                nc.gpsimd.tensor_tensor(both_first[:, i, :], tissue[pair][:, 0, i % 2], tissue[pair][:, 1, i % 2], ALU.mult)
-            for i in (2 * pair, 2 * pair + 1):
-                nc.gpsimd.tensor_scalar(shifted[:, i, :], both_first[:, i, :], 1.0, -3.125, ALU.mult, ALU.add)
-            if pair == 0:
-                nc.gpsimd.tensor_tensor(squared[:, 0, :], shifted[:, 0, :], both_first[:, 0, :], ALU.mult)
+        for i in range(2):
+            nc.gpsimd.tensor_tensor(both_first[:, i, :], tissue[0][:, 0, i], tissue[0][:, 1, i], ALU.mult)
+        nc.gpsimd.tensor_scalar(shifted[:], both_first[:, 0, :], 1.0, -3.125, ALU.mult, ALU.add)
+        product(1, nc.gpsimd, both_first[:, 2:4, :])
+        nc.gpsimd.tensor_tensor(squared[:, 0, :], shifted[:], both_first[:, 0, :], ALU.mult)
         both2 = keep.tile([P, 2, M], F32, name="both2", tag="tissue1", align_bytes=64)
         product(2, nc.gpsimd, both2[:])
-        nc.vector.tensor_tensor(squared[:, 1:, :], shifted[:, 1:, :], both_first[:, 1:, :], ALU.mult)
+        nc.vector.scalar_tensor_tensor(squared[:, 1:, :], both_first[:, 1:, :], -3.125, both_first[:, 1:, :], ALU.add, ALU.mult)
 
         w2_codes = keep.tile([P, PASSES, N], U32, name="w2_codes", tag="tissue2", align_bytes=64)
         w2_scale = keep.tile([P, PASSES, N], U8, name="w2_scale", align_bytes=64)
@@ -234,16 +232,16 @@ def tile_list_burial_isotope_mobility_kernel(
                 in_=w2_bf[b][:].rearrange("p n t -> p (n t)"),
             )
 
-        shifted2 = keep.tile([P, 2, 2 * P], F32, name="shifted2", tag="w2_bf0", align_bytes=64)
-        nc.vector.tensor_scalar(shifted2[:], both2[:, :, HALVES[0]], -3.125, None, ALU.add)
-        scaled_soil = keep.tile([P, PACK, M], F32, name="scaled_soil", tag="shifted", align_bytes=64)
+        scaled_soil = keep.tile([P, PACK, M], F32, name="scaled_soil", tag="w2_bf0", align_bytes=64)
         for t in range(PACK):
             scale_soil(t, nc.vector, scaled_soil[:, t, :])
         both3 = keep.tile([P, 2, M], F32, name="both3", tag="w2_bf1", align_bytes=64)
         product(3, nc.vector, both3[:])
 
-        squared2 = keep.tile([P, 2, 2 * P], F32, name="squared2")
-        nc.vector.tensor_tensor(squared2[:], shifted2[:], both2[:, :, HALVES[0]], ALU.mult)
+        squared2 = shared.tile([P, 2, 2 * P], F32, name="squared2", align_bytes=64, offset=TABLE1_AT + 4096)
+        nc.vector.scalar_tensor_tensor(
+            squared2[:], both2[:, :, HALVES[0]], -3.125, both2[:, :, HALVES[0]], ALU.add, ALU.mult
+        )
         inverse = shared.tile([P, PACK, M], F32, name="inverse", align_bytes=64, offset=H7_AT - 6144)
         second = keep.tile([P, PACK, M], F32, name="second", tag="tissue0", align_bytes=64)
 

@@ -22,19 +22,16 @@ P = 128
 PACK = 4
 PASSES = 2
 TILES = H // P
-PAIRS = TILES // 2
 BANK = 512
-CHUNKS = M // P
-FIRST = 2
 LN5 = math.log(5.0)
 HALVES = (slice(0, 256), slice(256, 512))
 PIECES = (slice(0, 256), slice(256, 384), slice(384, 512))
+CHUNKS = M // P
 
-TABLE1_AT = 4096
-TABLE0_AT = 16384
-WORDS_AT = 27648
-LAST_AT = 53248
-H7_AT = 73728
+PICKED_AT = 1984
+TABLE1_AT = 19264
+TISSUE4_AT = 33536
+H7_AT = 41728
 
 
 def tile_list_burial_isotope_mobility_kernel(
@@ -52,26 +49,28 @@ def tile_list_burial_isotope_mobility_kernel(
         offs_sb = keep.tile([P, S // 16], U16, name="offs_sb")
         pos_sb = [keep.tile([P, M // 16], U16, name="pos%d_sb" % j) for j in range(3)]
         tab_scale_rows = keep.tile([P, T], U8, name="tab_scale_rows", align_bytes=64)
+        w4_scale_rows = keep.tile([32, H], U8, name="w4_scale_rows", align_bytes=64)
         tab_sb = [
-            shared.tile([P, T], I32, name="tab_sb0", align_bytes=64, offset=TABLE0_AT),
+            keep.tile([P, T], I32, name="tab_sb0", tag="tab_sb0", align_bytes=64),
             shared.tile([P, T], I32, name="tab_sb1", align_bytes=64, offset=TABLE1_AT),
         ]
         w4_rows = w4_words.rearrange("a p c -> p a c")
-        w4_first = keep.tile([P, PASSES, 2 * P * FIRST], U8, name="w4_first", align_bytes=64)
+        w4_raw = [
+            keep.tile([P, PASSES, H // 4], I32, name="w4_raw0", align_bytes=64),
+            shared.tile([P, PASSES, H // 4], I32, name="w4_raw1", align_bytes=64, offset=PICKED_AT + 64 - 2048),
+        ]
         planes = [keep.tile([P, S + H], U8, name="planes%d" % a, align_bytes=64) for a in range(PASSES)]
 
         nc.sync.dma_start(offs_sb[:], offs)
         nc.sync.dma_start(
             tab_scale_rows[0:32, :].bitcast(I32), tab_scales.rearrange("a q t -> (a q) t").bitcast(I32)
         )
-        w4_scale_rows = keep.tile([32, H], U8, name="w4_scale_rows", align_bytes=64)
         nc.sync.dma_start(w4_scale_rows[:].bitcast(I32), w4_scales.rearrange("a q c -> (a q) c").bitcast(I32))
-        nc.sync.dma_start(pos_sb[0][:], pos1)
-        nc.sync.dma_start(pos_sb[1][:], pos2)
         nc.sync.dma_start(tab_sb[0][:], tab_words[0].rearrange("p t i -> p (t i)").bitcast(I32))
-        nc.sync.dma_start(w4_first[:].bitcast(I32), w4_rows[:, :, : 2 * P * FIRST].bitcast(I32))
+        nc.sync.dma_start(w4_raw[0][:], w4_rows[:, :, :H].bitcast(I32))
+        for j, pos in enumerate((pos1, pos2, pos3)):
+            nc.sync.dma_start(pos_sb[j][:], pos)
         nc.sync.dma_start(tab_sb[1][:], tab_words[1].rearrange("p t i -> p (t i)").bitcast(I32))
-        nc.sync.dma_start(pos_sb[2][:], pos3)
 
         warm = keep.tile([P, 2, 8], F32, name="warm")
         nc.gpsimd.memset(warm[:, 0, :], 0.0)
@@ -84,146 +83,156 @@ def tile_list_burial_isotope_mobility_kernel(
         ident = keep.tile([P, P], F32, name="ident", align_bytes=64)
         make_identity(nc, ident[:])
 
-        picked_scale_rows = keep.tile([P, S], U8, name="picked_scale_rows", align_bytes=64)
+        picked_scale_rows = shared.tile([P, S], U8, name="picked_scale_rows", align_bytes=64, offset=PICKED_AT)
         nc.vector.tensor_copy(picked_scale_rows[:], tab_scale_rows[:].indirect(offs_sb[:]))
-        nc.vector.tensor_copy(planes[0][0:32, S : S + BANK].bitcast(I32), w4_scale_rows[:, :BANK].bitcast(I32))
-        nc.vector.tensor_copy(
-            planes[0][0:32, S + BANK :].bitcast(I32).rearrange("p (t u) -> p t u", t=PACK),
-            w4_scale_rows[:, BANK:].bitcast(I32).rearrange("p (u t) -> p t u", t=PACK),
+        nc.scalar.copy(
+            planes[0][0:32, S : S + BANK].bitcast(U32).rearrange("p (t u) -> p t u", t=PACK),
+            w4_scale_rows[:, :BANK].bitcast(U32).rearrange("p (u t) -> p t u", t=PACK),
         )
+        nc.scalar.copy(planes[0][0:32, S + BANK :].bitcast(U32), w4_scale_rows[:, BANK:].bitcast(U32))
         nc.vector.tensor_copy(planes[0][0:32, :S].bitcast(I32), picked_scale_rows[0:32, :].bitcast(I32))
         for a in range(PASSES):
             for q in range(4):
                 if (a, q) != (0, 0):
-                    nc.scalar.dma_start(
+                    nc.sync.dma_start(
                         planes[a][32 * q : 32 * q + 4, :].bitcast(I32),
                         planes[0][16 * a + 4 * q : 16 * a + 4 * q + 4, :].bitcast(I32),
                     )
 
-        v_words = {}
+        v_words = [keep.tile([P, S], U32, name="v_words%d" % a, align_bytes=64) for a in range(PASSES)]
 
-        def pick_words(a):
-            for half in range(2):
-                v_words[a, half] = shared.tile(
-                    [P, BANK], U32, name="v_words%d_%d" % (a, half), align_bytes=64, offset=WORDS_AT + 4096 * (2 * a + half)
-                )
-                nc.vector.tensor_copy(
-                    v_words[a, half][:],
-                    tab_sb[a][:].bitcast(U32).indirect(offs_sb[:, 32 * half : 32 * half + 32]),
-                )
+        def pick_words(a, start, stop):
+            nc.vector.tensor_copy(
+                v_words[a][:, start:stop], tab_sb[a][:].bitcast(U32).indirect(offs_sb[:, start // 16 : stop // 16])
+            )
 
-        pick_words(0)
-        w4_next = shared.tile([P, PASSES, 2 * P * (PACK - FIRST)], U8, name="w4_next", align_bytes=64, offset=TABLE0_AT)
-        nc.sync.dma_start(w4_next[:].bitcast(I32), w4_rows[:, :, 2 * P * FIRST : 2 * P * PACK].bitcast(I32))
-        w2_raw = [
-            shared.tile([P, PACK, N], F32, name="w2_raw0", align_bytes=64, offset=TABLE0_AT + 3072),
-            shared.tile([P, PACK, N], F32, name="w2_raw1", align_bytes=64, offset=TABLE1_AT + 4096),
-        ]
-        nc.sync.dma_start(w2_raw[0][:], w2[:BANK, :].rearrange("(p t) n -> p t n", t=PACK))
-        w4_raw = shared.tile([P, PASSES, H // 4], I32, name="w4_raw", align_bytes=64, offset=TABLE0_AT + 1024)
-        nc.sync.dma_start(w4_raw[:], w4_rows[:, :, 2 * P * PACK :].bitcast(I32))
-        pick_words(1)
-        w4_last = keep.tile([P, PACK, PASSES, 2 * P], U8, name="w4_last", align_bytes=64)
-        nc.vector.tensor_copy(
-            w4_last[:].bitcast(I32).rearrange("p t a (u e) -> p t a u e", e=2),
-            w4_raw[:].rearrange("p a (u t e) -> p t a u e", t=PACK, e=2),
+        w4_dealt = keep.tile([P, PACK, PASSES, 2 * P], U8, name="w4_dealt", align_bytes=64)
+        nc.scalar.copy(
+            w4_dealt[:].bitcast(U32).rearrange("p t a (u e) -> p t a u e", e=2),
+            w4_raw[0][:].bitcast(U32).rearrange("p a (u t e) -> p t a u e", t=PACK, e=2),
         )
+        pick_words(0, 0, 512)
+        pick_words(0, 512, 1024)
+        pick_words(1, 0, 512)
+        pick_words(1, 512, 768)
+        pick_words(1, 768, 1024)
 
         def w4_of(i, a):
-            if i < FIRST:
-                return w4_first[:, a, 2 * P * i : 2 * P * (i + 1)]
             if i < PACK:
-                return w4_next[:, a, 2 * P * (i - FIRST) : 2 * P * (i - FIRST + 1)]
-            return w4_last[:, i - PACK, a, :]
+                return w4_dealt[:, i, a, :]
+            return w4_raw[1][:, a, 64 * (i - PACK) : 64 * (i - PACK + 1)]
 
+        w2_raw = [
+            shared.tile([P, PACK, N], F32, name="w2_raw0", align_bytes=64, offset=PICKED_AT + S - 64),
+            shared.tile([P, PACK, N], F32, name="w2_raw1", align_bytes=64, offset=TABLE1_AT + 64 - 8192),
+        ]
         for e in range(4):
-            nc.sync.dma_start(w2_raw[1][e:P:4, :, :], w2[BANK:, :].rearrange("(u t e) n -> e u t n", t=PACK, e=4)[e])
-        gain_rows = shared.tile([P, BANK], F32, name="gain_rows", align_bytes=64, offset=TABLE1_AT)
-        nc.sync.dma_start(gain_rows[:], gain[:BANK].partition_broadcast(P))
-        gain_cols = shared.tile([P, 8], F32, name="gain_cols", align_bytes=64, offset=TABLE1_AT + 2048)
+            nc.sync.dma_start(w2_raw[0][e:P:4, :, :], w2[:BANK, :].rearrange("(u t e) n -> e u t n", t=PACK, e=4)[e])
+        nc.sync.dma_start(w4_raw[1][:], w4_rows[:, :, H:].bitcast(I32))
+        nc.sync.dma_start(w2_raw[1][:], w2[BANK:, :].rearrange("(p t) n -> p t n", t=PACK))
+        gain_cols = shared.tile([P, 8], F32, name="gain_cols", align_bytes=64, offset=TABLE1_AT + 64)
         with nc.allow_non_contiguous_dma(reason="gain: one value for each partition and row tile"):
             for e in range(4):
-                nc.sync.dma_start(gain_cols[e:P:4, 0:PACK], gain[BANK:].rearrange("(u t e) -> e u t", t=PACK, e=4)[e])
-
-        neg_h = [keep.tile([P, S], F32, name="neg_h%d" % i, align_bytes=64) for i in range(TILES - 1)]
-        neg_h.append(shared.tile([P, S], F32, name="neg_h7", align_bytes=64, offset=H7_AT))
-        tissue = [keep.tile([P, 2, 2, M], F32, name="tissue%d" % k, tag="tissue%d" % k, align_bytes=64) for k in range(PAIRS - 1)]
-        tissue.append(shared.tile([P, 2, 2, M], F32, name="tissue3", align_bytes=64, offset=LAST_AT))
-
-        for i in range(TILES):
-            banks = []
-            for half in range(2):
-                banks.append(bank((2 * i + half) % 8, [P, BANK], "h_bank"))
-                for a in range(PASSES):
-                    nc.tensor.matmul_mx(
-                        out=banks[half][:],
-                        lhsT=w4_of(i, a).bitcast(FP4X4),
-                        lhsT_scale=planes[a][:, S + P * i : S + P * (i + 1)],
-                        rhs=v_words[a, half][:].bitcast(FP8X4),
-                        rhs_scale=planes[a][:, BANK * half : BANK * (half + 1)],
-                        start=(a == 0),
-                        stop=(a == PASSES - 1),
-                    )
-            for half in range(2):
-                cols = slice(BANK * half, BANK * (half + 1))
-                if (i, half) == (0, 1):
-                    nc.scalar.activation(neg_h[i][:, cols], banks[half][:], ACT.Copy, scale=-1.0)
-                else:
-                    nc.vector.tensor_scalar(neg_h[i][:, cols], banks[half][:], -1.0, None, ALU.mult)
-            for j in range(2):
-                nc.scalar.activation(
-                    tissue[i // 2][:, j, i % 2, :], neg_h[i][:].indirect(pos_sb[j][:]), ACT.Sigmoid, bias=LN5, scale=-1.0
-                )
+                nc.sync.dma_start(gain_cols[e:P:4, 0:PACK], gain[:BANK].rearrange("(u t e) -> e u t", t=PACK, e=4)[e])
+        gain_rows = shared.tile([P, BANK], F32, name="gain_rows", align_bytes=64, offset=TABLE1_AT + 128)
+        nc.sync.dma_start(gain_rows[:], gain[BANK:].partition_broadcast(P))
 
         w2_bf = []
         for b in range(PASSES):
-            w2_bf.append(keep.tile([P, N, PACK], BF16, name="w2_bf%d" % b, tag="w2_bf%d" % b, align_bytes=64))
+            w2_bf.append(
+                shared.tile([P, N, PACK], BF16, name="w2_bf%d" % b, align_bytes=64, offset=H7_AT + 20352 + 4096 * (1 - b))
+            )
             nc.gpsimd.tensor_scalar(w2_bf[b][:], w2_raw[b][:].rearrange("p t n -> p n t"), 1.0, 0.0, ALU.mult, ALU.add)
 
-        soil_pairs = [
-            shared.tile([P, 2, M], F32, name="neg_soil%d" % k, align_bytes=64, offset=WORDS_AT + 4096 * k) for k in range(PAIRS)
-        ]
-        neg_soil = [soil_pairs[i // 2][:, i % 2, :] for i in range(TILES)]
-        sums = {}
-        for i in list(range(PACK, TILES)) + list(range(PACK)):
-            nc.vector.tensor_copy(neg_soil[i], neg_h[i][:].indirect(pos_sb[2][:]))
+        h = [keep.tile([P, S], F32, name="h%d" % i, align_bytes=64) for i in range(TILES - 1)]
+        h.append(shared.tile([P, S], F32, name="h7", align_bytes=64, offset=H7_AT))
+        tissue_first = keep.tile([P, 2, PACK, M], F32, name="tissue_first", align_bytes=64)
+        tissue4 = shared.tile([P, 2, M], F32, name="tissue4", align_bytes=64, offset=TISSUE4_AT)
+        tissue_last = keep.tile([P, 2, PACK - 1, M], F32, name="tissue_last", align_bytes=64)
+
+        def tissue(j, i):
             if i < PACK:
-                for c in range(CHUNKS):
-                    if i == 0:
-                        sums[c] = bank(c, [P, BANK], "sums")
-                    nc.tensor.matmul(
-                        sums[c][:, P * i : P * (i + 1)],
-                        neg_soil[i][:, P * c : P * (c + 1)],
-                        ident[:],
-                        start=(i == 0),
-                        stop=False,
-                        is_transpose=True,
-                    )
+                return tissue_first[:, j, i, :]
+            if i == PACK:
+                return tissue4[:, j, :]
+            return tissue_last[:, j, i - PACK - 1, :]
 
-        both = {}
-        offset_of = {}
+        soil = [keep.tile([P, PACK, M], F32, name="soil%d" % b, tag="soil%d" % b, align_bytes=64) for b in range(PASSES)]
+        scaled = keep.tile([P, PACK, M], F32, name="scaled", align_bytes=64)
 
-        def product(pair, engine, tile):
-            both[pair] = tile
-            engine.tensor_tensor(tile, tissue[pair][:, 0], tissue[pair][:, 1], ALU.mult)
+        def first_product(i, cols, number, a, opened):
+            if a == 0:
+                opened[i, cols.start] = bank(number, [P, cols.stop - cols.start], "h_bank")
+            nc.tensor.matmul_mx(
+                out=opened[i, cols.start][:],
+                lhsT=w4_of(i, a).bitcast(FP4X4),
+                lhsT_scale=planes[a][:, S + P * i : S + P * (i + 1)],
+                rhs=v_words[a][:, cols].bitcast(FP8X4),
+                rhs_scale=planes[a][:, cols],
+                start=(a == 0),
+                stop=(a == PASSES - 1),
+            )
 
-        def scale_soil(t, engine, rows):
-            offset_of[t] = rows
-            engine.tensor_scalar(rows, neg_soil[PACK + t], -0.25, gain_cols[:, t : t + 1], ALU.add, ALU.mult)
+        sums = {}
 
-        both_first = shared.tile([P, PACK, M], F32, name="both_first", align_bytes=64, offset=TABLE1_AT + 4096)
-        shifted = keep.tile([P, M], F32, name="shifted")
-        squared = keep.tile([P, PACK, M], F32, name="squared", tag="tissue0", align_bytes=64)
-        for i in range(2):
-            nc.gpsimd.tensor_tensor(both_first[:, i, :], tissue[0][:, 0, i], tissue[0][:, 1, i], ALU.mult)
-        nc.gpsimd.tensor_scalar(shifted[:], both_first[:, 0, :], 1.0, -3.125, ALU.mult, ALU.add)
-        product(1, nc.gpsimd, both_first[:, 2:4, :])
-        nc.gpsimd.tensor_tensor(squared[:, 0, :], shifted[:], both_first[:, 0, :], ALU.mult)
-        both2 = keep.tile([P, 2, M], F32, name="both2", tag="tissue1", align_bytes=64)
-        product(2, nc.gpsimd, both2[:])
-        nc.vector.scalar_tensor_tensor(squared[:, 1:, :], both_first[:, 1:, :], -3.125, both_first[:, 1:, :], ALU.add, ALU.mult)
+        def turn_into_sums(rows, t, c, first, last):
+            nc.tensor.matmul(
+                sums[c][:, P * t : P * (t + 1)], rows[:, t, P * c : P * (c + 1)], ident[:], start=first, stop=last, is_transpose=True
+            )
 
-        w2_codes = keep.tile([P, PASSES, N], U32, name="w2_codes", tag="tissue2", align_bytes=64)
+        def pick_soil(i):
+            nc.vector.tensor_copy(soil[i // PACK][:, i % PACK, :], h[i][:].indirect(pos_sb[2][:]))
+
+        opened = {}
+        first_cols = (slice(0, 512), slice(512, 768), slice(768, 1024))
+        for a in range(PASSES):
+            for number, cols in enumerate(first_cols):
+                first_product(0, cols, number, a, opened)
+        nc.scalar.copy(h[0][:, first_cols[0]], opened[0, 0][:])
+        nc.vector.tensor_copy(h[0][:, first_cols[1]], opened[0, 512][:])
+        nc.vector.tensor_copy(h[0][:, first_cols[2]], opened[0, 768][:])
+        for i in range(TILES):
+            sign = 1.0 if i < PACK else -1.0
+            if i > 0:
+                for half in range(2):
+                    cols = slice(BANK * half, BANK * (half + 1))
+                    for a in range(PASSES):
+                        first_product(i, cols, (2 * i + half + 1) % 4, a, opened)
+                    if (i, half) == (1, 0):
+                        nc.scalar.activation(h[i][:, cols], opened[i, cols.start][:], ACT.Copy, scale=sign)
+                    else:
+                        nc.vector.tensor_scalar(h[i][:, cols], opened[i, cols.start][:], sign, None, ALU.mult)
+            for j in range(2):
+                nc.scalar.activation(
+                    tissue(j, i), h[i][:].indirect(pos_sb[j][:]), ACT.Sigmoid, bias=LN5, scale=sign
+                )
+            if i > 1:
+                pick_soil(i - 2)
+        pick_soil(TILES - 2)
+        pick_soil(TILES - 1)
+        for t in range(PACK):
+            for c in range(CHUNKS):
+                if t == 0:
+                    sums[c] = bank(c, [P, BANK], "sums")
+                turn_into_sums(soil[1], t, c, t == 0, False)
+
+        both_first = shared.tile([P, PACK, M], F32, name="both_first", align_bytes=64, offset=TABLE1_AT + 64 - 8192)
+        both4 = keep.tile([P, M], F32, name="both4", tag="soil0", align_bytes=64)
+        both_last = shared.tile([P, PACK - 1, M], F32, name="both_last", align_bytes=64, offset=TISSUE4_AT + 64 - 6144)
+        squared = keep.tile([P, PACK, M], F32, name="squared", align_bytes=64)
+
+        for pair in range(2):
+            nc.gpsimd.tensor_tensor(
+                both_first[:, 2 * pair : 2 * pair + 2],
+                tissue_first[:, 0, 2 * pair : 2 * pair + 2],
+                tissue_first[:, 1, 2 * pair : 2 * pair + 2],
+                ALU.mult,
+            )
+            for t in (2 * pair, 2 * pair + 1):
+                nc.gpsimd.tensor_scalar(scaled[:, t, :], soil[0][:, t, :], 0.25, gain_cols[:, t : t + 1], ALU.add, ALU.mult)
+        nc.gpsimd.tensor_tensor(both4[:], tissue(0, PACK), tissue(1, PACK), ALU.mult)
+
+        w2_codes = shared.tile([P, PASSES, N], U32, name="w2_codes", align_bytes=64, offset=TISSUE4_AT + 4096 - 64)
         w2_scale = keep.tile([P, PASSES, N], U8, name="w2_scale", align_bytes=64)
         for b in range(PASSES):
             nc.vector.quantize_mx(
@@ -232,137 +241,124 @@ def tile_list_burial_isotope_mobility_kernel(
                 in_=w2_bf[b][:].rearrange("p n t -> p (n t)"),
             )
 
-        scaled_soil = keep.tile([P, PACK, M], F32, name="scaled_soil", tag="w2_bf0", align_bytes=64)
-        for t in range(PACK):
-            scale_soil(t, nc.vector, scaled_soil[:, t, :])
-        both3 = keep.tile([P, 2, M], F32, name="both3", tag="w2_bf1", align_bytes=64)
-        product(3, nc.vector, both3[:])
+        def product(i):
+            nc.vector.tensor_tensor(both_last[:, i - 5], tissue(0, i), tissue(1, i), ALU.mult)
 
-        squared2 = shared.tile([P, 2, 2 * P], F32, name="squared2", align_bytes=64, offset=TABLE1_AT + 4096)
-        nc.vector.scalar_tensor_tensor(
-            squared2[:], both2[:, :, HALVES[0]], -3.125, both2[:, :, HALVES[0]], ALU.add, ALU.mult
-        )
-        inverse = shared.tile([P, PACK, M], F32, name="inverse", align_bytes=64, offset=H7_AT - 6144)
-        second = keep.tile([P, PACK, M], F32, name="second", tag="tissue0", align_bytes=64)
+        def square(i):
+            row = both4[:] if i == PACK else both_last[:, i - 5]
+            nc.vector.scalar_tensor_tensor(squared[:, i - PACK], row, -3.125, row, ALU.add, ALU.mult)
+
+        square(4)
+        product(5)
+        product(6)
+        square(5)
+        product(7)
+        square(6)
+        square(7)
+
+        roots = shared.tile([P, PASSES, PACK, M], F32, name="roots", align_bytes=64, offset=H7_AT + 4096 - 64)
+        term, inverse = roots[:, 0], roots[:, 1]
+        z_bf = keep.tile([P, M * PACK], BF16, name="z_bf", tag="tab_sb0", align_bytes=64)
+        z_codes = keep.tile([P, PASSES, M], U32, name="z_codes", align_bytes=64)
+        z_scale = keep.tile([P, PASSES, M], U8, name="z_scale", align_bytes=64)
+        z_rows = keep.tile([P, CHUNKS, BANK], BF16, name="z_rows", align_bytes=64)
+        z_words = [keep.tile([P, 2, P, 2], F32, name="z_words%d" % half, align_bytes=64) for half in range(2)]
+
+        def root(pair, cols):
+            rows = slice(2 * pair, 2 * pair + 2)
+            nc.scalar.activation(term[:, rows, cols], both_first[:, rows, cols], ACT.Abs_reciprocal_sqrt, bias=4.0, scale=-2.56)
+
+        def times_gain(t, cols):
+            row = term[:, t, cols]
+            nc.vector.scalar_tensor_tensor(row, row, gain_cols[:, t : t + 1], row, ALU.mult, ALU.mult)
+
+        def weave(cols):
+            nc.vector.tensor_tensor(
+                z_bf[:, PACK * cols.start : PACK * cols.stop].rearrange("p (g i t) -> p g t i", i=2, t=PACK),
+                term[:, :, cols].rearrange("p t (g i) -> p g t i", i=2),
+                scaled[:, :, cols].rearrange("p t (g i) -> p g t i", i=2),
+                ALU.subtract,
+            )
 
         def invert(c):
             cols = slice(P * c, P * (c + 1))
             nc.scalar.activation(inverse[:, :, cols], squared[:, :, cols], ACT.Abs_reciprocal_sqrt, bias=16.0, scale=6.5536)
-            for i in range(PACK):
-                nc.tensor.matmul(
-                    sums[c][:, P * i : P * (i + 1)],
-                    inverse[:, i, cols],
-                    ident[:],
-                    start=False,
-                    stop=(i == PACK - 1),
-                    is_transpose=True,
-                )
-
-        z_rows = {}
-        z_bf = keep.tile([P, M * PACK], BF16, name="z_bf", align_bytes=64)
-        z_codes = keep.tile([P, PASSES, M], U32, name="z_codes", align_bytes=64)
-        z_scale = keep.tile([P, PASSES, M], U8, name="z_scale", align_bytes=64)
-        term = shared.tile([P, PACK, M], F32, name="term", align_bytes=64, offset=LAST_AT + 64 + 4096)
+            for t in range(PACK):
+                turn_into_sums(inverse, t, c, False, t == PACK - 1)
 
         def scale_by_gain(c):
-            z_rows[c] = shared.tile([P, BANK], BF16, name="z_rows%d" % c, align_bytes=64, offset=LAST_AT + 64 + 1024 * c)
-            nc.vector.scalar_tensor_tensor(z_rows[c][:], sums[c][:], -0.25, gain_rows[:], ALU.add, ALU.mult)
+            nc.vector.scalar_tensor_tensor(z_rows[:, c], sums[c][:], -0.25, gain_rows[:], ALU.add, ALU.mult)
 
-        z_words = {}
-
-        def turn_back(c, copy):
+        def turn_back(c):
             turned = bank(c, [P, 2, P], "turned")
-            words = z_rows[c][:].bitcast(F32)
+            words = z_rows[:, c].bitcast(F32)
             for u in range(2):
                 nc.tensor.transpose(turned[:, u, :], words[:, u : 2 * P : 2], ident[:])
-            if c % 2 == 0:
-                z_words[c // 2] = keep.tile([P, 2, P, 2], F32, name="z_words%d" % (c // 2), align_bytes=64)
-            copy(z_words[c // 2][:, c % 2], turned[:].rearrange("p u m -> p m u"))
+            nc.scalar.copy(z_words[c // 2][:, c % 2], turned[:].rearrange("p u m -> p m u"))
 
-        def quantize_first(half):
+        def quantize_woven(cols):
             nc.vector.quantize_mx(
-                out=z_codes[:, 0, HALVES[half]].bitcast(FP8X4),
-                scales=z_scale[:, 0, HALVES[half]],
-                in_=z_words[half][:].rearrange("p c m u -> p (c m u)").bitcast(BF16),
-            )
-
-        def combine(t, cols):
-            nc.vector.scalar_tensor_tensor(
-                term[:, t, cols], second[:, t, cols], gain_cols[:, t : t + 1], offset_of[t][:, cols], ALU.mult, ALU.add
-            )
-
-        def weave(cols, copy):
-            copy(
-                z_bf[:, PACK * cols.start : PACK * cols.stop].rearrange("p (g i t) -> p g t i", i=4, t=PACK),
-                term[:, :, cols].rearrange("p t (g i) -> p g t i", i=4),
-            )
-
-        def quantize_second(cols):
-            nc.vector.quantize_mx(
-                out=z_codes[:, 1, cols].bitcast(FP8X4),
-                scales=z_scale[:, 1, cols],
+                out=z_codes[:, 0, cols].bitcast(FP8X4),
+                scales=z_scale[:, 0, cols],
                 in_=z_bf[:, PACK * cols.start : PACK * cols.stop],
             )
 
-        results = [(4, PIECES[0], (0, 1)), (5, PIECES[0], (2, 3)), (6, PIECES[1], (0, 1)), (1, PIECES[1], (2, 3)), (7, PIECES[2], (0, 1)), (0, PIECES[2], (2, 3))]
-        acc = {}
-
-        def multiply(k, b):
-            number, cols, rows = results[k]
-            if b == 0:
-                acc[k] = bank(number, [P, len(rows), cols.stop - cols.start], "acc")
-            for place, j in enumerate(rows):
-                nc.tensor.matmul_mx(
-                    out=acc[k][:, place, :],
-                    lhsT=w2_codes[:, b, P * j : P * (j + 1)].bitcast(FP8X4),
-                    lhsT_scale=w2_scale[:, b, P * j : P * (j + 1)],
-                    rhs=z_codes[:, b, cols].bitcast(FP8X4),
-                    rhs_scale=z_scale[:, b, cols],
-                    start=(b == 0 and place == 0),
-                    stop=(b == PASSES - 1 and place == len(rows) - 1),
-                )
-
-        def store(k, copy_out):
-            number, cols, rows = results[k]
-            result = keep.tile([P, len(rows), cols.stop - cols.start], F32, name="result%d" % k)
-            copy_out(result[:], acc[k][:])
-            nc.sync.dma_start(
-                out[P * rows[0] : P * (rows[-1] + 1), cols].rearrange("(j p) m -> p j m", p=P), result[:]
+        def quantize_turned(half):
+            nc.vector.quantize_mx(
+                out=z_codes[:, 1, HALVES[half]].bitcast(FP8X4),
+                scales=z_scale[:, 1, HALVES[half]],
+                in_=z_words[half][:].rearrange("p c m u -> p (c m u)").bitcast(BF16),
             )
 
-        def invert_second(cols):
-            for pair in (2, 3):
-                rows = second[:, 2 * pair - 4 : 2 * pair - 2, cols]
-                if pair == 2 and cols == HALVES[0]:
-                    nc.scalar.activation(rows, squared2[:], ACT.Abs_reciprocal_sqrt, bias=16.0, scale=6.5536)
-                    continue
-                nc.scalar.activation(rows, both[pair][:, :, cols], ACT.Abs_reciprocal_sqrt, bias=4.0, scale=-2.56)
-                nc.scalar.activation(rows, rows, ACT.Square)
+        def multiply_and_store(piece, first_row, order, copy_out):
+            cols = PIECES[piece]
+            number = 2 * piece + first_row // 2
+            acc = bank((4 + number) % 8, [P, 2, cols.stop - cols.start], "acc")
+            for step, b in enumerate(order):
+                for place in range(2):
+                    j = first_row + place
+                    nc.tensor.matmul_mx(
+                        out=acc[:, place, :],
+                        lhsT=w2_codes[:, b, P * j : P * (j + 1)].bitcast(FP8X4),
+                        lhsT_scale=w2_scale[:, b, P * j : P * (j + 1)],
+                        rhs=z_codes[:, b, cols].bitcast(FP8X4),
+                        rhs_scale=z_scale[:, b, cols],
+                        start=(step == 0 and place == 0),
+                        stop=(step == 1 and place == 1),
+                    )
+            result = keep.tile([P, 2, cols.stop - cols.start], F32, name="result%d" % number)
+            copy_out(result[:], acc[:])
+            nc.sync.dma_start(out[P * first_row : P * (first_row + 2), cols].rearrange("(j p) m -> p j m", p=P), result[:])
 
+        for pair in range(2):
+            root(pair, HALVES[0])
+            for t in (2 * pair, 2 * pair + 1):
+                times_gain(t, HALVES[0])
+        weave(HALVES[0])
         for c in range(CHUNKS):
             invert(c)
-        invert_second(HALVES[0])
-        for c in range(CHUNKS):
-            scale_by_gain(c)
         for c in range(2):
-            turn_back(c, nc.scalar.copy)
-        invert_second(HALVES[1])
+            scale_by_gain(c)
+        quantize_woven(HALVES[0])
+        for pair in range(2):
+            root(pair, HALVES[1])
+        for c in range(2):
+            turn_back(c)
+        scale_by_gain(2)
+        quantize_turned(0)
+        scale_by_gain(3)
         for c in range(2, CHUNKS):
-            turn_back(c, nc.scalar.copy)
+            turn_back(c)
+        for first_row in (0, 2):
+            multiply_and_store(0, first_row, (0, 1), nc.scalar.copy)
         for t in range(PACK):
-            combine(t, HALVES[0])
-        quantize_first(0)
-        weave(PIECES[0], nc.vector.tensor_copy)
-        combine(0, HALVES[1])
-        quantize_second(PIECES[0])
-        for t in range(1, PACK):
-            combine(t, HALVES[1])
-        weave(PIECES[1], nc.vector.tensor_copy)
-        quantize_first(1)
-        weave(PIECES[2], nc.vector.tensor_copy)
-        quantize_second(PIECES[1])
-        quantize_second(PIECES[2])
-        for k in range(6):
-            multiply(k, 0)
-            multiply(k, 1)
-            store(k, nc.vector.tensor_copy if k in (3, 5) else nc.scalar.copy)
+            times_gain(t, HALVES[1])
+        weave(PIECES[1])
+        quantize_turned(1)
+        weave(PIECES[2])
+        quantize_woven(PIECES[1])
+        quantize_woven(PIECES[2])
+        for piece in (1, 2):
+            for first_row in (0, 2):
+                last = piece == 2 and first_row == 2
+                multiply_and_store(piece, first_row, (1, 0), nc.vector.tensor_copy if last else nc.scalar.copy)

@@ -30,8 +30,8 @@ CHUNKS = M // P
 
 PICKED_AT = 1984
 TABLE1_AT = 19264
-TISSUE4_AT = 33536
-H7_AT = 41728
+H7_AT = 27456
+SOIL_AT = (62208, 74496)
 
 
 def tile_list_burial_isotope_mobility_kernel(
@@ -99,7 +99,9 @@ def tile_list_burial_isotope_mobility_kernel(
                         planes[0][16 * a + 4 * q : 16 * a + 4 * q + 4, :].bitcast(I32),
                     )
 
-        v_words = [keep.tile([P, S], U32, name="v_words%d" % a, align_bytes=64) for a in range(PASSES)]
+        v_words = [
+            shared.tile([P, S], U32, name="v_words%d" % a, align_bytes=64, offset=SOIL_AT[a]) for a in range(PASSES)
+        ]
 
         def pick_words(a, start, stop):
             nc.vector.tensor_copy(
@@ -130,11 +132,11 @@ def tile_list_burial_isotope_mobility_kernel(
             nc.sync.dma_start(w2_raw[0][e:P:4, :, :], w2[:BANK, :].rearrange("(u t e) n -> e u t n", t=PACK, e=4)[e])
         nc.sync.dma_start(w4_raw[1][:], w4_rows[:, :, H:].bitcast(I32))
         nc.sync.dma_start(w2_raw[1][:], w2[BANK:, :].rearrange("(p t) n -> p t n", t=PACK))
-        gain_cols = shared.tile([P, 8], F32, name="gain_cols", align_bytes=64, offset=TABLE1_AT + 64)
+        gain_cols = shared.tile([P, 8], F32, name="gain_cols", align_bytes=64, offset=TABLE1_AT + 192)
         with nc.allow_non_contiguous_dma(reason="gain: one value for each partition and row tile"):
             for e in range(4):
                 nc.sync.dma_start(gain_cols[e:P:4, 0:PACK], gain[:BANK].rearrange("(u t e) -> e u t", t=PACK, e=4)[e])
-        gain_rows = shared.tile([P, BANK], F32, name="gain_rows", align_bytes=64, offset=TABLE1_AT + 128)
+        gain_rows = shared.tile([P, BANK], F32, name="gain_rows", align_bytes=64, offset=TABLE1_AT + 256)
         nc.sync.dma_start(gain_rows[:], gain[BANK:].partition_broadcast(P))
 
         w2_bf = []
@@ -146,8 +148,8 @@ def tile_list_burial_isotope_mobility_kernel(
 
         h = [keep.tile([P, S], F32, name="h%d" % i, align_bytes=64) for i in range(TILES - 1)]
         h.append(shared.tile([P, S], F32, name="h7", align_bytes=64, offset=H7_AT))
-        tissue_first = keep.tile([P, 2, PACK, M], F32, name="tissue_first", align_bytes=64)
-        tissue4 = shared.tile([P, 2, M], F32, name="tissue4", align_bytes=64, offset=TISSUE4_AT)
+        tissue_first = keep.tile([P, 2, PACK, M], F32, name="tissue_first", tag="tissue_first", align_bytes=64)
+        tissue4 = keep.tile([P, 2, M], F32, name="tissue4", align_bytes=64)
         tissue_last = keep.tile([P, 2, PACK - 1, M], F32, name="tissue_last", align_bytes=64)
 
         def tissue(j, i):
@@ -157,8 +159,15 @@ def tile_list_burial_isotope_mobility_kernel(
                 return tissue4[:, j, :]
             return tissue_last[:, j, i - PACK - 1, :]
 
-        soil = [keep.tile([P, PACK, M], F32, name="soil%d" % b, tag="soil%d" % b, align_bytes=64) for b in range(PASSES)]
-        scaled = keep.tile([P, PACK, M], F32, name="scaled", align_bytes=64)
+        soil = [
+            shared.tile([P, PACK, M], F32, name="soil%d" % b, align_bytes=64, offset=SOIL_AT[b]) for b in range(PASSES)
+        ]
+        soil_first = keep.tile([P, M], F32, name="soil_first", align_bytes=64)
+
+        def soil_of(i):
+            return soil_first[:] if i == 0 else soil[i // PACK][:, i % PACK, :]
+
+        scaled = shared.tile([P, PACK, M], F32, name="scaled", align_bytes=64, offset=TABLE1_AT + 128 - 16384)
 
         def first_product(i, cols, number, a, opened):
             if a == 0:
@@ -181,7 +190,7 @@ def tile_list_burial_isotope_mobility_kernel(
             )
 
         def pick_soil(i):
-            nc.vector.tensor_copy(soil[i // PACK][:, i % PACK, :], h[i][:].indirect(pos_sb[2][:]))
+            nc.vector.tensor_copy(soil_of(i), h[i][:].indirect(pos_sb[2][:]))
 
         opened = {}
         first_cols = (slice(0, 512), slice(512, 768), slice(768, 1024))
@@ -197,7 +206,7 @@ def tile_list_burial_isotope_mobility_kernel(
                 for half in range(2):
                     cols = slice(BANK * half, BANK * (half + 1))
                     for a in range(PASSES):
-                        first_product(i, cols, (2 * i + half + 1) % 4, a, opened)
+                        first_product(i, cols, 2 * i + half - 4 if i in (4, 5) else (2 * i + half + 1) % 4, a, opened)
                     if (i, half) == (1, 0):
                         nc.scalar.activation(h[i][:, cols], opened[i, cols.start][:], ACT.Copy, scale=sign)
                     else:
@@ -206,33 +215,35 @@ def tile_list_burial_isotope_mobility_kernel(
                 nc.scalar.activation(
                     tissue(j, i), h[i][:].indirect(pos_sb[j][:]), ACT.Sigmoid, bias=LN5, scale=sign
                 )
-            if i > 1:
-                pick_soil(i - 2)
-        pick_soil(TILES - 2)
-        pick_soil(TILES - 1)
+        for i in range(TILES):
+            pick_soil(i)
         for t in range(PACK):
             for c in range(CHUNKS):
                 if t == 0:
                     sums[c] = bank(c, [P, BANK], "sums")
                 turn_into_sums(soil[1], t, c, t == 0, False)
 
-        both_first = shared.tile([P, PACK, M], F32, name="both_first", align_bytes=64, offset=TABLE1_AT + 64 - 8192)
-        both4 = keep.tile([P, M], F32, name="both4", tag="soil0", align_bytes=64)
-        both_last = shared.tile([P, PACK - 1, M], F32, name="both_last", align_bytes=64, offset=TISSUE4_AT + 64 - 6144)
+        both_first = shared.tile([P, PACK, M], F32, name="both_first", align_bytes=64, offset=TABLE1_AT + 128 - 8192)
+        both4 = keep.tile([P, M], F32, name="both4", tag="tissue_first", align_bytes=64)
+        both_last = shared.tile([P, PACK - 1, M], F32, name="both_last", align_bytes=64, offset=SOIL_AT[0] + 64 - 6144)
         squared = keep.tile([P, PACK, M], F32, name="squared", align_bytes=64)
 
-        for pair in range(2):
-            nc.gpsimd.tensor_tensor(
-                both_first[:, 2 * pair : 2 * pair + 2],
-                tissue_first[:, 0, 2 * pair : 2 * pair + 2],
-                tissue_first[:, 1, 2 * pair : 2 * pair + 2],
-                ALU.mult,
-            )
-            for t in (2 * pair, 2 * pair + 1):
-                nc.gpsimd.tensor_scalar(scaled[:, t, :], soil[0][:, t, :], 0.25, gain_cols[:, t : t + 1], ALU.add, ALU.mult)
-        nc.gpsimd.tensor_tensor(both4[:], tissue(0, PACK), tissue(1, PACK), ALU.mult)
+        def pair_product(pair):
+            rows = slice(2 * pair, 2 * pair + 2)
+            nc.gpsimd.tensor_tensor(both_first[:, rows], tissue_first[:, 0, rows], tissue_first[:, 1, rows], ALU.mult)
 
-        w2_codes = shared.tile([P, PASSES, N], U32, name="w2_codes", align_bytes=64, offset=TISSUE4_AT + 4096 - 64)
+        def scale_soil(t):
+            nc.gpsimd.tensor_scalar(scaled[:, t, :], soil_of(t), 0.25, gain_cols[:, t : t + 1], ALU.add, ALU.mult)
+
+        pair_product(0)
+        scale_soil(0)
+        pair_product(1)
+        scale_soil(1)
+        scale_soil(2)
+        nc.gpsimd.tensor_tensor(both4[:], tissue(0, PACK), tissue(1, PACK), ALU.mult)
+        scale_soil(3)
+
+        w2_codes = shared.tile([P, PASSES, N], U32, name="w2_codes", align_bytes=64, offset=SOIL_AT[0] + 8192 - 64)
         w2_scale = keep.tile([P, PASSES, N], U8, name="w2_scale", align_bytes=64)
         for b in range(PASSES):
             nc.vector.quantize_mx(

@@ -285,9 +285,9 @@ def tile_list_burial_isotope_mobility_kernel(
 
         def weave(cols):
             nc.vector.tensor_tensor(
-                z_bf[:, PACK * cols.start : PACK * cols.stop].rearrange("p (g i t) -> p g t i", i=2, t=PACK),
-                term[:, :, cols].rearrange("p t (g i) -> p g t i", i=2),
-                scaled[:, :, cols].rearrange("p t (g i) -> p g t i", i=2),
+                z_bf[:, PACK * cols.start : PACK * cols.stop].rearrange("p (g i t) -> p g t i", i=4, t=PACK),
+                term[:, :, cols].rearrange("p t (g i) -> p g t i", i=4),
+                scaled[:, :, cols].rearrange("p t (g i) -> p g t i", i=4),
                 ALU.subtract,
             )
 

@@ -31,7 +31,7 @@ CHUNKS = M // P
 PICKED_AT = 1984
 TABLE1_AT = 19264
 H7_AT = 27456
-SOIL_AT = (62208, 74496)
+SOIL_AT = (74560, 62208)
 
 
 def tile_list_burial_isotope_mobility_kernel(
@@ -85,19 +85,16 @@ def tile_list_burial_isotope_mobility_kernel(
 
         picked_scale_rows = shared.tile([P, S], U8, name="picked_scale_rows", align_bytes=64, offset=PICKED_AT)
         nc.vector.tensor_copy(picked_scale_rows[:], tab_scale_rows[:].indirect(offs_sb[:]))
+        nc.scalar.copy(planes[0][0:32, S : S + BANK].bitcast(U32), w4_scale_rows[:, :BANK].bitcast(U32))
         nc.scalar.copy(
-            planes[0][0:32, S : S + BANK].bitcast(U32).rearrange("p (t u) -> p t u", t=PACK),
-            w4_scale_rows[:, :BANK].bitcast(U32).rearrange("p (u t) -> p t u", t=PACK),
+            planes[0][0:32, S + BANK :].bitcast(U32).rearrange("p (t u) -> p t u", t=PACK),
+            w4_scale_rows[:, BANK:].bitcast(U32).rearrange("p (u t) -> p t u", t=PACK),
         )
-        nc.scalar.copy(planes[0][0:32, S + BANK :].bitcast(U32), w4_scale_rows[:, BANK:].bitcast(U32))
         nc.vector.tensor_copy(planes[0][0:32, :S].bitcast(I32), picked_scale_rows[0:32, :].bitcast(I32))
-        for a in range(PASSES):
-            for q in range(4):
-                if (a, q) != (0, 0):
-                    nc.sync.dma_start(
-                        planes[a][32 * q : 32 * q + 4, :].bitcast(I32),
-                        planes[0][16 * a + 4 * q : 16 * a + 4 * q + 4, :].bitcast(I32),
-                    )
+        for q in range(1, 4):
+            nc.sync.dma_start(planes[0][32 * q : 32 * q + 4, :].bitcast(I32), planes[0][4 * q : 4 * q + 4, :].bitcast(I32))
+        for r in range(4):
+            nc.sync.dma_start(planes[1][r:P:32, :].bitcast(I32), planes[0][16 + r : 32 : 4, :].bitcast(I32))
 
         v_words = [
             shared.tile([P, S], U32, name="v_words%d" % a, align_bytes=64, offset=SOIL_AT[a]) for a in range(PASSES)
@@ -109,10 +106,6 @@ def tile_list_burial_isotope_mobility_kernel(
             )
 
         w4_dealt = keep.tile([P, PACK, PASSES, 2 * P], U8, name="w4_dealt", align_bytes=64)
-        nc.scalar.copy(
-            w4_dealt[:].bitcast(U32).rearrange("p t a (u e) -> p t a u e", e=2),
-            w4_raw[0][:].bitcast(U32).rearrange("p a (u t e) -> p t a u e", t=PACK, e=2),
-        )
         pick_words(0, 0, 512)
         pick_words(0, 512, 1024)
         pick_words(1, 0, 512)
@@ -121,23 +114,27 @@ def tile_list_burial_isotope_mobility_kernel(
 
         def w4_of(i, a):
             if i < PACK:
-                return w4_dealt[:, i, a, :]
-            return w4_raw[1][:, a, 64 * (i - PACK) : 64 * (i - PACK + 1)]
+                return w4_raw[0][:, a, 64 * i : 64 * (i + 1)]
+            return w4_dealt[:, i - PACK, a, :]
 
         w2_raw = [
             shared.tile([P, PACK, N], F32, name="w2_raw0", align_bytes=64, offset=PICKED_AT + S - 64),
             shared.tile([P, PACK, N], F32, name="w2_raw1", align_bytes=64, offset=TABLE1_AT + 64 - 8192),
         ]
-        for e in range(4):
-            nc.sync.dma_start(w2_raw[0][e:P:4, :, :], w2[:BANK, :].rearrange("(u t e) n -> e u t n", t=PACK, e=4)[e])
         nc.sync.dma_start(w4_raw[1][:], w4_rows[:, :, H:].bitcast(I32))
-        nc.sync.dma_start(w2_raw[1][:], w2[BANK:, :].rearrange("(p t) n -> p t n", t=PACK))
+        nc.sync.dma_start(w2_raw[0][:], w2[:BANK, :].rearrange("(p t) n -> p t n", t=PACK))
+        for e in range(4):
+            nc.sync.dma_start(w2_raw[1][e:P:4, :, :], w2[BANK:, :].rearrange("(u t e) n -> e u t n", t=PACK, e=4)[e])
+        nc.gpsimd.tensor_copy(
+            w4_dealt[:].bitcast(U32).rearrange("p t a (u e) -> p t a u e", e=2),
+            w4_raw[1][:].bitcast(U32).rearrange("p a (u t e) -> p t a u e", t=PACK, e=2),
+        )
         gain_cols = shared.tile([P, 8], F32, name="gain_cols", align_bytes=64, offset=TABLE1_AT + 192)
         with nc.allow_non_contiguous_dma(reason="gain: one value for each partition and row tile"):
             for e in range(4):
-                nc.sync.dma_start(gain_cols[e:P:4, 0:PACK], gain[:BANK].rearrange("(u t e) -> e u t", t=PACK, e=4)[e])
+                nc.sync.dma_start(gain_cols[e:P:4, 0:PACK], gain[BANK:].rearrange("(u t e) -> e u t", t=PACK, e=4)[e])
         gain_rows = shared.tile([P, BANK], F32, name="gain_rows", align_bytes=64, offset=TABLE1_AT + 256)
-        nc.sync.dma_start(gain_rows[:], gain[BANK:].partition_broadcast(P))
+        nc.sync.dma_start(gain_rows[:], gain[:BANK].partition_broadcast(P))
 
         w2_bf = []
         for b in range(PASSES):
@@ -184,66 +181,65 @@ def tile_list_burial_isotope_mobility_kernel(
 
         sums = {}
 
-        def turn_into_sums(rows, t, c, first, last):
+        def turn_into_sums(row, t, c, first, last):
             nc.tensor.matmul(
-                sums[c][:, P * t : P * (t + 1)], rows[:, t, P * c : P * (c + 1)], ident[:], start=first, stop=last, is_transpose=True
+                sums[c][:, P * t : P * (t + 1)], row[:, P * c : P * (c + 1)], ident[:], start=first, stop=last, is_transpose=True
             )
 
         def pick_soil(i):
             nc.vector.tensor_copy(soil_of(i), h[i][:].indirect(pos_sb[2][:]))
 
         opened = {}
-        first_cols = (slice(0, 512), slice(512, 768), slice(768, 1024))
+        first_cols = [slice(256 * q, 256 * (q + 1)) for q in range(4)]
         for a in range(PASSES):
             for number, cols in enumerate(first_cols):
                 first_product(0, cols, number, a, opened)
-        nc.scalar.copy(h[0][:, first_cols[0]], opened[0, 0][:])
-        nc.vector.tensor_copy(h[0][:, first_cols[1]], opened[0, 512][:])
-        nc.vector.tensor_copy(h[0][:, first_cols[2]], opened[0, 768][:])
+        for q, cols in enumerate(first_cols):
+            if q == 2:
+                nc.vector.tensor_scalar(h[0][:, cols], opened[0, cols.start][:], -1.0, None, ALU.mult)
+            else:
+                nc.scalar.activation(h[0][:, cols], opened[0, cols.start][:], ACT.Copy, scale=-1.0)
         for i in range(TILES):
-            sign = 1.0 if i < PACK else -1.0
+            sign = -1.0 if i < PACK else 1.0
             if i > 0:
                 for half in range(2):
                     cols = slice(BANK * half, BANK * (half + 1))
                     for a in range(PASSES):
-                        first_product(i, cols, 2 * i + half - 4 if i in (4, 5) else (2 * i + half + 1) % 4, a, opened)
-                    if (i, half) == (1, 0):
-                        nc.scalar.activation(h[i][:, cols], opened[i, cols.start][:], ACT.Copy, scale=sign)
-                    else:
-                        nc.vector.tensor_scalar(h[i][:, cols], opened[i, cols.start][:], sign, None, ALU.mult)
+                        first_product(i, cols, 2 * i + half - 4 if i in (4, 5) else (2 * i + half - 2) % 4, a, opened)
+                    nc.vector.tensor_scalar(h[i][:, cols], opened[i, cols.start][:], sign, None, ALU.mult)
             for j in range(2):
                 nc.scalar.activation(
                     tissue(j, i), h[i][:].indirect(pos_sb[j][:]), ACT.Sigmoid, bias=LN5, scale=sign
                 )
-        for i in range(TILES):
+        for i in [0] + list(range(PACK, TILES)) + list(range(1, PACK)):
             pick_soil(i)
         for t in range(PACK):
             for c in range(CHUNKS):
                 if t == 0:
                     sums[c] = bank(c, [P, BANK], "sums")
-                turn_into_sums(soil[1], t, c, t == 0, False)
+                turn_into_sums(soil_of(t), t, c, t == 0, False)
 
         both_first = shared.tile([P, PACK, M], F32, name="both_first", align_bytes=64, offset=TABLE1_AT + 128 - 8192)
         both4 = keep.tile([P, M], F32, name="both4", tag="tissue_first", align_bytes=64)
-        both_last = shared.tile([P, PACK - 1, M], F32, name="both_last", align_bytes=64, offset=SOIL_AT[0] + 64 - 6144)
-        squared = keep.tile([P, PACK, M], F32, name="squared", align_bytes=64)
+        both_last = shared.tile([P, PACK - 1, M], F32, name="both_last", align_bytes=64, offset=SOIL_AT[1] + 64 - 6144)
+        squared = shared.tile([P, PACK, M], F32, name="squared", align_bytes=64, offset=SOIL_AT[1] + 64 + 4096)
 
         def pair_product(pair):
             rows = slice(2 * pair, 2 * pair + 2)
             nc.gpsimd.tensor_tensor(both_first[:, rows], tissue_first[:, 0, rows], tissue_first[:, 1, rows], ALU.mult)
 
         def scale_soil(t):
-            nc.gpsimd.tensor_scalar(scaled[:, t, :], soil_of(t), 0.25, gain_cols[:, t : t + 1], ALU.add, ALU.mult)
+            nc.gpsimd.tensor_scalar(scaled[:, t, :], soil_of(PACK + t), 0.25, gain_cols[:, t : t + 1], ALU.add, ALU.mult)
 
         pair_product(0)
-        scale_soil(0)
         pair_product(1)
+        scale_soil(0)
         scale_soil(1)
-        scale_soil(2)
         nc.gpsimd.tensor_tensor(both4[:], tissue(0, PACK), tissue(1, PACK), ALU.mult)
+        scale_soil(2)
         scale_soil(3)
 
-        w2_codes = shared.tile([P, PASSES, N], U32, name="w2_codes", align_bytes=64, offset=SOIL_AT[0] + 8192 - 64)
+        w2_codes = shared.tile([P, PASSES, N], U32, name="w2_codes", align_bytes=64, offset=SOIL_AT[1] + 64)
         w2_scale = keep.tile([P, PASSES, N], U8, name="w2_scale", align_bytes=64)
         for b in range(PASSES):
             nc.vector.quantize_mx(
@@ -255,47 +251,57 @@ def tile_list_burial_isotope_mobility_kernel(
         def product(i):
             nc.vector.tensor_tensor(both_last[:, i - 5], tissue(0, i), tissue(1, i), ALU.mult)
 
-        def square(i):
-            row = both4[:] if i == PACK else both_last[:, i - 5]
-            nc.vector.scalar_tensor_tensor(squared[:, i - PACK], row, -3.125, row, ALU.add, ALU.mult)
-
-        square(4)
+        nc.vector.scalar_tensor_tensor(squared[:], both_first[:], -3.125, both_first[:], ALU.add, ALU.mult)
+        ahead = shared.tile([P, 2, 2 * P], F32, name="ahead", align_bytes=64, offset=TABLE1_AT + 128 - 2048)
         product(5)
         product(6)
-        square(5)
+        for t, row in enumerate((both4[:, HALVES[0]], both_last[:, 0, HALVES[0]])):
+            nc.vector.scalar_tensor_tensor(ahead[:, t], row, -3.125, row, ALU.add, ALU.mult)
         product(7)
-        square(6)
-        square(7)
 
         roots = shared.tile([P, PASSES, PACK, M], F32, name="roots", align_bytes=64, offset=H7_AT + 4096 - 64)
         term, inverse = roots[:, 0], roots[:, 1]
         z_bf = keep.tile([P, M * PACK], BF16, name="z_bf", tag="tab_sb0", align_bytes=64)
+        z_wide = keep.tile([P, PACK, M], F32, name="z_wide", align_bytes=64)
         z_codes = keep.tile([P, PASSES, M], U32, name="z_codes", align_bytes=64)
         z_scale = keep.tile([P, PASSES, M], U8, name="z_scale", align_bytes=64)
         z_rows = keep.tile([P, CHUNKS, BANK], BF16, name="z_rows", align_bytes=64)
         z_words = [keep.tile([P, 2, P, 2], F32, name="z_words%d" % half, align_bytes=64) for half in range(2)]
 
-        def root(pair, cols):
-            rows = slice(2 * pair, 2 * pair + 2)
-            nc.scalar.activation(term[:, rows, cols], both_first[:, rows, cols], ACT.Abs_reciprocal_sqrt, bias=4.0, scale=-2.56)
+        def root(cols):
+            if cols == HALVES[0]:
+                nc.scalar.activation(term[:, :2, cols], ahead[:], ACT.Abs_reciprocal_sqrt, bias=16.0, scale=6.5536)
+                rooted = slice(2, PACK)
+            else:
+                nc.scalar.activation(term[:, 0, cols], both4[:, cols], ACT.Abs_reciprocal_sqrt, bias=4.0, scale=-2.56)
+                rooted = slice(1, PACK)
+            nc.scalar.activation(
+                term[:, rooted, cols],
+                both_last[:, rooted.start - 1 :, cols],
+                ACT.Abs_reciprocal_sqrt,
+                bias=4.0,
+                scale=-2.56,
+            )
+            for rows in (slice(0, 2), slice(2, 4)):
+                if cols != HALVES[0] or rows.start:
+                    nc.scalar.activation(term[:, rows, cols], term[:, rows, cols], ACT.Square)
 
         def times_gain(t, cols):
-            row = term[:, t, cols]
-            nc.vector.scalar_tensor_tensor(row, row, gain_cols[:, t : t + 1], row, ALU.mult, ALU.mult)
+            nc.vector.scalar_tensor_tensor(
+                z_wide[:, t, cols], term[:, t, cols], gain_cols[:, t : t + 1], scaled[:, t, cols], ALU.mult, ALU.subtract
+            )
 
         def weave(cols):
-            nc.vector.tensor_tensor(
+            nc.vector.tensor_copy(
                 z_bf[:, PACK * cols.start : PACK * cols.stop].rearrange("p (g i t) -> p g t i", i=4, t=PACK),
-                term[:, :, cols].rearrange("p t (g i) -> p g t i", i=4),
-                scaled[:, :, cols].rearrange("p t (g i) -> p g t i", i=4),
-                ALU.subtract,
+                z_wide[:, :, cols].rearrange("p t (g i) -> p g t i", i=4),
             )
 
         def invert(c):
             cols = slice(P * c, P * (c + 1))
             nc.scalar.activation(inverse[:, :, cols], squared[:, :, cols], ACT.Abs_reciprocal_sqrt, bias=16.0, scale=6.5536)
             for t in range(PACK):
-                turn_into_sums(inverse, t, c, False, t == PACK - 1)
+                turn_into_sums(inverse[:, t], t, c, False, t == PACK - 1)
 
         def scale_by_gain(c):
             nc.vector.scalar_tensor_tensor(z_rows[:, c], sums[c][:], -0.25, gain_rows[:], ALU.add, ALU.mult)
@@ -309,15 +315,15 @@ def tile_list_burial_isotope_mobility_kernel(
 
         def quantize_woven(cols):
             nc.vector.quantize_mx(
-                out=z_codes[:, 0, cols].bitcast(FP8X4),
-                scales=z_scale[:, 0, cols],
+                out=z_codes[:, 1, cols].bitcast(FP8X4),
+                scales=z_scale[:, 1, cols],
                 in_=z_bf[:, PACK * cols.start : PACK * cols.stop],
             )
 
         def quantize_turned(half):
             nc.vector.quantize_mx(
-                out=z_codes[:, 1, HALVES[half]].bitcast(FP8X4),
-                scales=z_scale[:, 1, HALVES[half]],
+                out=z_codes[:, 0, HALVES[half]].bitcast(FP8X4),
+                scales=z_scale[:, 0, HALVES[half]],
                 in_=z_words[half][:].rearrange("p c m u -> p (c m u)").bitcast(BF16),
             )
 
@@ -341,35 +347,30 @@ def tile_list_burial_isotope_mobility_kernel(
             copy_out(result[:], acc[:])
             nc.sync.dma_start(out[P * first_row : P * (first_row + 2), cols].rearrange("(j p) m -> p j m", p=P), result[:])
 
-        for pair in range(2):
-            root(pair, HALVES[0])
-            for t in (2 * pair, 2 * pair + 1):
-                times_gain(t, HALVES[0])
-        weave(HALVES[0])
         for c in range(CHUNKS):
             invert(c)
-        for c in range(2):
+        root(HALVES[0])
+        for c in range(CHUNKS):
             scale_by_gain(c)
-        quantize_woven(HALVES[0])
-        for pair in range(2):
-            root(pair, HALVES[1])
         for c in range(2):
             turn_back(c)
-        scale_by_gain(2)
-        quantize_turned(0)
-        scale_by_gain(3)
+        root(HALVES[1])
         for c in range(2, CHUNKS):
             turn_back(c)
-        for first_row in (0, 2):
-            multiply_and_store(0, first_row, (0, 1), nc.scalar.copy)
         for t in range(PACK):
+            times_gain(t, HALVES[0])
+        quantize_turned(0)
+        weave(HALVES[0])
+        times_gain(0, HALVES[1])
+        quantize_woven(HALVES[0])
+        for t in range(1, PACK):
             times_gain(t, HALVES[1])
         weave(PIECES[1])
         quantize_turned(1)
         weave(PIECES[2])
         quantize_woven(PIECES[1])
         quantize_woven(PIECES[2])
-        for piece in (1, 2):
+        for piece in range(3):
             for first_row in (0, 2):
                 last = piece == 2 and first_row == 2
-                multiply_and_store(piece, first_row, (1, 0), nc.vector.tensor_copy if last else nc.scalar.copy)
+                multiply_and_store(piece, first_row, (0, 1), nc.vector.tensor_copy if last else nc.scalar.copy)

@@ -138,9 +138,7 @@ def tile_list_burial_isotope_mobility_kernel(
 
         w2_bf = []
         for b in range(PASSES):
-            w2_bf.append(
-                shared.tile([P, N, PACK], BF16, name="w2_bf%d" % b, align_bytes=64, offset=H7_AT + 20352 + 4096 * (1 - b))
-            )
+            w2_bf.append(keep.tile([P, N, PACK], BF16, name="w2_bf%d" % b, align_bytes=64))
             nc.gpsimd.tensor_scalar(w2_bf[b][:], w2_raw[b][:].rearrange("p t n -> p n t"), 1.0, 0.0, ALU.mult, ALU.add)
 
         h = [keep.tile([P, S], F32, name="h%d" % i, align_bytes=64) for i in range(TILES - 1)]
@@ -220,44 +218,40 @@ def tile_list_burial_isotope_mobility_kernel(
                 turn_into_sums(soil_of(t), t, c, t == 0, False)
 
         both_first = shared.tile([P, PACK, M], F32, name="both_first", align_bytes=64, offset=TABLE1_AT + 128 - 8192)
-        both4 = keep.tile([P, M], F32, name="both4", tag="tissue_first", align_bytes=64)
-        both_last = shared.tile([P, PACK - 1, M], F32, name="both_last", align_bytes=64, offset=SOIL_AT[1] + 64 - 6144)
+        both_last = shared.tile([P, PACK, M], F32, name="both_last", align_bytes=64, offset=SOIL_AT[1] + 64 - 8192)
         squared = shared.tile([P, PACK, M], F32, name="squared", align_bytes=64, offset=SOIL_AT[1] + 64 + 4096)
 
         def pair_product(pair):
             rows = slice(2 * pair, 2 * pair + 2)
             nc.gpsimd.tensor_tensor(both_first[:, rows], tissue_first[:, 0, rows], tissue_first[:, 1, rows], ALU.mult)
 
-        def scale_soil(t):
-            nc.gpsimd.tensor_scalar(scaled[:, t, :], soil_of(PACK + t), 0.25, gain_cols[:, t : t + 1], ALU.add, ALU.mult)
+        def scale_soil(t, engine):
+            engine.tensor_scalar(scaled[:, t, :], soil_of(PACK + t), 0.25, gain_cols[:, t : t + 1], ALU.add, ALU.mult)
 
         pair_product(0)
         pair_product(1)
-        scale_soil(0)
-        scale_soil(1)
-        nc.gpsimd.tensor_tensor(both4[:], tissue(0, PACK), tissue(1, PACK), ALU.mult)
-        scale_soil(2)
-        scale_soil(3)
+        for t in range(PACK):
+            scale_soil(t, nc.gpsimd if t < 2 else nc.vector)
 
         w2_codes = shared.tile([P, PASSES, N], U32, name="w2_codes", align_bytes=64, offset=SOIL_AT[1] + 64)
         w2_scale = keep.tile([P, PASSES, N], U8, name="w2_scale", align_bytes=64)
+
+        def product(i):
+            nc.vector.tensor_tensor(both_last[:, i - PACK], tissue(0, i), tissue(1, i), ALU.mult)
+
+        nc.vector.scalar_tensor_tensor(squared[:], both_first[:], -3.125, both_first[:], ALU.add, ALU.mult)
+        ahead = shared.tile([P, 2, 2 * P], F32, name="ahead", align_bytes=64, offset=TABLE1_AT + 128 - 2048)
+        for i in range(PACK, TILES - 1):
+            product(i)
+        rows = both_last[:, :2, HALVES[0]]
+        nc.vector.scalar_tensor_tensor(ahead[:], rows, -3.125, rows, ALU.add, ALU.mult)
+        product(TILES - 1)
         for b in range(PASSES):
             nc.vector.quantize_mx(
                 out=w2_codes[:, b, :].bitcast(FP8X4),
                 scales=w2_scale[:, b, :],
                 in_=w2_bf[b][:].rearrange("p n t -> p (n t)"),
             )
-
-        def product(i):
-            nc.vector.tensor_tensor(both_last[:, i - 5], tissue(0, i), tissue(1, i), ALU.mult)
-
-        nc.vector.scalar_tensor_tensor(squared[:], both_first[:], -3.125, both_first[:], ALU.add, ALU.mult)
-        ahead = shared.tile([P, 2, 2 * P], F32, name="ahead", align_bytes=64, offset=TABLE1_AT + 128 - 2048)
-        product(5)
-        product(6)
-        for t, row in enumerate((both4[:, HALVES[0]], both_last[:, 0, HALVES[0]])):
-            nc.vector.scalar_tensor_tensor(ahead[:, t], row, -3.125, row, ALU.add, ALU.mult)
-        product(7)
 
         roots = shared.tile([P, PASSES, PACK, M], F32, name="roots", align_bytes=64, offset=H7_AT + 4096 - 64)
         term, inverse = roots[:, 0], roots[:, 1]
@@ -269,22 +263,14 @@ def tile_list_burial_isotope_mobility_kernel(
         z_words = [keep.tile([P, 2, P, 2], F32, name="z_words%d" % half, align_bytes=64) for half in range(2)]
 
         def root(cols):
-            if cols == HALVES[0]:
-                nc.scalar.activation(term[:, :2, cols], ahead[:], ACT.Abs_reciprocal_sqrt, bias=16.0, scale=6.5536)
-                rooted = slice(2, PACK)
-            else:
-                nc.scalar.activation(term[:, 0, cols], both4[:, cols], ACT.Abs_reciprocal_sqrt, bias=4.0, scale=-2.56)
-                rooted = slice(1, PACK)
-            nc.scalar.activation(
-                term[:, rooted, cols],
-                both_last[:, rooted.start - 1 :, cols],
-                ACT.Abs_reciprocal_sqrt,
-                bias=4.0,
-                scale=-2.56,
-            )
             for rows in (slice(0, 2), slice(2, 4)):
-                if cols != HALVES[0] or rows.start:
-                    nc.scalar.activation(term[:, rows, cols], term[:, rows, cols], ACT.Square)
+                if cols == HALVES[0] and rows.start == 0:
+                    nc.scalar.activation(term[:, rows, cols], ahead[:], ACT.Abs_reciprocal_sqrt, bias=16.0, scale=6.5536)
+                    continue
+                nc.scalar.activation(
+                    term[:, rows, cols], both_last[:, rows, cols], ACT.Abs_reciprocal_sqrt, bias=4.0, scale=-2.56
+                )
+                nc.scalar.activation(term[:, rows, cols], term[:, rows, cols], ACT.Square)
 
         def times_gain(t, cols):
             nc.vector.scalar_tensor_tensor(

@@ -28,10 +28,10 @@ HALVES = (slice(0, 256), slice(256, 512))
 PIECES = (slice(0, 256), slice(256, 384), slice(384, 512))
 CHUNKS = M // P
 
-PICKED_AT = 1984
-TABLE1_AT = 19264
-H7_AT = 27456
-SOIL_AT = (74560, 62208)
+PICKED_AT = 3520
+TABLE1_AT = 20800
+H7_AT = 28992
+SOIL_AT = (69952, 57600)
 
 
 def tile_list_burial_isotope_mobility_kernel(
@@ -55,10 +55,8 @@ def tile_list_burial_isotope_mobility_kernel(
             shared.tile([P, T], I32, name="tab_sb1", align_bytes=64, offset=TABLE1_AT),
         ]
         w4_rows = w4_words.rearrange("a p c -> p a c")
-        w4_raw = [
-            keep.tile([P, PASSES, H // 4], I32, name="w4_raw0", align_bytes=64),
-            shared.tile([P, PASSES, H // 4], I32, name="w4_raw1", align_bytes=64, offset=PICKED_AT + 64 - 2048),
-        ]
+        w4_first = keep.tile([P, PASSES, 64], I32, name="w4_first", align_bytes=64)
+        w4_rest = shared.tile([P, PASSES, 64 * (TILES - 1)], I32, name="w4_rest", align_bytes=64, offset=PICKED_AT + 64 - 3584)
         planes = [keep.tile([P, S + H], U8, name="planes%d" % a, align_bytes=64) for a in range(PASSES)]
 
         nc.sync.dma_start(offs_sb[:], offs)
@@ -67,7 +65,7 @@ def tile_list_burial_isotope_mobility_kernel(
         )
         nc.sync.dma_start(w4_scale_rows[:].bitcast(I32), w4_scales.rearrange("a q c -> (a q) c").bitcast(I32))
         nc.sync.dma_start(tab_sb[0][:], tab_words[0].rearrange("p t i -> p (t i)").bitcast(I32))
-        nc.sync.dma_start(w4_raw[0][:], w4_rows[:, :, :H].bitcast(I32))
+        nc.sync.dma_start(w4_first[:], w4_rows[:, :, : 2 * P].bitcast(I32))
         for j, pos in enumerate((pos1, pos2, pos3)):
             nc.sync.dma_start(pos_sb[j][:], pos)
         nc.sync.dma_start(tab_sb[1][:], tab_words[1].rearrange("p t i -> p (t i)").bitcast(I32))
@@ -113,21 +111,23 @@ def tile_list_burial_isotope_mobility_kernel(
         pick_words(1, 768, 1024)
 
         def w4_of(i, a):
+            if i == 0:
+                return w4_first[:, a, :]
             if i < PACK:
-                return w4_raw[0][:, a, 64 * i : 64 * (i + 1)]
+                return w4_rest[:, a, 64 * (i - 1) : 64 * i]
             return w4_dealt[:, i - PACK, a, :]
 
         w2_raw = [
             shared.tile([P, PACK, N], F32, name="w2_raw0", align_bytes=64, offset=PICKED_AT + S - 64),
             shared.tile([P, PACK, N], F32, name="w2_raw1", align_bytes=64, offset=TABLE1_AT + 64 - 8192),
         ]
-        nc.sync.dma_start(w4_raw[1][:], w4_rows[:, :, H:].bitcast(I32))
+        nc.sync.dma_start(w4_rest[:], w4_rows[:, :, 2 * P :].bitcast(I32))
         nc.sync.dma_start(w2_raw[0][:], w2[:BANK, :].rearrange("(p t) n -> p t n", t=PACK))
         for e in range(4):
             nc.sync.dma_start(w2_raw[1][e:P:4, :, :], w2[BANK:, :].rearrange("(u t e) n -> e u t n", t=PACK, e=4)[e])
         nc.gpsimd.tensor_copy(
             w4_dealt[:].bitcast(U32).rearrange("p t a (u e) -> p t a u e", e=2),
-            w4_raw[1][:].bitcast(U32).rearrange("p a (u t e) -> p t a u e", t=PACK, e=2),
+            w4_rest[:, :, 64 * (PACK - 1) :].bitcast(U32).rearrange("p a (u t e) -> p t a u e", t=PACK, e=2),
         )
         gain_cols = shared.tile([P, 8], F32, name="gain_cols", align_bytes=64, offset=TABLE1_AT + 192)
         with nc.allow_non_contiguous_dma(reason="gain: one value for each partition and row tile"):
@@ -231,7 +231,7 @@ def tile_list_burial_isotope_mobility_kernel(
         pair_product(0)
         pair_product(1)
         for t in range(PACK):
-            scale_soil(t, nc.gpsimd if t < 2 else nc.vector)
+            scale_soil(t, nc.gpsimd)
 
         w2_codes = shared.tile([P, PASSES, N], U32, name="w2_codes", align_bytes=64, offset=SOIL_AT[1] + 64)
         w2_scale = keep.tile([P, PASSES, N], U8, name="w2_scale", align_bytes=64)
@@ -240,10 +240,10 @@ def tile_list_burial_isotope_mobility_kernel(
             nc.vector.tensor_tensor(both_last[:, i - PACK], tissue(0, i), tissue(1, i), ALU.mult)
 
         nc.vector.scalar_tensor_tensor(squared[:], both_first[:], -3.125, both_first[:], ALU.add, ALU.mult)
-        ahead = shared.tile([P, 2, 2 * P], F32, name="ahead", align_bytes=64, offset=TABLE1_AT + 128 - 2048)
+        ahead = shared.tile([P, 2, M], F32, name="ahead", align_bytes=64, offset=TABLE1_AT + 128 - 4096)
         for i in range(PACK, TILES - 1):
             product(i)
-        rows = both_last[:, :2, HALVES[0]]
+        rows = both_last[:, :2]
         nc.vector.scalar_tensor_tensor(ahead[:], rows, -3.125, rows, ALU.add, ALU.mult)
         product(TILES - 1)
         for b in range(PASSES):
@@ -260,12 +260,16 @@ def tile_list_burial_isotope_mobility_kernel(
         z_codes = keep.tile([P, PASSES, M], U32, name="z_codes", align_bytes=64)
         z_scale = keep.tile([P, PASSES, M], U8, name="z_scale", align_bytes=64)
         z_rows = keep.tile([P, CHUNKS, BANK], BF16, name="z_rows", align_bytes=64)
-        z_words = [keep.tile([P, 2, P, 2], F32, name="z_words%d" % half, align_bytes=64) for half in range(2)]
+        z_words = [
+            keep.tile([P, cols.stop - cols.start, 2], F32, name="z_words%d" % cols.start, align_bytes=64) for cols in PIECES
+        ]
 
         def root(cols):
             for rows in (slice(0, 2), slice(2, 4)):
-                if cols == HALVES[0] and rows.start == 0:
-                    nc.scalar.activation(term[:, rows, cols], ahead[:], ACT.Abs_reciprocal_sqrt, bias=16.0, scale=6.5536)
+                if rows.start == 0:
+                    nc.scalar.activation(
+                        term[:, rows, cols], ahead[:, :, cols], ACT.Abs_reciprocal_sqrt, bias=16.0, scale=6.5536
+                    )
                     continue
                 nc.scalar.activation(
                     term[:, rows, cols], both_last[:, rows, cols], ACT.Abs_reciprocal_sqrt, bias=4.0, scale=-2.56
@@ -297,7 +301,8 @@ def tile_list_burial_isotope_mobility_kernel(
             words = z_rows[:, c].bitcast(F32)
             for u in range(2):
                 nc.tensor.transpose(turned[:, u, :], words[:, u : 2 * P : 2], ident[:])
-            nc.scalar.copy(z_words[c // 2][:, c % 2], turned[:].rearrange("p u m -> p m u"))
+            words_out = z_words[0][:, P * c : P * (c + 1)] if c < 2 else z_words[c - 1][:]
+            nc.scalar.copy(words_out, turned[:].rearrange("p u m -> p m u"))
 
         def quantize_woven(cols):
             nc.vector.quantize_mx(
@@ -306,11 +311,12 @@ def tile_list_burial_isotope_mobility_kernel(
                 in_=z_bf[:, PACK * cols.start : PACK * cols.stop],
             )
 
-        def quantize_turned(half):
+        def quantize_turned(piece):
+            cols = PIECES[piece]
             nc.vector.quantize_mx(
-                out=z_codes[:, 0, HALVES[half]].bitcast(FP8X4),
-                scales=z_scale[:, 0, HALVES[half]],
-                in_=z_words[half][:].rearrange("p c m u -> p (c m u)").bitcast(BF16),
+                out=z_codes[:, 0, cols].bitcast(FP8X4),
+                scales=z_scale[:, 0, cols],
+                in_=z_words[piece][:].rearrange("p m u -> p (m u)").bitcast(BF16),
             )
 
         def multiply_and_store(piece, first_row, order, copy_out):
@@ -336,27 +342,33 @@ def tile_list_burial_isotope_mobility_kernel(
         for c in range(CHUNKS):
             invert(c)
         root(HALVES[0])
-        for c in range(CHUNKS):
-            scale_by_gain(c)
         for c in range(2):
+            scale_by_gain(c)
             turn_back(c)
         root(HALVES[1])
-        for c in range(2, CHUNKS):
-            turn_back(c)
         for t in range(PACK):
             times_gain(t, HALVES[0])
         quantize_turned(0)
         weave(HALVES[0])
-        times_gain(0, HALVES[1])
+        scale_by_gain(2)
         quantize_woven(HALVES[0])
-        for t in range(1, PACK):
-            times_gain(t, HALVES[1])
+        scale_by_gain(3)
+        turn_back(2)
+        for first_row in (0, 2):
+            multiply_and_store(0, first_row, (0, 1), nc.scalar.copy)
+        turn_back(3)
+        for t in range(PACK):
+            times_gain(t, PIECES[1])
+        times_gain(0, PIECES[2])
         weave(PIECES[1])
         quantize_turned(1)
-        weave(PIECES[2])
         quantize_woven(PIECES[1])
+        for t in range(1, PACK):
+            times_gain(t, PIECES[2])
+        quantize_turned(2)
+        weave(PIECES[2])
         quantize_woven(PIECES[2])
-        for piece in range(3):
+        for piece in (1, 2):
             for first_row in (0, 2):
                 last = piece == 2 and first_row == 2
                 multiply_and_store(piece, first_row, (0, 1), nc.vector.tensor_copy if last else nc.scalar.copy)

@@ -155,12 +155,18 @@ def tile_list_burial_isotope_mobility_kernel(
             return tissue_last[:, j, i - PACK - 1, :]
 
         soil = [
-            shared.tile([P, PACK, M], F32, name="soil%d" % b, align_bytes=64, offset=SOIL_AT[b]) for b in range(PASSES)
+            shared.tile([P, PACK - 1, M], F32, name="soil%d" % b, align_bytes=64, offset=SOIL_AT[b] + 2048 * (1 - b))
+            for b in range(PASSES)
         ]
         soil_first = keep.tile([P, M], F32, name="soil_first", align_bytes=64)
+        soil_last = shared.tile([P, M], F32, name="soil_last", align_bytes=64, offset=SOIL_AT[0])
 
         def soil_of(i):
-            return soil_first[:] if i == 0 else soil[i // PACK][:, i % PACK, :]
+            if i == 0:
+                return soil_first[:]
+            if i == TILES - 1:
+                return soil_last[:]
+            return soil[i // PACK][:, (i - 1) % PACK if i < PACK else i % PACK, :]
 
         scaled = shared.tile([P, PACK, M], F32, name="scaled", align_bytes=64, offset=TABLE1_AT + 128 - 16384)
 
@@ -231,7 +237,7 @@ def tile_list_burial_isotope_mobility_kernel(
         pair_product(0)
         pair_product(1)
         for t in range(PACK):
-            scale_soil(t, nc.gpsimd)
+            scale_soil(t, nc.gpsimd if t < PACK - 1 else nc.vector)
 
         w2_codes = shared.tile([P, PASSES, N], U32, name="w2_codes", align_bytes=64, offset=SOIL_AT[1] + 64)
         w2_scale = keep.tile([P, PASSES, N], U8, name="w2_scale", align_bytes=64)

@@ -30,8 +30,8 @@ CHUNKS = M // P
 
 PICKED_AT = 3520
 TABLE1_AT = 20800
-H7_AT = 28992
-SOIL_AT = (69952, 57600)
+WORDS_AT = (36864, 40960)
+ROOTS_AT = 57344
 
 
 def tile_list_burial_isotope_mobility_kernel(
@@ -95,7 +95,7 @@ def tile_list_burial_isotope_mobility_kernel(
             nc.sync.dma_start(planes[1][r:P:32, :].bitcast(I32), planes[0][16 + r : 32 : 4, :].bitcast(I32))
 
         v_words = [
-            shared.tile([P, S], U32, name="v_words%d" % a, align_bytes=64, offset=SOIL_AT[a]) for a in range(PASSES)
+            shared.tile([P, S], U32, name="v_words%d" % a, align_bytes=64, offset=WORDS_AT[a]) for a in range(PASSES)
         ]
 
         def pick_words(a, start, stop):
@@ -123,16 +123,23 @@ def tile_list_burial_isotope_mobility_kernel(
         ]
         nc.sync.dma_start(w4_rest[:], w4_rows[:, :, 2 * P :].bitcast(I32))
         nc.sync.dma_start(w2_raw[0][:], w2[:BANK, :].rearrange("(p t) n -> p t n", t=PACK))
+        gain_cols = shared.tile([P, 8], F32, name="gain_cols", align_bytes=64, offset=PICKED_AT + 128)
+        with nc.allow_non_contiguous_dma(reason="gain: one value for each partition and row tile"):
+            for e in range(4):
+                nc.sync.dma_start(gain_cols[e:P:4, 0:PACK], gain[BANK:].rearrange("(u t e) -> e u t", t=PACK, e=4)[e])
         for e in range(4):
             nc.sync.dma_start(w2_raw[1][e:P:4, :, :], w2[BANK:, :].rearrange("(u t e) n -> e u t n", t=PACK, e=4)[e])
         nc.gpsimd.tensor_copy(
             w4_dealt[:].bitcast(U32).rearrange("p t a (u e) -> p t a u e", e=2),
             w4_rest[:, :, 64 * (PACK - 1) :].bitcast(U32).rearrange("p a (u t e) -> p t a u e", t=PACK, e=2),
         )
-        gain_cols = shared.tile([P, 8], F32, name="gain_cols", align_bytes=64, offset=TABLE1_AT + 192)
-        with nc.allow_non_contiguous_dma(reason="gain: one value for each partition and row tile"):
-            for e in range(4):
-                nc.sync.dma_start(gain_cols[e:P:4, 0:PACK], gain[BANK:].rearrange("(u t e) -> e u t", t=PACK, e=4)[e])
+        neg_gain = keep.tile([P, PACK], F32, name="neg_gain", align_bytes=64)
+        is_zero = keep.tile([P, PACK], F32, name="is_zero", align_bytes=64)
+        divisor = keep.tile([P, PACK], F32, name="divisor", align_bytes=64)
+        undo_gain = shared.tile([P, PACK], F32, name="undo_gain", align_bytes=64, offset=ROOTS_AT)
+        nc.gpsimd.tensor_scalar(is_zero[:], gain_cols[:, 0:PACK], 0.0, None, ALU.is_equal)
+        nc.gpsimd.tensor_scalar(neg_gain[:], gain_cols[:, 0:PACK], -1.0, 0.0, ALU.mult, ALU.add)
+        nc.gpsimd.tensor_tensor(divisor[:], is_zero[:], gain_cols[:, 0:PACK], ALU.subtract)
         gain_rows = shared.tile([P, BANK], F32, name="gain_rows", align_bytes=64, offset=TABLE1_AT + 256)
         nc.sync.dma_start(gain_rows[:], gain[:BANK].partition_broadcast(P))
 
@@ -141,34 +148,22 @@ def tile_list_burial_isotope_mobility_kernel(
             w2_bf.append(keep.tile([P, N, PACK], BF16, name="w2_bf%d" % b, align_bytes=64))
             nc.gpsimd.tensor_scalar(w2_bf[b][:], w2_raw[b][:].rearrange("p t n -> p n t"), 1.0, 0.0, ALU.mult, ALU.add)
 
-        h = [keep.tile([P, S], F32, name="h%d" % i, align_bytes=64) for i in range(TILES - 1)]
-        h.append(shared.tile([P, S], F32, name="h7", align_bytes=64, offset=H7_AT))
-        tissue_first = keep.tile([P, 2, PACK, M], F32, name="tissue_first", tag="tissue_first", align_bytes=64)
-        tissue4 = keep.tile([P, 2, M], F32, name="tissue4", align_bytes=64)
-        tissue_last = keep.tile([P, 2, PACK - 1, M], F32, name="tissue_last", align_bytes=64)
+        h = [keep.tile([P, S], F32, name="h%d" % i, align_bytes=64) for i in range(TILES)]
+        tissue_first = keep.tile([P, 2, PACK, M], F32, name="tissue_first", align_bytes=64)
+        tissue_last = [keep.tile([P, 2, M], F32, name="tissue%d" % i, align_bytes=64) for i in range(PACK, TILES)]
 
         def tissue(j, i):
             if i < PACK:
                 return tissue_first[:, j, i, :]
-            if i == PACK:
-                return tissue4[:, j, :]
-            return tissue_last[:, j, i - PACK - 1, :]
+            return tissue_last[i - PACK][:, j, :]
 
-        soil = [
-            shared.tile([P, PACK - 1, M], F32, name="soil%d" % b, align_bytes=64, offset=SOIL_AT[b] + 2048 * (1 - b))
-            for b in range(PASSES)
-        ]
         soil_first = keep.tile([P, M], F32, name="soil_first", align_bytes=64)
-        soil_last = shared.tile([P, M], F32, name="soil_last", align_bytes=64, offset=SOIL_AT[0])
+        soil_rest = shared.tile([P, PACK + 2, M], F32, name="soil_rest", align_bytes=64, offset=WORDS_AT[0] + 64 - 12288)
 
         def soil_of(i):
             if i == 0:
                 return soil_first[:]
-            if i == TILES - 1:
-                return soil_last[:]
-            return soil[i // PACK][:, (i - 1) % PACK if i < PACK else i % PACK, :]
-
-        scaled = shared.tile([P, PACK, M], F32, name="scaled", align_bytes=64, offset=TABLE1_AT + 128 - 16384)
+            return soil_rest[:, i - 1, :]
 
         def first_product(i, cols, number, a, opened):
             if a == 0:
@@ -204,18 +199,31 @@ def tile_list_burial_isotope_mobility_kernel(
             else:
                 nc.scalar.activation(h[0][:, cols], opened[0, cols.start][:], ACT.Copy, scale=-1.0)
         for i in range(TILES):
-            sign = -1.0 if i < PACK else 1.0
+            if i == PACK:
+                nc.vector.reciprocal(undo_gain[:], divisor[:])
             if i > 0:
                 for half in range(2):
                     cols = slice(BANK * half, BANK * (half + 1))
                     for a in range(PASSES):
                         first_product(i, cols, 2 * i + half - 4 if i in (4, 5) else (2 * i + half - 2) % 4, a, opened)
-                    nc.vector.tensor_scalar(h[i][:, cols], opened[i, cols.start][:], sign, None, ALU.mult)
+                    if i < PACK:
+                        nc.vector.tensor_scalar(h[i][:, cols], opened[i, cols.start][:], -1.0, None, ALU.mult)
+                    else:
+                        nc.vector.tensor_scalar(
+                            h[i][:, cols], opened[i, cols.start][:], 0.25, neg_gain[:, i - PACK : i - PACK + 1], ALU.add, ALU.mult
+                        )
             for j in range(2):
-                nc.scalar.activation(
-                    tissue(j, i), h[i][:].indirect(pos_sb[j][:]), ACT.Sigmoid, bias=LN5, scale=sign
-                )
-        for i in [0] + list(range(PACK, TILES)) + list(range(1, PACK)):
+                if i < PACK:
+                    nc.scalar.activation(tissue(j, i), h[i][:].indirect(pos_sb[j][:]), ACT.Sigmoid, bias=LN5, scale=-1.0)
+                else:
+                    nc.scalar.activation(
+                        tissue(j, i),
+                        h[i][:].indirect(pos_sb[j][:]),
+                        ACT.Sigmoid,
+                        bias=LN5 - 0.25,
+                        scale=undo_gain[:, i - PACK : i - PACK + 1],
+                    )
+        for i in range(PACK + 3):
             pick_soil(i)
         for t in range(PACK):
             for c in range(CHUNKS):
@@ -223,45 +231,36 @@ def tile_list_burial_isotope_mobility_kernel(
                     sums[c] = bank(c, [P, BANK], "sums")
                 turn_into_sums(soil_of(t), t, c, t == 0, False)
 
-        both_first = shared.tile([P, PACK, M], F32, name="both_first", align_bytes=64, offset=TABLE1_AT + 128 - 8192)
-        both_last = shared.tile([P, PACK, M], F32, name="both_last", align_bytes=64, offset=SOIL_AT[1] + 64 - 8192)
-        squared = shared.tile([P, PACK, M], F32, name="squared", align_bytes=64, offset=SOIL_AT[1] + 64 + 4096)
-
-        def pair_product(pair):
-            rows = slice(2 * pair, 2 * pair + 2)
-            nc.gpsimd.tensor_tensor(both_first[:, rows], tissue_first[:, 0, rows], tissue_first[:, 1, rows], ALU.mult)
-
-        def scale_soil(t, engine):
-            engine.tensor_scalar(scaled[:, t, :], soil_of(PACK + t), 0.25, gain_cols[:, t : t + 1], ALU.add, ALU.mult)
-
-        pair_product(0)
-        pair_product(1)
-        for t in range(PACK):
-            scale_soil(t, nc.gpsimd if t < PACK - 1 else nc.vector)
-
-        w2_codes = shared.tile([P, PASSES, N], U32, name="w2_codes", align_bytes=64, offset=SOIL_AT[1] + 64)
+        both_first = shared.tile([P, 2, M], F32, name="both_first", align_bytes=64, offset=WORDS_AT[1] + 4096 - 64)
+        both_pair = shared.tile([P, 2, M], F32, name="both_pair", align_bytes=64, offset=TABLE1_AT + 64 - 8192)
+        both_last = keep.tile([P, PACK, M], F32, name="both_last", align_bytes=64)
+        squared = keep.tile([P, PACK, M], F32, name="squared", align_bytes=64)
+        w2_codes = keep.tile([P, PASSES, N], U32, name="w2_codes", align_bytes=64)
         w2_scale = keep.tile([P, PASSES, N], U8, name="w2_scale", align_bytes=64)
 
         def product(i):
             nc.vector.tensor_tensor(both_last[:, i - PACK], tissue(0, i), tissue(1, i), ALU.mult)
 
-        nc.vector.scalar_tensor_tensor(squared[:], both_first[:], -3.125, both_first[:], ALU.add, ALU.mult)
-        ahead = shared.tile([P, 2, M], F32, name="ahead", align_bytes=64, offset=TABLE1_AT + 128 - 4096)
-        for i in range(PACK, TILES - 1):
-            product(i)
-        rows = both_last[:, :2]
-        nc.vector.scalar_tensor_tensor(ahead[:], rows, -3.125, rows, ALU.add, ALU.mult)
-        product(TILES - 1)
-        for b in range(PASSES):
+        def quantize_w2(b):
             nc.vector.quantize_mx(
                 out=w2_codes[:, b, :].bitcast(FP8X4),
                 scales=w2_scale[:, b, :],
                 in_=w2_bf[b][:].rearrange("p n t -> p (n t)"),
             )
 
-        roots = shared.tile([P, PASSES, PACK, M], F32, name="roots", align_bytes=64, offset=H7_AT + 4096 - 64)
+        nc.gpsimd.tensor_tensor(both_pair[:], tissue_first[:, 0, :2], tissue_first[:, 1, :2], ALU.mult)
+        nc.vector.tensor_tensor(both_first[:], tissue_first[:, 0, 2:], tissue_first[:, 1, 2:], ALU.mult)
+        nc.vector.scalar_tensor_tensor(squared[:, :2], both_pair[:], -3.125, both_pair[:], ALU.add, ALU.mult)
+        nc.vector.scalar_tensor_tensor(squared[:, 2:], both_first[:], -3.125, both_first[:], ALU.add, ALU.mult)
+        for i in range(PACK, TILES):
+            product(i)
+        quantize_w2(0)
+        quantize_w2(1)
+
+        roots = shared.tile([P, PASSES, PACK, M], F32, name="roots", align_bytes=64, offset=ROOTS_AT)
         term, inverse = roots[:, 0], roots[:, 1]
-        z_bf = keep.tile([P, M * PACK], BF16, name="z_bf", tag="tab_sb0", align_bytes=64)
+        gained = keep.tile([P, M], F32, name="gained", align_bytes=64)
+        z_bf = [keep.tile([P, cols.stop - cols.start, PACK], BF16, name="z_bf%d" % cols.start, align_bytes=64) for cols in PIECES]
         z_wide = keep.tile([P, PACK, M], F32, name="z_wide", align_bytes=64)
         z_codes = keep.tile([P, PASSES, M], U32, name="z_codes", align_bytes=64)
         z_scale = keep.tile([P, PASSES, M], U8, name="z_scale", align_bytes=64)
@@ -271,25 +270,29 @@ def tile_list_burial_isotope_mobility_kernel(
         ]
 
         def root(cols):
-            for rows in (slice(0, 2), slice(2, 4)):
-                if rows.start == 0:
-                    nc.scalar.activation(
-                        term[:, rows, cols], ahead[:, :, cols], ACT.Abs_reciprocal_sqrt, bias=16.0, scale=6.5536
-                    )
-                    continue
-                nc.scalar.activation(
-                    term[:, rows, cols], both_last[:, rows, cols], ACT.Abs_reciprocal_sqrt, bias=4.0, scale=-2.56
-                )
-                nc.scalar.activation(term[:, rows, cols], term[:, rows, cols], ACT.Square)
+            nc.scalar.activation(term[:, :, cols], both_last[:, :, cols], ACT.Abs_reciprocal_sqrt, bias=4.0, scale=-2.56)
 
-        def times_gain(t, cols):
+        def square(cols):
+            nc.scalar.activation(term[:, :3, cols], term[:, :3, cols], ACT.Square)
+
+        def square_with_gain(t, cols):
             nc.vector.scalar_tensor_tensor(
-                z_wide[:, t, cols], term[:, t, cols], gain_cols[:, t : t + 1], scaled[:, t, cols], ALU.mult, ALU.subtract
+                gained[:, cols], term[:, t, cols], gain_cols[:, t : t + 1], term[:, t, cols], ALU.mult, ALU.mult
             )
 
-        def weave(cols):
+        def combine(t, cols):
+            if t < 3:
+                nc.vector.scalar_tensor_tensor(
+                    z_wide[:, t, cols], term[:, t, cols], gain_cols[:, t : t + 1], soil_of(PACK + t)[:, cols], ALU.mult, ALU.add
+                )
+            else:
+                picked = h[PACK + t][:].indirect(pos_sb[2][:, cols.start // 16 : cols.stop // 16])
+                nc.vector.tensor_tensor(z_wide[:, t, cols], picked, gained[:, cols], ALU.add)
+
+        def weave(piece):
+            cols = PIECES[piece]
             nc.vector.tensor_copy(
-                z_bf[:, PACK * cols.start : PACK * cols.stop].rearrange("p (g i t) -> p g t i", i=4, t=PACK),
+                z_bf[piece][:].rearrange("p (g i) t -> p g t i", i=4),
                 z_wide[:, :, cols].rearrange("p t (g i) -> p g t i", i=4),
             )
 
@@ -310,11 +313,12 @@ def tile_list_burial_isotope_mobility_kernel(
             words_out = z_words[0][:, P * c : P * (c + 1)] if c < 2 else z_words[c - 1][:]
             nc.scalar.copy(words_out, turned[:].rearrange("p u m -> p m u"))
 
-        def quantize_woven(cols):
+        def quantize_woven(piece):
+            cols = PIECES[piece]
             nc.vector.quantize_mx(
                 out=z_codes[:, 1, cols].bitcast(FP8X4),
                 scales=z_scale[:, 1, cols],
-                in_=z_bf[:, PACK * cols.start : PACK * cols.stop],
+                in_=z_bf[piece][:].rearrange("p m t -> p (m t)"),
             )
 
         def quantize_turned(piece):
@@ -351,29 +355,33 @@ def tile_list_burial_isotope_mobility_kernel(
         for c in range(2):
             scale_by_gain(c)
             turn_back(c)
+        square(HALVES[0])
         root(HALVES[1])
-        for t in range(PACK):
-            times_gain(t, HALVES[0])
-        quantize_turned(0)
-        weave(HALVES[0])
+        square(HALVES[1])
+        square_with_gain(3, HALVES[0])
         scale_by_gain(2)
-        quantize_woven(HALVES[0])
+        for t in (3, 0, 1, 2):
+            combine(t, HALVES[0])
+        quantize_turned(0)
+        weave(0)
         scale_by_gain(3)
+        quantize_woven(0)
         turn_back(2)
         for first_row in (0, 2):
             multiply_and_store(0, first_row, (0, 1), nc.scalar.copy)
         turn_back(3)
+        square_with_gain(3, HALVES[1])
         for t in range(PACK):
-            times_gain(t, PIECES[1])
-        times_gain(0, PIECES[2])
-        weave(PIECES[1])
+            combine(t, PIECES[1])
+        combine(0, PIECES[2])
+        weave(1)
         quantize_turned(1)
-        quantize_woven(PIECES[1])
+        quantize_woven(1)
         for t in range(1, PACK):
-            times_gain(t, PIECES[2])
+            combine(t, PIECES[2])
         quantize_turned(2)
-        weave(PIECES[2])
-        quantize_woven(PIECES[2])
+        weave(2)
+        quantize_woven(2)
         for piece in (1, 2):
             for first_row in (0, 2):
                 last = piece == 2 and first_row == 2

@@ -30,7 +30,7 @@ CHUNKS = M // P
 
 PICKED_AT = 3520
 TABLE1_AT = 20800
-WORDS_AT = (36864, 40960)
+WORDS_AT = (38912, 43008)
 ROOTS_AT = 57344
 
 
@@ -158,7 +158,7 @@ def tile_list_burial_isotope_mobility_kernel(
             return tissue_last[i - PACK][:, j, :]
 
         soil_first = keep.tile([P, M], F32, name="soil_first", align_bytes=64)
-        soil_rest = shared.tile([P, PACK + 2, M], F32, name="soil_rest", align_bytes=64, offset=WORDS_AT[0] + 64 - 12288)
+        soil_rest = shared.tile([P, TILES - 1, M], F32, name="soil_rest", align_bytes=64, offset=WORDS_AT[0] + 64 - 14336)
 
         def soil_of(i):
             if i == 0:
@@ -223,7 +223,7 @@ def tile_list_burial_isotope_mobility_kernel(
                         bias=LN5 - 0.25,
                         scale=undo_gain[:, i - PACK : i - PACK + 1],
                     )
-        for i in range(PACK + 3):
+        for i in range(TILES):
             pick_soil(i)
         for t in range(PACK):
             for c in range(CHUNKS):
@@ -231,15 +231,23 @@ def tile_list_burial_isotope_mobility_kernel(
                     sums[c] = bank(c, [P, BANK], "sums")
                 turn_into_sums(soil_of(t), t, c, t == 0, False)
 
-        both_first = shared.tile([P, 2, M], F32, name="both_first", align_bytes=64, offset=WORDS_AT[1] + 4096 - 64)
-        both_pair = shared.tile([P, 2, M], F32, name="both_pair", align_bytes=64, offset=TABLE1_AT + 64 - 8192)
-        both_last = keep.tile([P, PACK, M], F32, name="both_last", align_bytes=64)
+        both_first = shared.tile([P, PACK, M], F32, name="both_first", align_bytes=64, offset=TABLE1_AT + 128 - 8192)
+        both_mid = shared.tile([P, 2, M], F32, name="both_mid", align_bytes=64, offset=TABLE1_AT + 128 - 8192 - 4096)
+        both_last = [
+            shared.tile([P, M], F32, name="both6", align_bytes=64, offset=TABLE1_AT + 128 - 8192),
+            shared.tile([P, M], F32, name="both7", align_bytes=64, offset=TABLE1_AT + 128 - 8192 - 4096),
+        ]
+        ahead = keep.tile([P, PACK - 1, M], F32, name="ahead", align_bytes=64)
+
+        def both_of(i):
+            return both_mid[:, i - PACK] if i < PACK + 2 else both_last[i - PACK - 2][:]
         squared = keep.tile([P, PACK, M], F32, name="squared", align_bytes=64)
-        w2_codes = keep.tile([P, PASSES, N], U32, name="w2_codes", align_bytes=64)
+        w2_codes = shared.tile([P, PASSES, N], U32, name="w2_codes", align_bytes=64, offset=TABLE1_AT + 128 - 4096)
         w2_scale = keep.tile([P, PASSES, N], U8, name="w2_scale", align_bytes=64)
 
         def product(i):
-            nc.vector.tensor_tensor(both_last[:, i - PACK], tissue(0, i), tissue(1, i), ALU.mult)
+            engine = nc.gpsimd if i < PACK + 2 else nc.vector
+            engine.tensor_tensor(both_of(i), tissue(0, i), tissue(1, i), ALU.mult)
 
         def quantize_w2(b):
             nc.vector.quantize_mx(
@@ -248,18 +256,20 @@ def tile_list_burial_isotope_mobility_kernel(
                 in_=w2_bf[b][:].rearrange("p n t -> p (n t)"),
             )
 
-        nc.gpsimd.tensor_tensor(both_pair[:], tissue_first[:, 0, :2], tissue_first[:, 1, :2], ALU.mult)
-        nc.vector.tensor_tensor(both_first[:], tissue_first[:, 0, 2:], tissue_first[:, 1, 2:], ALU.mult)
-        nc.vector.scalar_tensor_tensor(squared[:, :2], both_pair[:], -3.125, both_pair[:], ALU.add, ALU.mult)
-        nc.vector.scalar_tensor_tensor(squared[:, 2:], both_first[:], -3.125, both_first[:], ALU.add, ALU.mult)
-        for i in range(PACK, TILES):
-            product(i)
+        for rows in (slice(0, 2), slice(2, 4)):
+            nc.gpsimd.tensor_tensor(both_first[:, rows], tissue_first[:, 0, rows], tissue_first[:, 1, rows], ALU.mult)
+        product(4)
+        product(5)
+        nc.vector.scalar_tensor_tensor(squared[:], both_first[:], -3.125, both_first[:], ALU.add, ALU.mult)
+        nc.vector.scalar_tensor_tensor(ahead[:, :2], both_mid[:], -3.125, both_mid[:], ALU.add, ALU.mult)
+        product(6)
         quantize_w2(0)
+        nc.vector.scalar_tensor_tensor(ahead[:, 2], both_last[0][:], -3.125, both_last[0][:], ALU.add, ALU.mult)
+        product(7)
         quantize_w2(1)
 
         roots = shared.tile([P, PASSES, PACK, M], F32, name="roots", align_bytes=64, offset=ROOTS_AT)
         term, inverse = roots[:, 0], roots[:, 1]
-        gained = keep.tile([P, M], F32, name="gained", align_bytes=64)
         z_bf = [keep.tile([P, cols.stop - cols.start, PACK], BF16, name="z_bf%d" % cols.start, align_bytes=64) for cols in PIECES]
         z_wide = keep.tile([P, PACK, M], F32, name="z_wide", align_bytes=64)
         z_codes = keep.tile([P, PASSES, M], U32, name="z_codes", align_bytes=64)
@@ -270,24 +280,14 @@ def tile_list_burial_isotope_mobility_kernel(
         ]
 
         def root(cols):
-            nc.scalar.activation(term[:, :, cols], both_last[:, :, cols], ACT.Abs_reciprocal_sqrt, bias=4.0, scale=-2.56)
-
-        def square(cols):
-            nc.scalar.activation(term[:, :3, cols], term[:, :3, cols], ACT.Square)
-
-        def square_with_gain(t, cols):
-            nc.vector.scalar_tensor_tensor(
-                gained[:, cols], term[:, t, cols], gain_cols[:, t : t + 1], term[:, t, cols], ALU.mult, ALU.mult
-            )
+            nc.scalar.activation(term[:, :3, cols], ahead[:, :, cols], ACT.Abs_reciprocal_sqrt, bias=16.0, scale=6.5536)
+            nc.scalar.activation(term[:, 3, cols], both_last[1][:, cols], ACT.Abs_reciprocal_sqrt, bias=4.0, scale=-2.56)
+            nc.scalar.activation(term[:, 3, cols], term[:, 3, cols], ACT.Square)
 
         def combine(t, cols):
-            if t < 3:
-                nc.vector.scalar_tensor_tensor(
-                    z_wide[:, t, cols], term[:, t, cols], gain_cols[:, t : t + 1], soil_of(PACK + t)[:, cols], ALU.mult, ALU.add
-                )
-            else:
-                picked = h[PACK + t][:].indirect(pos_sb[2][:, cols.start // 16 : cols.stop // 16])
-                nc.vector.tensor_tensor(z_wide[:, t, cols], picked, gained[:, cols], ALU.add)
+            nc.vector.scalar_tensor_tensor(
+                z_wide[:, t, cols], term[:, t, cols], gain_cols[:, t : t + 1], soil_of(PACK + t)[:, cols], ALU.mult, ALU.add
+            )
 
         def weave(piece):
             cols = PIECES[piece]
@@ -355,22 +355,18 @@ def tile_list_burial_isotope_mobility_kernel(
         for c in range(2):
             scale_by_gain(c)
             turn_back(c)
-        square(HALVES[0])
         root(HALVES[1])
-        square(HALVES[1])
-        square_with_gain(3, HALVES[0])
-        scale_by_gain(2)
-        for t in (3, 0, 1, 2):
+        for t in range(PACK):
             combine(t, HALVES[0])
         quantize_turned(0)
         weave(0)
-        scale_by_gain(3)
+        scale_by_gain(2)
         quantize_woven(0)
+        scale_by_gain(3)
         turn_back(2)
         for first_row in (0, 2):
             multiply_and_store(0, first_row, (0, 1), nc.scalar.copy)
         turn_back(3)
-        square_with_gain(3, HALVES[1])
         for t in range(PACK):
             combine(t, PIECES[1])
         combine(0, PIECES[2])

@@ -233,20 +233,17 @@ def tile_list_burial_isotope_mobility_kernel(
 
         both_first = shared.tile([P, PACK, M], F32, name="both_first", align_bytes=64, offset=TABLE1_AT + 128 - 8192)
         both_mid = shared.tile([P, 2, M], F32, name="both_mid", align_bytes=64, offset=TABLE1_AT + 128 - 8192 - 4096)
-        both_last = [
-            shared.tile([P, M], F32, name="both6", align_bytes=64, offset=TABLE1_AT + 128 - 8192),
-            shared.tile([P, M], F32, name="both7", align_bytes=64, offset=TABLE1_AT + 128 - 8192 - 4096),
-        ]
-        ahead = keep.tile([P, PACK - 1, M], F32, name="ahead", align_bytes=64)
+        both_last = shared.tile([P, 2, M], F32, name="both_last", align_bytes=64, offset=TABLE1_AT + 128 - 8192)
+        ahead = keep.tile([P, 2, M], F32, name="ahead", align_bytes=64)
 
         def both_of(i):
-            return both_mid[:, i - PACK] if i < PACK + 2 else both_last[i - PACK - 2][:]
+            return both_mid[:, i - PACK] if i < PACK + 2 else both_last[:, i - PACK - 2]
         squared = keep.tile([P, PACK, M], F32, name="squared", align_bytes=64)
         w2_codes = shared.tile([P, PASSES, N], U32, name="w2_codes", align_bytes=64, offset=TABLE1_AT + 128 - 4096)
         w2_scale = keep.tile([P, PASSES, N], U8, name="w2_scale", align_bytes=64)
 
         def product(i):
-            engine = nc.gpsimd if i < PACK + 2 else nc.vector
+            engine = nc.gpsimd if i == PACK else nc.vector
             engine.tensor_tensor(both_of(i), tissue(0, i), tissue(1, i), ALU.mult)
 
         def quantize_w2(b):
@@ -261,11 +258,10 @@ def tile_list_burial_isotope_mobility_kernel(
         product(4)
         product(5)
         nc.vector.scalar_tensor_tensor(squared[:], both_first[:], -3.125, both_first[:], ALU.add, ALU.mult)
-        nc.vector.scalar_tensor_tensor(ahead[:, :2], both_mid[:], -3.125, both_mid[:], ALU.add, ALU.mult)
         product(6)
-        quantize_w2(0)
-        nc.vector.scalar_tensor_tensor(ahead[:, 2], both_last[0][:], -3.125, both_last[0][:], ALU.add, ALU.mult)
+        nc.vector.scalar_tensor_tensor(ahead[:], both_mid[:], -3.125, both_mid[:], ALU.add, ALU.mult)
         product(7)
+        quantize_w2(0)
         quantize_w2(1)
 
         roots = shared.tile([P, PASSES, PACK, M], F32, name="roots", align_bytes=64, offset=ROOTS_AT)
@@ -280,9 +276,9 @@ def tile_list_burial_isotope_mobility_kernel(
         ]
 
         def root(cols):
-            nc.scalar.activation(term[:, :3, cols], ahead[:, :, cols], ACT.Abs_reciprocal_sqrt, bias=16.0, scale=6.5536)
-            nc.scalar.activation(term[:, 3, cols], both_last[1][:, cols], ACT.Abs_reciprocal_sqrt, bias=4.0, scale=-2.56)
-            nc.scalar.activation(term[:, 3, cols], term[:, 3, cols], ACT.Square)
+            nc.scalar.activation(term[:, 2:, cols], both_last[:, :, cols], ACT.Abs_reciprocal_sqrt, bias=4.0, scale=-2.56)
+            nc.scalar.activation(term[:, :2, cols], ahead[:, :, cols], ACT.Abs_reciprocal_sqrt, bias=16.0, scale=6.5536)
+            nc.scalar.activation(term[:, 2:, cols], term[:, 2:, cols], ACT.Square)
 
         def combine(t, cols):
             nc.vector.scalar_tensor_tensor(

@@ -123,23 +123,18 @@ def tile_list_burial_isotope_mobility_kernel(
         ]
         nc.sync.dma_start(w4_rest[:], w4_rows[:, :, 2 * P :].bitcast(I32))
         nc.sync.dma_start(w2_raw[0][:], w2[:BANK, :].rearrange("(p t) n -> p t n", t=PACK))
-        gain_cols = shared.tile([P, 8], F32, name="gain_cols", align_bytes=64, offset=PICKED_AT + 128)
-        with nc.allow_non_contiguous_dma(reason="gain: one value for each partition and row tile"):
-            for e in range(4):
-                nc.sync.dma_start(gain_cols[e:P:4, 0:PACK], gain[BANK:].rearrange("(u t e) -> e u t", t=PACK, e=4)[e])
         for e in range(4):
             nc.sync.dma_start(w2_raw[1][e:P:4, :, :], w2[BANK:, :].rearrange("(u t e) n -> e u t n", t=PACK, e=4)[e])
         nc.gpsimd.tensor_copy(
             w4_dealt[:].bitcast(U32).rearrange("p t a (u e) -> p t a u e", e=2),
             w4_rest[:, :, 64 * (PACK - 1) :].bitcast(U32).rearrange("p a (u t e) -> p t a u e", t=PACK, e=2),
         )
-        neg_gain = keep.tile([P, PACK], F32, name="neg_gain", align_bytes=64)
-        is_zero = keep.tile([P, PACK], F32, name="is_zero", align_bytes=64)
+        gain_cols = shared.tile([P, 8], F32, name="gain_cols", align_bytes=64, offset=TABLE1_AT + 192)
+        with nc.allow_non_contiguous_dma(reason="gain: one value for each partition and row tile"):
+            for e in range(4):
+                nc.sync.dma_start(gain_cols[e:P:4, 0:PACK], gain[BANK:].rearrange("(u t e) -> e u t", t=PACK, e=4)[e])
         divisor = keep.tile([P, PACK], F32, name="divisor", align_bytes=64)
         undo_gain = shared.tile([P, PACK], F32, name="undo_gain", align_bytes=64, offset=ROOTS_AT)
-        nc.gpsimd.tensor_scalar(is_zero[:], gain_cols[:, 0:PACK], 0.0, None, ALU.is_equal)
-        nc.gpsimd.tensor_scalar(neg_gain[:], gain_cols[:, 0:PACK], -1.0, 0.0, ALU.mult, ALU.add)
-        nc.gpsimd.tensor_tensor(divisor[:], is_zero[:], gain_cols[:, 0:PACK], ALU.subtract)
         gain_rows = shared.tile([P, BANK], F32, name="gain_rows", align_bytes=64, offset=TABLE1_AT + 256)
         nc.sync.dma_start(gain_rows[:], gain[:BANK].partition_broadcast(P))
 
@@ -158,7 +153,7 @@ def tile_list_burial_isotope_mobility_kernel(
             return tissue_last[i - PACK][:, j, :]
 
         soil_first = keep.tile([P, M], F32, name="soil_first", align_bytes=64)
-        soil_rest = shared.tile([P, TILES - 1, M], F32, name="soil_rest", align_bytes=64, offset=WORDS_AT[0] + 64 - 14336)
+        soil_rest = keep.tile([P, TILES - 1, M], F32, name="soil_rest", align_bytes=64)
 
         def soil_of(i):
             if i == 0:
@@ -199,6 +194,10 @@ def tile_list_burial_isotope_mobility_kernel(
             else:
                 nc.scalar.activation(h[0][:, cols], opened[0, cols.start][:], ACT.Copy, scale=-1.0)
         for i in range(TILES):
+            if i == PACK - 1:
+                nc.vector.scalar_tensor_tensor(
+                    divisor[:], gain_cols[:, 0:PACK], 0.0, gain_cols[:, 0:PACK], ALU.is_equal, ALU.add
+                )
             if i == PACK:
                 nc.vector.reciprocal(undo_gain[:], divisor[:])
             if i > 0:
@@ -210,8 +209,10 @@ def tile_list_burial_isotope_mobility_kernel(
                         nc.vector.tensor_scalar(h[i][:, cols], opened[i, cols.start][:], -1.0, None, ALU.mult)
                     else:
                         nc.vector.tensor_scalar(
-                            h[i][:, cols], opened[i, cols.start][:], 0.25, neg_gain[:, i - PACK : i - PACK + 1], ALU.add, ALU.mult
+                            h[i][:, cols], opened[i, cols.start][:], 0.25, gain_cols[:, i - PACK : i - PACK + 1], ALU.add, ALU.mult
                         )
+            if i >= 1:
+                pick_soil(i - 1)
             for j in range(2):
                 if i < PACK:
                     nc.scalar.activation(tissue(j, i), h[i][:].indirect(pos_sb[j][:]), ACT.Sigmoid, bias=LN5, scale=-1.0)
@@ -223,8 +224,7 @@ def tile_list_burial_isotope_mobility_kernel(
                         bias=LN5 - 0.25,
                         scale=undo_gain[:, i - PACK : i - PACK + 1],
                     )
-        for i in range(TILES):
-            pick_soil(i)
+        pick_soil(TILES - 1)
         for t in range(PACK):
             for c in range(CHUNKS):
                 if t == 0:
@@ -282,7 +282,7 @@ def tile_list_burial_isotope_mobility_kernel(
 
         def combine(t, cols):
             nc.vector.scalar_tensor_tensor(
-                z_wide[:, t, cols], term[:, t, cols], gain_cols[:, t : t + 1], soil_of(PACK + t)[:, cols], ALU.mult, ALU.add
+                z_wide[:, t, cols], term[:, t, cols], gain_cols[:, t : t + 1], soil_of(PACK + t)[:, cols], ALU.mult, ALU.subtract
             )
 
         def weave(piece):

@@ -108,7 +108,8 @@ def tile_list_burial_isotope_mobility_kernel(
         pick_words(0, 512, 1024)
         pick_words(1, 0, 512)
         pick_words(1, 512, 768)
-        pick_words(1, 768, 1024)
+        pick_words(1, 768, 896)
+        pick_words(1, 896, 1024)
 
         def w4_of(i, a):
             if i == 0:
@@ -184,12 +185,12 @@ def tile_list_burial_isotope_mobility_kernel(
             nc.vector.tensor_copy(soil_of(i), h[i][:].indirect(pos_sb[2][:]))
 
         opened = {}
-        first_cols = [slice(256 * q, 256 * (q + 1)) for q in range(4)]
+        first_cols = [slice(0, 256), slice(256, 512), slice(512, 768), slice(768, 896), slice(896, 1024)]
         for a in range(PASSES):
             for number, cols in enumerate(first_cols):
                 first_product(0, cols, number, a, opened)
         for q, cols in enumerate(first_cols):
-            if q == 2:
+            if q == 3:
                 nc.vector.tensor_scalar(h[0][:, cols], opened[0, cols.start][:], -1.0, None, ALU.mult)
             else:
                 nc.scalar.activation(h[0][:, cols], opened[0, cols.start][:], ACT.Copy, scale=-1.0)
@@ -233,17 +234,20 @@ def tile_list_burial_isotope_mobility_kernel(
 
         both_first = shared.tile([P, PACK, M], F32, name="both_first", align_bytes=64, offset=TABLE1_AT + 128 - 8192)
         both_mid = shared.tile([P, 2, M], F32, name="both_mid", align_bytes=64, offset=TABLE1_AT + 128 - 8192 - 4096)
-        both_last = shared.tile([P, 2, M], F32, name="both_last", align_bytes=64, offset=TABLE1_AT + 128 - 8192)
-        ahead = keep.tile([P, 2, M], F32, name="ahead", align_bytes=64)
+        both_last = [
+            shared.tile([P, M], F32, name="both6", align_bytes=64, offset=TABLE1_AT + 128 - 8192),
+            shared.tile([P, M], F32, name="both7", align_bytes=64, offset=TABLE1_AT + 128 - 8192 - 4096),
+        ]
+        ahead = keep.tile([P, PACK - 1, M], F32, name="ahead", align_bytes=64)
 
         def both_of(i):
-            return both_mid[:, i - PACK] if i < PACK + 2 else both_last[:, i - PACK - 2]
+            return both_mid[:, i - PACK] if i < PACK + 2 else both_last[i - PACK - 2][:]
         squared = keep.tile([P, PACK, M], F32, name="squared", align_bytes=64)
         w2_codes = shared.tile([P, PASSES, N], U32, name="w2_codes", align_bytes=64, offset=TABLE1_AT + 128 - 4096)
         w2_scale = keep.tile([P, PASSES, N], U8, name="w2_scale", align_bytes=64)
 
         def product(i):
-            engine = nc.gpsimd if i == PACK else nc.vector
+            engine = nc.gpsimd if i < PACK + 2 else nc.vector
             engine.tensor_tensor(both_of(i), tissue(0, i), tissue(1, i), ALU.mult)
 
         def quantize_w2(b):
@@ -258,10 +262,11 @@ def tile_list_burial_isotope_mobility_kernel(
         product(4)
         product(5)
         nc.vector.scalar_tensor_tensor(squared[:], both_first[:], -3.125, both_first[:], ALU.add, ALU.mult)
+        nc.vector.scalar_tensor_tensor(ahead[:, :2], both_mid[:], -3.125, both_mid[:], ALU.add, ALU.mult)
         product(6)
-        nc.vector.scalar_tensor_tensor(ahead[:], both_mid[:], -3.125, both_mid[:], ALU.add, ALU.mult)
-        product(7)
         quantize_w2(0)
+        nc.vector.scalar_tensor_tensor(ahead[:, 2], both_last[0][:], -3.125, both_last[0][:], ALU.add, ALU.mult)
+        product(7)
         quantize_w2(1)
 
         roots = shared.tile([P, PASSES, PACK, M], F32, name="roots", align_bytes=64, offset=ROOTS_AT)
@@ -276,9 +281,9 @@ def tile_list_burial_isotope_mobility_kernel(
         ]
 
         def root(cols):
-            nc.scalar.activation(term[:, 2:, cols], both_last[:, :, cols], ACT.Abs_reciprocal_sqrt, bias=4.0, scale=-2.56)
-            nc.scalar.activation(term[:, :2, cols], ahead[:, :, cols], ACT.Abs_reciprocal_sqrt, bias=16.0, scale=6.5536)
-            nc.scalar.activation(term[:, 2:, cols], term[:, 2:, cols], ACT.Square)
+            nc.scalar.activation(term[:, 3, cols], both_last[1][:, cols], ACT.Abs_reciprocal_sqrt, bias=4.0, scale=-2.56)
+            nc.scalar.activation(term[:, :3, cols], ahead[:, :, cols], ACT.Abs_reciprocal_sqrt, bias=16.0, scale=6.5536)
+            nc.scalar.activation(term[:, 3, cols], term[:, 3, cols], ACT.Square)
 
         def combine(t, cols):
             nc.vector.scalar_tensor_tensor(

@@ -330,12 +330,12 @@ def tile_list_burial_isotope_mobility_kernel(
                 in_=z_words[piece][:].rearrange("p m u -> p (m u)").bitcast(BF16),
             )
 
-        def multiply_and_store(piece, first_row, order, copy_out):
+        def multiply_and_store(piece, first_row, order, copy_out, places=2):
             cols = PIECES[piece]
-            number = 2 * piece + first_row // 2
-            acc = bank((4 + number) % 8, [P, 2, cols.stop - cols.start], "acc")
+            number = (0, 4, 6)[piece] + first_row // places
+            acc = bank((4 + number) % 8, [P, places, cols.stop - cols.start], "acc")
             for step, b in enumerate(order):
-                for place in range(2):
+                for place in range(places):
                     j = first_row + place
                     nc.tensor.matmul_mx(
                         out=acc[:, place, :],
@@ -344,11 +344,11 @@ def tile_list_burial_isotope_mobility_kernel(
                         rhs=z_codes[:, b, cols].bitcast(FP8X4),
                         rhs_scale=z_scale[:, b, cols],
                         start=(step == 0 and place == 0),
-                        stop=(step == 1 and place == 1),
+                        stop=(step == 1 and place == places - 1),
                     )
-            result = keep.tile([P, 2, cols.stop - cols.start], F32, name="result%d" % number)
+            result = keep.tile([P, places, cols.stop - cols.start], F32, name="result%d" % number)
             copy_out(result[:], acc[:])
-            nc.sync.dma_start(out[P * first_row : P * (first_row + 2), cols].rearrange("(j p) m -> p j m", p=P), result[:])
+            nc.sync.dma_start(out[P * first_row : P * (first_row + places), cols].rearrange("(j p) m -> p j m", p=P), result[:])
 
         for c in range(CHUNKS):
             invert(c)
@@ -365,8 +365,8 @@ def tile_list_burial_isotope_mobility_kernel(
         quantize_woven(0)
         scale_by_gain(3)
         turn_back(2)
-        for first_row in (0, 2):
-            multiply_and_store(0, first_row, (0, 1), nc.scalar.copy)
+        for j in range(4):
+            multiply_and_store(0, j, (0, 1), nc.scalar.copy, places=1)
         turn_back(3)
         for t in range(PACK):
             combine(t, PIECES[1])
@@ -379,7 +379,7 @@ def tile_list_burial_isotope_mobility_kernel(
         quantize_turned(2)
         weave(2)
         quantize_woven(2)
-        for piece in (1, 2):
-            for first_row in (0, 2):
-                last = piece == 2 and first_row == 2
-                multiply_and_store(piece, first_row, (0, 1), nc.vector.tensor_copy if last else nc.scalar.copy)
+        for first_row in (0, 2):
+            multiply_and_store(1, first_row, (0, 1), nc.scalar.copy)
+        for j in range(4):
+            multiply_and_store(2, j, (0, 1), nc.scalar.copy if j == 2 else nc.vector.tensor_copy, places=1)

import math
from contextlib import ExitStack

import concourse.mybir as mybir
from concourse.masks import make_identity

K, H, N, T, S, M = 1024, 1024, 512, 2048, 1024, 512
FLOPS = 2 * K * H * S + 2 * H * N * M

F32 = mybir.dt.float32
BF16 = mybir.dt.bfloat16
I32 = mybir.dt.int32
U32 = mybir.dt.uint32
U16 = mybir.dt.uint16
U8 = mybir.dt.uint8
FP8X4 = mybir.dt.float8_e4m3fn_x4
FP4X4 = mybir.dt.float4_e2m1fn_x4
ACT = mybir.ActivationFunctionType
ALU = mybir.AluOpType

P = 128
PACK = 4
PASSES = 2
TILES = H // P
BANK = 512
LN5 = math.log(5.0)
HALVES = (slice(0, 256), slice(256, 512))
PIECES = (slice(0, 256), slice(256, 384), slice(384, 512))
CHUNKS = M // P

PICKED_AT = 3520
TABLE1_AT = 20800
WORDS_AT = (38912, 43008)
ROOTS_AT = 57344


def tile_list_burial_isotope_mobility_kernel(
    tc, tab_words, tab_scales, offs, pos1, pos2, pos3, w4_words, w4_scales, gain, w2, out
):
    nc = tc.nc
    with ExitStack() as ctx:
        keep = ctx.enter_context(tc.tile_pool(name="keep", bufs=1))
        shared = ctx.enter_context(tc.tile_pool(name="shared", bufs=1))
        psum = ctx.enter_context(tc.psum_pool(name="psum", bufs=1))

        def bank(number, shape, name):
            return psum.tile(shape, F32, name=name, tag="bank%d" % number)

        offs_sb = keep.tile([P, S // 16], U16, name="offs_sb")
        pos_sb = [keep.tile([P, M // 16], U16, name="pos%d_sb" % j) for j in range(3)]
        tab_scale_rows = keep.tile([P, T], U8, name="tab_scale_rows", align_bytes=64)
        w4_scale_rows = keep.tile([32, H], U8, name="w4_scale_rows", align_bytes=64)
        tab_sb = [
            keep.tile([P, T], I32, name="tab_sb0", tag="tab_sb0", align_bytes=64),
            shared.tile([P, T], I32, name="tab_sb1", align_bytes=64, offset=TABLE1_AT),
        ]
        w4_rows = w4_words.rearrange("a p c -> p a c")
        w4_first = keep.tile([P, PASSES, 64], I32, name="w4_first", align_bytes=64)
        w4_rest = shared.tile([P, PASSES, 64 * (TILES - 1)], I32, name="w4_rest", align_bytes=64, offset=PICKED_AT + 64 - 3584)
        planes = [keep.tile([P, S + H], U8, name="planes%d" % a, align_bytes=64) for a in range(PASSES)]

        nc.sync.dma_start(offs_sb[:], offs)
        nc.sync.dma_start(
            tab_scale_rows[0:32, :].bitcast(I32), tab_scales.rearrange("a q t -> (a q) t").bitcast(I32)
        )
        nc.sync.dma_start(w4_scale_rows[:].bitcast(I32), w4_scales.rearrange("a q c -> (a q) c").bitcast(I32))
        nc.sync.dma_start(tab_sb[0][:], tab_words[0].rearrange("p t i -> p (t i)").bitcast(I32))
        nc.sync.dma_start(w4_first[:], w4_rows[:, :, : 2 * P].bitcast(I32))
        for j, pos in enumerate((pos1, pos2, pos3)):
            nc.sync.dma_start(pos_sb[j][:], pos)
        nc.sync.dma_start(tab_sb[1][:], tab_words[1].rearrange("p t i -> p (t i)").bitcast(I32))

        warm = keep.tile([P, 2, 8], F32, name="warm")
        nc.gpsimd.memset(warm[:, 0, :], 0.0)
        nc.scalar.activation(warm[:, 1, :], warm[:, 0, :], ACT.Sigmoid)

        for rows in (slice(32, 64), slice(64, 128)):
            nc.vector.memset(tab_scale_rows[rows, :].bitcast(I32), 0)
            nc.gpsimd.memset(planes[0][rows, :].bitcast(I32), 0)
        nc.gpsimd.memset(planes[1][:].bitcast(I32), 0)
        ident = keep.tile([P, P], F32, name="ident", align_bytes=64)
        make_identity(nc, ident[:])

        picked_scale_rows = shared.tile([P, S], U8, name="picked_scale_rows", align_bytes=64, offset=PICKED_AT)
        nc.vector.tensor_copy(picked_scale_rows[:], tab_scale_rows[:].indirect(offs_sb[:]))
        nc.scalar.copy(planes[0][0:32, S : S + BANK].bitcast(U32), w4_scale_rows[:, :BANK].bitcast(U32))
        nc.scalar.copy(
            planes[0][0:32, S + BANK :].bitcast(U32).rearrange("p (t u) -> p t u", t=PACK),
            w4_scale_rows[:, BANK:].bitcast(U32).rearrange("p (u t) -> p t u", t=PACK),
        )
        nc.vector.tensor_copy(planes[0][0:32, :S].bitcast(I32), picked_scale_rows[0:32, :].bitcast(I32))
        for q in range(1, 4):
            nc.sync.dma_start(planes[0][32 * q : 32 * q + 4, :].bitcast(I32), planes[0][4 * q : 4 * q + 4, :].bitcast(I32))
        for r in range(4):
            nc.sync.dma_start(planes[1][r:P:32, :].bitcast(I32), planes[0][16 + r : 32 : 4, :].bitcast(I32))

        v_words = [
            shared.tile([P, S], U32, name="v_words%d" % a, align_bytes=64, offset=WORDS_AT[a]) for a in range(PASSES)
        ]

        def pick_words(a, start, stop):
            nc.vector.tensor_copy(
                v_words[a][:, start:stop], tab_sb[a][:].bitcast(U32).indirect(offs_sb[:, start // 16 : stop // 16])
            )

        w4_dealt = keep.tile([P, PACK, PASSES, 2 * P], U8, name="w4_dealt", align_bytes=64)
        pick_words(0, 0, 512)
        pick_words(0, 512, 1024)
        pick_words(1, 0, 512)
        pick_words(1, 512, 768)
        pick_words(1, 768, 896)
        pick_words(1, 896, 1024)

        def w4_of(i, a):
            if i == 0:
                return w4_first[:, a, :]
            if i < PACK:
                return w4_rest[:, a, 64 * (i - 1) : 64 * i]
            return w4_dealt[:, i - PACK, a, :]

        w2_raw = [
            shared.tile([P, PACK, N], F32, name="w2_raw0", align_bytes=64, offset=PICKED_AT + S - 64),
            shared.tile([P, PACK, N], F32, name="w2_raw1", align_bytes=64, offset=TABLE1_AT + 64 - 8192),
        ]
        nc.sync.dma_start(w4_rest[:], w4_rows[:, :, 2 * P :].bitcast(I32))
        nc.sync.dma_start(w2_raw[0][:], w2[:BANK, :].rearrange("(p t) n -> p t n", t=PACK))
        for e in range(4):
            nc.sync.dma_start(w2_raw[1][e:P:4, :, :], w2[BANK:, :].rearrange("(u t e) n -> e u t n", t=PACK, e=4)[e])
        nc.gpsimd.tensor_copy(
            w4_dealt[:].bitcast(U32).rearrange("p t a (u e) -> p t a u e", e=2),
            w4_rest[:, :, 64 * (PACK - 1) :].bitcast(U32).rearrange("p a (u t e) -> p t a u e", t=PACK, e=2),
        )
        gain_cols = shared.tile([P, 8], F32, name="gain_cols", align_bytes=64, offset=TABLE1_AT + 192)
        with nc.allow_non_contiguous_dma(reason="gain: one value for each partition and row tile"):
            for e in range(4):
                nc.sync.dma_start(gain_cols[e:P:4, 0:PACK], gain[BANK:].rearrange("(u t e) -> e u t", t=PACK, e=4)[e])
        divisor = keep.tile([P, PACK], F32, name="divisor", align_bytes=64)
        undo_gain = shared.tile([P, PACK], F32, name="undo_gain", align_bytes=64, offset=ROOTS_AT)
        gain_rows = shared.tile([P, BANK], F32, name="gain_rows", align_bytes=64, offset=TABLE1_AT + 256)
        nc.sync.dma_start(gain_rows[:], gain[:BANK].partition_broadcast(P))

        w2_bf = []
        for b in range(PASSES):
            w2_bf.append(keep.tile([P, N, PACK], BF16, name="w2_bf%d" % b, align_bytes=64))
            nc.gpsimd.tensor_scalar(w2_bf[b][:], w2_raw[b][:].rearrange("p t n -> p n t"), 1.0, 0.0, ALU.mult, ALU.add)

        h = [keep.tile([P, S], F32, name="h%d" % i, align_bytes=64) for i in range(TILES)]
        tissue_first = keep.tile([P, 2, PACK, M], F32, name="tissue_first", align_bytes=64)
        tissue_last = [keep.tile([P, 2, M], F32, name="tissue%d" % i, align_bytes=64) for i in range(PACK, TILES)]

        def tissue(j, i):
            if i < PACK:
                return tissue_first[:, j, i, :]
            return tissue_last[i - PACK][:, j, :]

        soil_first = keep.tile([P, M], F32, name="soil_first", align_bytes=64)
        soil_rest = keep.tile([P, TILES - 1, M], F32, name="soil_rest", align_bytes=64)

        def soil_of(i):
            if i == 0:
                return soil_first[:]
            return soil_rest[:, i - 1, :]

        def first_product(i, cols, number, a, opened):
            if a == 0:
                opened[i, cols.start] = bank(number, [P, cols.stop - cols.start], "h_bank")
            nc.tensor.matmul_mx(
                out=opened[i, cols.start][:],
                lhsT=w4_of(i, a).bitcast(FP4X4),
                lhsT_scale=planes[a][:, S + P * i : S + P * (i + 1)],
                rhs=v_words[a][:, cols].bitcast(FP8X4),
                rhs_scale=planes[a][:, cols],
                start=(a == 0),
                stop=(a == PASSES - 1),
            )

        sums = {}

        def turn_into_sums(row, t, c, first, last):
            nc.tensor.matmul(
                sums[c][:, P * t : P * (t + 1)], row[:, P * c : P * (c + 1)], ident[:], start=first, stop=last, is_transpose=True
            )

        def pick_soil(i):
            nc.vector.tensor_copy(soil_of(i), h[i][:].indirect(pos_sb[2][:]))

        opened = {}
        first_cols = [slice(0, 256), slice(256, 512), slice(512, 768), slice(768, 896), slice(896, 1024)]
        for a in range(PASSES):
            for number, cols in enumerate(first_cols):
                first_product(0, cols, number, a, opened)
        for q, cols in enumerate(first_cols):
            if q == 3:
                nc.vector.tensor_scalar(h[0][:, cols], opened[0, cols.start][:], -1.0, None, ALU.mult)
            else:
                nc.scalar.activation(h[0][:, cols], opened[0, cols.start][:], ACT.Copy, scale=-1.0)
        for i in range(TILES):
            if i == PACK - 1:
                nc.vector.scalar_tensor_tensor(
                    divisor[:], gain_cols[:, 0:PACK], 0.0, gain_cols[:, 0:PACK], ALU.is_equal, ALU.add
                )
            if i == PACK:
                nc.vector.reciprocal(undo_gain[:], divisor[:])
            if i > 0:
                for half in range(2):
                    cols = slice(BANK * half, BANK * (half + 1))
                    for a in range(PASSES):
                        first_product(i, cols, 2 * i + half - 4 if i in (4, 5) else (2 * i + half - 2) % 4, a, opened)
                    if i < PACK:
                        nc.vector.tensor_scalar(h[i][:, cols], opened[i, cols.start][:], -1.0, None, ALU.mult)
                    else:
                        nc.vector.tensor_scalar(
                            h[i][:, cols], opened[i, cols.start][:], 0.25, gain_cols[:, i - PACK : i - PACK + 1], ALU.add, ALU.mult
                        )
            if i >= 1:
                pick_soil(i - 1)
            for j in range(2):
                if i < PACK:
                    nc.scalar.activation(tissue(j, i), h[i][:].indirect(pos_sb[j][:]), ACT.Sigmoid, bias=LN5, scale=-1.0)
                else:
                    nc.scalar.activation(
                        tissue(j, i),
                        h[i][:].indirect(pos_sb[j][:]),
                        ACT.Sigmoid,
                        bias=LN5 - 0.25,
                        scale=undo_gain[:, i - PACK : i - PACK + 1],
                    )
        pick_soil(TILES - 1)
        for t in range(PACK):
            for c in range(CHUNKS):
                if t == 0:
                    sums[c] = bank(c, [P, BANK], "sums")
                turn_into_sums(soil_of(t), t, c, t == 0, False)

        both_first = shared.tile([P, PACK, M], F32, name="both_first", align_bytes=64, offset=TABLE1_AT + 128 - 8192)
        both_mid = shared.tile([P, 2, M], F32, name="both_mid", align_bytes=64, offset=TABLE1_AT + 128 - 8192 - 4096)
        both_last = [
            shared.tile([P, M], F32, name="both6", align_bytes=64, offset=TABLE1_AT + 128 - 8192),
            shared.tile([P, M], F32, name="both7", align_bytes=64, offset=TABLE1_AT + 128 - 8192 - 4096),
        ]
        ahead = keep.tile([P, PACK - 1, M], F32, name="ahead", align_bytes=64)

        def both_of(i):
            return both_mid[:, i - PACK] if i < PACK + 2 else both_last[i - PACK - 2][:]
        squared = keep.tile([P, PACK, M], F32, name="squared", align_bytes=64)
        w2_codes = shared.tile([P, PASSES, N], U32, name="w2_codes", align_bytes=64, offset=TABLE1_AT + 128 - 4096)
        w2_scale = keep.tile([P, PASSES, N], U8, name="w2_scale", align_bytes=64)

        def product(i):
            engine = nc.gpsimd if i < PACK + 2 else nc.vector
            engine.tensor_tensor(both_of(i), tissue(0, i), tissue(1, i), ALU.mult)

        def quantize_w2(b):
            nc.vector.quantize_mx(
                out=w2_codes[:, b, :].bitcast(FP8X4),
                scales=w2_scale[:, b, :],
                in_=w2_bf[b][:].rearrange("p n t -> p (n t)"),
            )

        for rows in (slice(0, 2), slice(2, 4)):
            nc.gpsimd.tensor_tensor(both_first[:, rows], tissue_first[:, 0, rows], tissue_first[:, 1, rows], ALU.mult)
        product(4)
        product(5)
        nc.vector.scalar_tensor_tensor(squared[:], both_first[:], -3.125, both_first[:], ALU.add, ALU.mult)
        nc.vector.scalar_tensor_tensor(ahead[:, :2], both_mid[:], -3.125, both_mid[:], ALU.add, ALU.mult)
        product(6)
        quantize_w2(0)
        nc.vector.scalar_tensor_tensor(ahead[:, 2], both_last[0][:], -3.125, both_last[0][:], ALU.add, ALU.mult)
        product(7)
        quantize_w2(1)

        roots = shared.tile([P, PASSES, PACK, M], F32, name="roots", align_bytes=64, offset=ROOTS_AT)
        term, inverse = roots[:, 0], roots[:, 1]
        z_bf = [keep.tile([P, cols.stop - cols.start, PACK], BF16, name="z_bf%d" % cols.start, align_bytes=64) for cols in PIECES]
        z_wide = keep.tile([P, PACK, M], F32, name="z_wide", align_bytes=64)
        z_codes = keep.tile([P, PASSES, M], U32, name="z_codes", align_bytes=64)
        z_scale = keep.tile([P, PASSES, M], U8, name="z_scale", align_bytes=64)
        z_rows = keep.tile([P, CHUNKS, BANK], BF16, name="z_rows", align_bytes=64)
        z_words = [
            keep.tile([P, cols.stop - cols.start, 2], F32, name="z_words%d" % cols.start, align_bytes=64) for cols in PIECES
        ]

        def root(cols):
            nc.scalar.activation(term[:, 3, cols], both_last[1][:, cols], ACT.Abs_reciprocal_sqrt, bias=4.0, scale=-2.56)
            nc.scalar.activation(term[:, :3, cols], ahead[:, :, cols], ACT.Abs_reciprocal_sqrt, bias=16.0, scale=6.5536)
            nc.scalar.activation(term[:, 3, cols], term[:, 3, cols], ACT.Square)

        def combine(t, cols):
            nc.vector.scalar_tensor_tensor(
                z_wide[:, t, cols], term[:, t, cols], gain_cols[:, t : t + 1], soil_of(PACK + t)[:, cols], ALU.mult, ALU.subtract
            )

        def weave(piece):
            cols = PIECES[piece]
            nc.vector.tensor_copy(
                z_bf[piece][:].rearrange("p (g i) t -> p g t i", i=4),
                z_wide[:, :, cols].rearrange("p t (g i) -> p g t i", i=4),
            )

        def invert(c):
            cols = slice(P * c, P * (c + 1))
            nc.scalar.activation(inverse[:, :, cols], squared[:, :, cols], ACT.Abs_reciprocal_sqrt, bias=16.0, scale=6.5536)
            for t in range(PACK):
                turn_into_sums(inverse[:, t], t, c, False, t == PACK - 1)

        def scale_by_gain(c):
            nc.vector.scalar_tensor_tensor(z_rows[:, c], sums[c][:], -0.25, gain_rows[:], ALU.add, ALU.mult)

        def turn_back(c):
            turned = bank(c, [P, 2, P], "turned")
            words = z_rows[:, c].bitcast(F32)
            for u in range(2):
                nc.tensor.transpose(turned[:, u, :], words[:, u : 2 * P : 2], ident[:])
            words_out = z_words[0][:, P * c : P * (c + 1)] if c < 2 else z_words[c - 1][:]
            nc.scalar.copy(words_out, turned[:].rearrange("p u m -> p m u"))

        def quantize_woven(piece):
            cols = PIECES[piece]
            nc.vector.quantize_mx(
                out=z_codes[:, 1, cols].bitcast(FP8X4),
                scales=z_scale[:, 1, cols],
                in_=z_bf[piece][:].rearrange("p m t -> p (m t)"),
            )

        def quantize_turned(piece):
            cols = PIECES[piece]
            nc.vector.quantize_mx(
                out=z_codes[:, 0, cols].bitcast(FP8X4),
                scales=z_scale[:, 0, cols],
                in_=z_words[piece][:].rearrange("p m u -> p (m u)").bitcast(BF16),
            )

        def multiply_and_store(piece, first_row, order, copy_out, places=2):
            cols = PIECES[piece]
            number = (0, 4, 6)[piece] + first_row // places
            acc = bank((4 + number) % 8, [P, places, cols.stop - cols.start], "acc")
            for step, b in enumerate(order):
                for place in range(places):
                    j = first_row + place
                    nc.tensor.matmul_mx(
                        out=acc[:, place, :],
                        lhsT=w2_codes[:, b, P * j : P * (j + 1)].bitcast(FP8X4),
                        lhsT_scale=w2_scale[:, b, P * j : P * (j + 1)],
                        rhs=z_codes[:, b, cols].bitcast(FP8X4),
                        rhs_scale=z_scale[:, b, cols],
                        start=(step == 0 and place == 0),
                        stop=(step == 1 and place == places - 1),
                    )
            result = keep.tile([P, places, cols.stop - cols.start], F32, name="result%d" % number)
            copy_out(result[:], acc[:])
            nc.sync.dma_start(out[P * first_row : P * (first_row + places), cols].rearrange("(j p) m -> p j m", p=P), result[:])

        for c in range(CHUNKS):
            invert(c)
        root(HALVES[0])
        for c in range(2):
            scale_by_gain(c)
            turn_back(c)
        root(HALVES[1])
        for t in range(PACK):
            combine(t, HALVES[0])
        quantize_turned(0)
        weave(0)
        scale_by_gain(2)
        quantize_woven(0)
        scale_by_gain(3)
        turn_back(2)
        for j in range(4):
            multiply_and_store(0, j, (0, 1), nc.scalar.copy, places=1)
        turn_back(3)
        for t in range(PACK):
            combine(t, PIECES[1])
        combine(0, PIECES[2])
        weave(1)
        quantize_turned(1)
        quantize_woven(1)
        for t in range(1, PACK):
            combine(t, PIECES[2])
        quantize_turned(2)
        weave(2)
        quantize_woven(2)
        for first_row in (0, 2):
            multiply_and_store(1, first_row, (0, 1), nc.scalar.copy)
        for j in range(4):
            multiply_and_store(2, j, (0, 1), nc.scalar.copy if j == 2 else nc.vector.tensor_copy, places=1)
